import numpy as np, ml_dtypes
CORES = [2,3,42,43,82,83,122,123]
N = 8
import mx_ref
BF = ml_dtypes.bfloat16
def pick(q, e):
    c = np.concatenate([q[0].reshape(128, -1, 4), np.zeros((128, 1, 4), np.uint8)], axis=1); s = np.concatenate([q[1], np.ones((16, 1), np.uint8)], axis=1)
    return (np.ascontiguousarray(c[:, e].reshape(128, -1)), np.ascontiguousarray(s[:, e]))
def join(*qs):
    return (np.concatenate([q[0] for q in qs], axis=1), np.concatenate([q[1] for q in qs], axis=1))
def put(q, e, v):
    c, s = q[0].reshape(128, -1, 4).copy(), q[1].copy(); c[:, e] = v[0].reshape(128, -1, 4); s[:, e] = v[1]
    return (c.reshape(128, -1), s)
def pk(c, s):
    return (np.ascontiguousarray(c), mx_ref.live(s))
def emit(q):
    return q[0], q[1]
def packed(v, rng):
    q = [mx_ref.quantize(np.ascontiguousarray(v[r])) for r in range(N)]
    return np.stack([a for a, b in q]), np.stack([mx_ref.plane(b, rng) for a, b in q])
def values_of_codes():
    e, c = np.zeros((128, 128, 4), np.float32), np.zeros((128, 2, 4), np.uint8)
    e[np.arange(128), np.arange(128), 0] = 1
    c[:127, :, 0] = np.arange(256).reshape(2, 128).T[:127]
    return mx_ref.matmul(mx_ref.quantize(e.reshape(128, 512).astype(BF)), (c.reshape(128, 8), np.full((16, 2), 127, np.uint8))).T.reshape(-1).astype(np.float64)
CODE_VALUE, SCALE_VALUE = values_of_codes(), 2.0 ** (np.arange(256) - 127.0)
def decode(q):
    return (CODE_VALUE[q[0]].reshape(16, 8, -1, 4) * SCALE_VALUE[q[1]][:, None, :, None] + 0.0).reshape(128, -1).astype(np.float32)
def f(rng, *shape):
    return mx_ref.flush((rng.standard_normal(shape, dtype=np.float32) * np.exp2(rng.integers(-2, 3, shape[:-1] + (1,)))).astype(BF))
def wide(rng, *shape, cols=0):
    v = rng.standard_normal(shape, dtype=np.float32) * np.exp2(rng.integers(-12, 13, shape)).astype(np.float32)
    if cols: v *= np.repeat(np.exp2(rng.integers(-cols, cols + 1, shape[:-2] + (1, shape[-1] // 4))) * (rng.random(shape[:-2] + (1, shape[-1] // 4)) > 0.0625), 4, axis=-1).astype(np.float32)
    return mx_ref.flush(v.astype(BF))
C, L, R = 256, 32, 3
def match(p):
    s = np.array(p.reshape(8, 16, C)[:, :8].transpose(2, 0, 1) + np.float32(0.0), order="C")
    j = np.arange(C)
    g = np.zeros((8, C), np.int64)
    for k in range(8):
        e = np.argmax(s.reshape(C, 64), axis=1)
        g[e % 8, j] = e // 8
        s[j, e // 8] = -np.inf
        s[j, :, e % 8] = -np.inf
    return g
def order(p, g):
    m = p[16 * g + np.arange(8)[:, None], np.arange(C)]
    return np.argsort(-(m + np.float32(0.0)), axis=1, kind="stable")
def sung(t, g, o):
    b = t.reshape(8, 16, C, 4)[np.take_along_axis(g, o, axis=1), :, o]
    return np.ascontiguousarray(b.transpose(0, 2, 1, 3)).reshape(128, -1)
def numbers_of(rng):
    return {"x": np.array(f(rng, N, 128, 4 * C)), "u": np.array(f(rng, N, 128, 512)), "v": np.array(f(rng, N, 128, 512))}
def weights(rng, w):
    c, p = packed(w, rng)
    return {"wc": c, "ws": p}
def still(rng):
    return weights(rng, np.zeros((N, 128, 2048), BF))
def setup_inputs(rng):
    return {**numbers_of(rng), **weights(rng, f(rng, N, 128, 2048))}
def setup_inputs_ties(rng):
    d = numbers_of(rng)
    e = rng.permutation(N)
    x = d["x"].reshape(N, 8, 16, C, 4)
    u = d["u"].reshape(N, 8, 16, 128, 4)
    for r in range(N):
        k = np.zeros(C, int) if r == e[2] else rng.permutation(C) % 3
        a = x[r][:, :8, :3].copy()
        a[:, :, 2] = 0
        x[r][:, :8] = a[:, :, k]
        i = np.ones((8, 16), int)
        i[np.arange(8), rng.permutation(8)] = 0
        if r == e[0]: i[:] = 0
        a = u[r][:, :8, :2].copy()
        u[r][:, :8] = a[:, :, i.reshape(-1)]
    x[e[1]] = 0
    u[:, :, 8:] = 0
    w = np.array(f(rng, N, 128, 2048)).reshape(N, 8, 16, 4, 8, 16, 4)
    w[:, :, 8:, :, :, :8] = 0
    return {"x": x.reshape(N, 128, 4 * C), "u": u.reshape(N, 128, 512), "v": d["v"], **weights(rng, w.reshape(N, 128, 2048))}
def setup_inputs_near(rng):
    d = numbers_of(rng)
    turned = np.argsort(rng.random((N, 8)), axis=1) + 8 * rng.integers(0, 32, (N, 8))
    s = (np.arange(C) // 2) ^ turned[:, :, None]
    a = np.stack([rng.permutation([1.0, 1.0, 1.0, -1.0, -1.0, -1.0, 0.0, 0.0]) for r in range(N)])
    x = (rng.integers(4, 8, (N, 8, 16, C, 4)) * rng.choice([-1.0, 1.0], (N, 8, 16, C, 4))).astype(np.float32)
    x[:, :, :8] *= np.float32(2.0 ** -9)
    x[:, :, 8:] *= np.float32(2.0 ** -27)
    x[:, :, 0] = 0
    x[:, :, 0, :, 0] = a[:, :, None] * 2.0 ** -7
    b = ((s[..., None] >> np.arange(8)) & 1) * np.exp2(np.arange(8) - 30.0)
    x[:, :, 8] = b[..., :4]
    x[:, :, 9] = b[..., 4:]
    c = 4 + np.repeat(rng.integers(0, 2, (N, 8, C // 2, 4)), 2, axis=2) + (np.arange(C) % 2)[:, None]
    x[:, :, 11] = (a == 0)[:, :, None, None] * c * 2.0 ** -32
    for r in range(N):
        x[r, rng.permutation(8)[:4], 0, int(rng.integers(C)), 0] = np.array([1.0, 1.0, -1.0, -1.0]) * 2.0 ** 30
    u = d["u"].reshape(N, 128, 128, 4)
    k = np.where(rng.permutation(N) < N // 2, 2.0 ** -30, 1.0).astype(np.float32).astype(BF)
    for g in range(8):
        for h in range(8):
            u[:, :, 16 * g + h] = 0
            u[:, 16 * g, 16 * g + h, 0] = k
            u[:, 16 * g + 8:16 * g + 10, 16 * g + h] = k[:, None, None]
            u[:, 16 * g + 8 + h // 4, 16 * g + h, h % 4] = 0
            u[:, 16 * g + 11, 16 * g + h, h % 4] = k
    return {"x": x.reshape(N, 128, 4 * C).astype(BF), "u": u.reshape(N, 128, 512), "v": d["v"], **still(rng)}
def setup_inputs_huge(rng):
    d = numbers_of(rng)
    o = rng.permutation(N) % 4
    c, a = np.ones((N, C)), np.ones((N, 128))
    for r in range(N):
        if o[r] == 0: a[r] = -1
        if o[r] == 2: c[r] = rng.permutation(C) % 2 * 2.0 - 1.0
        if o[r] == 3: a[r] = rng.permutation(128) % 2 * 2.0 - 1.0
    x = 2.0 ** 30 * (0.6 + 0.4 * rng.random((N, 128, C, 4))) * c[:, None, :, None]
    u = 2.0 ** 30 * (1 - 0.25 * rng.random((N, 128, 128, 4))) * a[:, None, :, None]
    return {"x": x.astype(np.float32).reshape(N, 128, 4 * C).astype(BF), "u": u.astype(np.float32).reshape(N, 128, 512).astype(BF), "v": d["v"], **still(rng)}
def setup_inputs_spread(rng):
    d = setup_inputs(rng)
    d["x"] = wide(rng, N, 128, 4 * C, cols=6)
    return d
def check_inputs(d):
    b = []
    for k in ("x", "u", "v"):
        a = np.abs(d[k].astype(np.float32))
        if not (np.isfinite(a).all() and ((a == 0) | (a >= 2.0 ** -30) & (a <= 2.0 ** 30)).all()): b.append("a value of " + k)
    if np.isin(d["wc"], (127, 255)).any(): b.append("a code of wc")
    none, low, high = [int(mx_ref.quantize(np.full((128, 16), k, np.float32).astype(BF))[1].max()) for k in (0.0, 2.0 ** -30, 2.0 ** 30)]
    s = np.stack([mx_ref.live(p) for p in d["ws"]])
    if not ((s == none) | (s >= low) & (s <= high)).all(): b.append("a scale of ws")
    return b
def reference(x, u, v, wc, ws):
    qu = [mx_ref.quantize(u[r]) for r in range(N)]
    lay = [pk(wc[r], ws[r]) for r in range(N)]
    now = [mx_ref.quantize(x[r]) for r in range(N)]
    for t in range(R):
        g, o, sent = [], [], []
        for r in range(N):
            p = mx_ref.matmul(qu[r], now[r])
            g.append(match(p))
            o.append(order(p, g[r]))
            sent.append(mx_ref.quantize(sung(decode(now[r]).astype(BF), g[r], o[r])))
        for r in range(N):
            m = join(*[pick(sent[s], np.arange(L * r, L * r + L)) for s in range(N)])
            z = np.stack([np.maximum(mx_ref.matmul(pick(lay[r], np.arange(128 * b, 128 * b + 128)), m), np.float32(0.0)) * np.float32(0.03125) for b in range(4)], axis=2)
            now[r] = mx_ref.quantize((decode(m) + z.reshape(128, -1)).astype(BF))
    y, ol = np.zeros((N, 128, C), np.float32), np.zeros((N, 8, 2 * C), np.float32)
    oc, osc = np.zeros((N, 128, 4 * C), np.uint8), np.zeros((N, 16, C), np.uint8)
    for r in range(N):
        y[r] = mx_ref.matmul(mx_ref.quantize(v[r]), now[r])
        ol[r] = np.concatenate([o[r], g[r]], axis=1)
        oc[r], osc[r] = emit(now[r])
    return {"y": y, "ol": ol, "oc": oc, "osc": osc}

@@ -1,0 +1,437 @@
+from concourse.bass import DstId, RemoteDMATransfer
+from concourse.mybir import dt, AluOpType, AxisListType, ActivationFunctionType
+
+N, C, L, R = 8, 256, 32, 3
+F32, BF, I32, U16, Q8, U8 = "float32", "bfloat16", "int32", "uint16", "float8_e4m3fn_x4", "uint8"
+PEN = 2.0 ** 94
+ROWPEN = 16 * PEN
+BIG = 2.0 ** 90
+KL = 8192.0
+EW = 144
+LEAD = 27
+CT = [(0, 256, ["d", 15, 14, 13]), (256, 192, [12, 11, 10, 9]), (448, 128, [8, 7, 6, 5]), (576, 128, [4, 3, 2, 1])]
+
+SCRATCH = {}
+for _n, _w, _d in [("xin", 1024, BF), ("uin", 512, BF), ("vin", 512, BF), ("X", 1024, BF), ("Bt", 1024, BF),
+                   ("Ez", 4 * EW + 4, BF), ("Kb", 512, BF), ("Kl", 512, BF), ("At", 512, BF), ("Ct", 4 * 704, BF),
+                   ("Wn", 8192, BF), ("Sw", 2048, F32), ("CW", 2048, F32), ("CG", 2048, F32), ("Rb", 1024, F32),
+                   ("pi", 4, I32), ("pt", 4, I32), ("pf", 4, F32), ("stg", 104, F32), ("offc", 104, U16),
+                   ("gd0", 128, BF), ("gd", 256, BF), ("hc", 128, BF), ("dh", 128, BF),
+                   ("di", 8, I32), ("dj", 8, I32), ("df", 8, F32), ("j16", 256, F32), ("jr", 256, F32),
+                   ("ab", 256, F32), ("nq", 256, F32), ("cap", 256, F32), ("kap", 256, F32), ("rst", 256, F32),
+                   ("sgj", 256, F32), ("keep", 256, BF), ("mka", 128, BF), ("cl", 16, F32), ("cr", 16, F32), ("cor", 4, F32),
+                   ("Sp", 128, F32), ("mm", 4, F32), ("ne", 128, BF), ("fg", 128, BF), ("fh", 128, BF),
+                   ("rp", 128, BF), ("cp", 128, BF), ("rc", 128, BF),
+                   ("t0", 16, F32), ("t1", 16, F32), ("t2", 16, F32), ("t3", 16, F32), ("t4", 16, F32), ("t5", 16, F32),
+                   ("t6", 32, F32), ("sg", 4, F32),
+                   ("l1f", 16, F32), ("l1", 16, U16), ("Rr", 256, F32), ("Rm", 256, F32), ("Lt", 256, F32), ("Pr", 256, F32),
+                   ("sn", 256 * 3, BF), ("junk", 1280, BF), ("rs", 16, F32), ("ds", 256, BF), ("u1", 16, F32), ("u2", 16, F32),
+                   ("ex", 256, F32), ("rkf", 16, F32), ("rk", 16, U16), ("Or", 256, F32), ("ex2", 256, F32), ("l2", 16, U16),
+                   ("oi", 256, I32), ("oj", 256, I32), ("OL", 512, F32), ("ys", 256, F32)]:
+    SCRATCH[_n] = ("sbuf", [128, _w], _d)
+for _n, _w in [("u", 128), ("u1c", 128), ("uR", 1024), ("v", 128), ("W", 512), ("T", 256), ("E", 4 * EW), ("K", 128),
+               ("L", 128), ("A", 128), ("C", 704)] + [("B%d" % _t, 256) for _t in range(R)] + [("M%d" % _t, 256) for _t in range(R)]:
+    SCRATCH["q" + _n] = ("sbuf", [128, _w], Q8)
+    SCRATCH["s" + _n] = ("sbuf", [128, _w], U8)
+for _b in range(8):
+    SCRATCH["ps%d" % _b] = ("psum", [128, 512], F32)
+
+SEMAPHORES = (["cv", "cs", "ct", "cg", "ldx", "ldu", "ldw", "ldv", "rot0", "rot1", "outs", "sent"]
+              + ["arr%d%d" % (_t, _k) for _t in range(R) for _k in range(2)])
+
+
+def deal(T, topo, s, k):
+    src = T.cores[s]
+    others = [d for d in [(s + i) % N for i in range(1, N)] if d // 4 == k]
+    far = [d for d in others if topo.chip(T.cores[d]) != topo.chip(src)]
+    eng = topo.engines(src, T.cores[far[0]])
+    each = len(eng) // len(far)
+    out = [(d, eng[each * i:each * i + each]) for i, d in enumerate(far)]
+    return out + [(d, [e for e in topo.engines(src, T.cores[d]) if e not in eng]) for d in others if d not in far]
+
+
+def rank_program(g, core, T, topo):
+    rank = T.rank_of(core)
+    if rank is None:
+        return
+    A, AF, AX = AluOpType, ActivationFunctionType, AxisListType.X
+    Q = {"v": g.vector, "s": g.scalar, "t": g.tensor, "g": g, "y": g.sync}
+    V, S, P = g.vector, g.scalar, g.tensor
+    cnt, seen, wr, rd, turn = {}, {}, {}, {}, [0]
+
+    def need(q, reads, writes, skip=None):
+        want = {}
+        toks = [wr[k] for k in reads + writes if k in wr]
+        for k in writes:
+            toks += rd.get(k, [])
+        for sem, val in toks:
+            want[sem] = max(want.get(sem, 0), cnt[sem] if val is None else val)
+        for sem, val in want.items():
+            if sem != skip and seen.get((q, sem), 0) < val:
+                Q[q].wait_ge(T.sem[sem], val)
+                seen[(q, sem)] = val
+
+    def note(tok, reads, writes):
+        for k in reads:
+            rd.setdefault(k, []).append(tok)
+        for k in writes:
+            wr[k] = tok
+            rd[k] = []
+
+    def op(q, reads, writes, fn):
+        reads, writes = reads.split(), writes.split()
+        need(q, reads, writes)
+        sem = "c" + q
+        fn().then_inc(T.sem[sem], 1)
+        cnt[sem] = cnt.get(sem, 0) + 1
+        note((sem, cnt[sem]), reads, writes)
+
+    def dma(q, sem, reads, writes, out, in_):
+        reads, writes = reads.split(), writes.split()
+        need(q, reads, writes, sem)
+        Q[q].dma_start(out, in_).then_inc(T.sem[sem], 16)
+        cnt[sem] = cnt.get(sem, 0) + 16
+        note((sem, None), reads, writes)
+
+    def ts(r, w, out, in0, s1, o0, s2=None, o1=None):
+        if o1 is None:
+            op("v", r, w, lambda: V.tensor_scalar(out, in0, s1, None, o0))
+        else:
+            op("v", r, w, lambda: V.tensor_scalar(out, in0, s1, s2, o0, o1))
+
+    def tt(r, w, out, in0, in1, o):
+        op("v", r, w, lambda: V.tensor_tensor(out, in0, in1, o))
+
+    def cp(r, w, out, in_):
+        op("v", r, w, lambda: V.tensor_copy(out, in_))
+
+    def scan(r, w, out, d0, d1, o0, o1):
+        op("v", r, w, lambda: V.tensor_tensor_scan(out, d0, d1, 0.0, o0, o1))
+
+    def red(r, w, out, in_, o, neg=False):
+        op("v", r, w, lambda: V.tensor_reduce(out, in_, AX, o, negate=neg))
+
+    def act(r, w, out, in_, f, **kw):
+        op("s", r, w, lambda: S.activation(out, in_, f, **kw))
+
+    def quant(r, w, n, a, b, in_):
+        op("v", r, w, lambda: V.quantize_mx(T["q" + n][:, a:b], T["s" + n][:, a:b], in_))
+
+    def mm(r, w, bank, n, l, la, m, ma, start=True, stop=True):
+        op("t", r, w, lambda: P.matmul_mx(T["ps%d" % bank][:, 0:n], T["q" + l][:, la:la + 128], T["s" + l][:, la:la + 128],
+                                          T["q" + m][:, ma:ma + n], T["s" + m][:, ma:ma + n], start, stop))
+
+    def prod(r, l, la, m, k):
+        bk = 2 + turn[0] % 6
+        turn[0] += 1
+        mm(r, "p%d" % bk, bk, 128, l, la, m, 128 * k)
+        return "p%d" % bk, T["ps%d" % bk][:, 0:128]
+
+    def iota(w, out, pat, base, cm=0, small=True):
+        if small:
+            op("g", "", w, lambda: g.iota(out, pat, base, cm, allow_small_or_imprecise_dtypes=True))
+        else:
+            op("g", "", w, lambda: g.iota(out, pat, base, cm))
+
+    def sel(k, ap, pat, cmp, fill, base, cm):
+        op("g", k, k, lambda: g.affine_select(ap, ap, pat, cmp, fill, base, cm))
+
+    def words(n, a, b):
+        return T["q" + n][:, a:b].bitcast(dt.uint32)
+
+    def bytes_of(n, a, b):
+        return T["q" + n][:, a:b].bitcast(dt.uint8)
+
+    dma("s", "ldu", "", "uin", T.uin[:], T.u[:])
+    dma("y", "ldx", "", "xin", T.xin[:], T.x[:])
+    dma("y", "ldw", "", "qW", bytes_of("W", 0, 512), T.wc[:])
+    dma("y", "ldw", "", "sW", T.sW[:], T.ws[:])
+    dma("y", "ldv", "", "vin", T.vin[:], T.v[:])
+
+    icol, c8col = T.pf[:, 0:1], T.pf[:, 1:2]
+    for key, ap, val in [("Ez", T.Ez[:], 0.0), ("dg", T.gd[:, 128:256], 0.0), ("dh", T.dh[:], 1.0), ("dg", T.gd[:, 135:256:8], -PEN),
+                         ("dh", T.dh[:, 7:128:8], -7.0), ("dg", T.gd[:, 191:256:64], -8 * PEN), ("dh", T.dh[:, 63:128:64], 0.0)]:
+        op("v", "", key, lambda: V.memset(ap, val))
+    iota("pi", T.pi[:, 0:1], [[0, 1]], 0, 1, small=False)
+    iota("s64", T.stg[:, 64:72], [[0, 2], [-32, 4]], 119)
+    iota("s88", T.stg[:, 88:104], [[16, 16]], 0)
+    iota("s72", T.stg[:, 72:88], [[0, 2], [-1, 8]], 7)
+    iota("s0", T.stg[:, 0:64], [[16, 8], [1, 8]], 0)
+    ez = T.Ez[:, 3:4 * EW + 3:4]
+    sel("Ez", ez, [[1, EW]], A.not_equal, 1.0, 0, -1)
+    sel("Ez", ez, [[1, EW]], A.not_equal, 1.0, -128, -1)
+    ts("pi", "pt0", T.pt[:, 0:1], T.pi[:, 0:1], 15, A.bitwise_and)
+    ts("pi", "pt1", T.pt[:, 1:2], T.pi[:, 0:1], 8, A.bitwise_and)
+    cp("pt0 pt1", "pf", T.pf[:, 0:2], T.pt[:, 0:2])
+    ts("pf s64", "s64", T.stg[:, 64:72], T.stg[:, 64:72], icol, A.subtract, c8col, A.subtract)
+    ts("pf s88", "s88", T.stg[:, 88:104], T.stg[:, 88:104], icol, A.add)
+    cp("s0 s64 s72 s88", "offc", T.offc[:], T.stg[:])
+    for b in range(3):
+        quant("Ez", "E%d" % b, "E", EW * b, EW * b + EW, T.Ez[:, 3 - b:3 - b + 4 * EW])
+    iota("gd0", T.gd0[:], [[0, 2], [-1, 8], [0, 8]], 15)
+    iota("hc", T.hc[:], [[0, 16], [-1, 8]], 7)
+    quant("uin", "u", "u", 0, 128, T.uin[:])
+    cp("u offc", "qu1c", words("u1c", 0, 128), words("u", 0, 128).indirect(T.offc[:, 64:72]))
+    act("u offc", "su1c", T.su1c[:], T.su[:].indirect(T.offc[:, 64:72]), AF.Copy)
+    act("u offc", "suR", T.suR[:], T.su[:].indirect(T.offc[:, 0:64]), AF.Copy)
+    cp("u offc", "quR", words("uR", 0, 1024), words("u", 0, 128).indirect(T.offc[:, 0:64]))
+
+    def late_constants_g():
+        iota("j16", T.j16[:], [[0, 16], [1, 16]], 0)
+        iota("di", T.di[:], [[16, 8]], 143, -1, small=False)
+        iota("jr", T.jr[:], [[4096, 2], [1, 128]], 0)
+        iota("Kl", T.Kl[:, 64:512], [[0, 448]], 0)
+        kl = T.Kl[:, 0:64]
+        iota("Kl", kl, [[0, 64]], 256)
+        sel("Kl", kl, [[-1, 2], [0, 8], [1, 4]], A.is_equal, 0.0, 0, 0)
+        sel("Kl", kl, [[0, 2], [-16, 8], [0, 4]], A.is_ge, 0.0, 0, 1)
+        sel("Kl", kl, [[0, 2], [16, 8], [0, 4]], A.is_ge, 0.0, 15, -1)
+        iota("A0 A1", T.At[:], [[0, 512]], 0)
+        iota("Kb", T.Kb[:], [[0, 512]], 1)
+        sel("Kb", T.Kb[:], [[-16, 8], [0, 64]], A.is_ge, 0.0, 0, 1)
+        sel("Kb", T.Kb[:], [[16, 8], [0, 64]], A.is_ge, 0.0, 15, -1)
+        for a, n, cs in CT:
+            lo = 4 * (a + 16 * cs[3])
+            iota(" ".join("C%s" % c for c in cs), T.Ct[:, lo:4 * (a + n)], [[0, 4 * (a + n) - lo]], 0)
+        iota("rs0", T.rs[:, 0:1], [[0, 1]], 0)
+        iota("Or", T.Or[:], [[0, 256]], 0)
+        iota("CG", T.CG[:], [[1, 8], [0, 256]], 0)
+
+    def late_constants_s():
+        act("j16 pf", "ab", T.ab[:], T.j16[:], AF.Abs, bias=icol, scale=-1.0)
+        act("ab", "nq", T.nq[:], T.ab[:], AF.Sign)
+        act("j16", "sgj", T.sgj[:], T.j16[:], AF.Sign)
+        act("nq", "mka", T.mka[:], T.nq[:, 0:128], AF.Identity, bias=1.0, scale=-1.0)
+        act("nq", "cap", T.cap[:], T.nq[:], AF.Identity, bias=-BIG, scale=2 * BIG)
+        act("nq", "kap", T.kap[:], T.nq[:], AF.Identity, bias=16 * KL, scale=-17 * KL)
+        act("sgj", "rst", T.rst[:], T.sgj[:], AF.Identity, bias=BIG, scale=-2 * BIG)
+        act("sgj", "keep", T.keep[:], T.sgj[:], AF.Copy)
+        act("pf", "cor", T.cor[:, 0:1], icol, AF.Identity, bias=15 * KL, scale=-KL)
+        act("s88", "cl", T.cl[:], T.stg[:, 88:104], AF.Identity, bias=896.0)
+        act("s88 cor", "cr", T.cr[:], T.stg[:, 88:104], AF.Identity, bias=T.cor[:, 0:1])
+
+    def offsets_window():
+        ts("di", "dj", T.dj[:], T.di[:], 4, A.arith_shift_right, 7, A.bitwise_and)
+        quant("Kl", "L", "L", 0, 128, T.Kl[:])
+        ts("dj", "df", T.df[:], T.dj[:], 512.0, A.mult)
+        for k in range(8):
+            act("jr df", "CW%d" % k, T.CW[:, 256 * k:256 * k + 256], T.jr[:], AF.Identity, bias=T.df[:, k:k + 1])
+
+    wall = " ".join(n + str(k) for k in range(2) for n in ["W0_%d" % i for i in range(8)] + ["W1a", "W1b", "W2a", "W2b", "W3a", "W3b"])
+    sw = " ".join("Sw%d%d" % (i, k) for i in range(8) for k in range(2))
+    cw = " ".join("CW%d" % i for i in range(8))
+
+    def parts(k):
+        w0, o = " ".join("W0_%d%d" % (i, k) for i in range(8)), 4096 * k
+        for i in range(8):
+            key, ps = prod("T%d E%d" % (k, i % 4), "E", EW * (i % 4) + 16 * (i // 4), "T", k)
+            act(key, "W0_%d%d" % (i, k), T.Wn[:, o + 128 * i:o + 128 * i + 128], ps, AF.Copy)
+        for q in range(1, 4):
+            n, rot = 32 * q, "rot%d" % k
+            dma("y", rot, w0, "W%da%d" % (q, k), T.Wn[0:128 - n, o + 1024 * q:o + 1024 * q + 1024], T.Wn[n:128, o:o + 1024])
+            dma("y", rot, w0, "W%db%d" % (q, k), T.Wn[128 - n:128, o + 1024 * q:o + 1024 * q + 1024], T.Wn[0:n, o:o + 1024])
+
+    def likings(k):
+        for i in range(8):
+            key, ps = prod("T%d quR suR" % k, "uR", 128 * i, "T", k)
+            o = 256 * i + 128 * k
+            act(key, "Sw%d%d" % (i, k), T.Sw[:, o:o + 128], ps, AF.Copy)
+
+    def state(t, k):
+        Mn = "M%d" % t
+
+        def one(b):
+            kw, pw = prod("M%d mq ms qW sW" % k, "W", 128 * b, Mn, k)
+            kd, pd = prod("M%d mq ms E%d" % (k, b), "E", EW * b, Mn, k)
+            rb = T.Rb[:, 256 * b + 128 * k:256 * b + 128 * k + 128]
+            act(kw, "R%d%d" % (b, k), rb, pw, AF.Relu, scale=0.03125)
+            tt(kd + " R%d%d" % (b, k), "X%d%d" % (b, k), T.X[:, 512 * k + b:512 * k + 512:4], pd, rb, A.add)
+        return [lambda b=b: one(b) for b in range(4)] + [lambda: quant(
+            " ".join("X%d%d" % (b, k) for b in range(4)), "T%d" % k, "T", 128 * k, 128 * k + 128, T.X[:, 512 * k:512 * k + 512])]
+
+    def matching(ks, extra):
+        out = []
+        lo, hi = 64 * ks[0], 64 * ks[-1] + 64
+
+        def each(fn):
+            for k in ks:
+                out.append(lambda k=k: fn(k, 64 * k, 64 * k + 64))
+
+        def keys(n):
+            return " ".join(n + str(k) for k in ks)
+
+        for step in range(7):
+            def src(k, step=step):
+                return (T["ps%d" % k][:, 0:64], "p%d" % k) if step == 0 else (T.Sp[:, 64 * k:64 * k + 64], "Sp%d" % k)
+            each(lambda k, a, b, src=src: red(src(k)[1], "mm%d" % k, T.mm[:, k:k + 1], src(k)[0], A.max))
+            if step == 6:
+                each(lambda k, a, b: tt("Sp%d" % k, "t0%d" % k, T.t0[:, 8 * k:8 * k + 8], T.Sp[:, a:a + 8], T.Sp[:, a + 8:a + 16], A.min))
+            each(lambda k, a, b, src=src: ts(src(k)[1] + " mm%d" % k, "ne%d" % k, T.ne[:, a:b], src(k)[0], T.mm[:, k:k + 1], A.is_lt))
+            if step == 6:
+                each(lambda k, a, b: tt("Sp%d t0%d" % (k, k), "t1%d" % k, T.t1[:, 8 * k:8 * k + 8], T.t0[:, 8 * k:8 * k + 8],
+                                        T.Sp[:, a + 16:a + 24], A.min))
+            out.append(lambda: scan(keys("ne") + " dg", keys("fg"), T.fg[:, lo:hi], T.ne[:, lo:hi], T.gd[:, 128 + lo:128 + hi], A.mult, A.add))
+            out.append(lambda: scan(keys("ne") + " dh", keys("fh"), T.fh[:, lo:hi], T.ne[:, lo:hi], T.dh[:, lo:hi], A.mult, A.add))
+            if step == 6:
+                break
+            each(lambda k, a, b: ts("gd fg%d" % k, "rp%d" % k, T.rp[:, a:b], T.gd[:, a:b], T.fg[:, b - 1:b], A.is_equal, -ROWPEN, A.mult))
+            each(lambda k, a, b: ts("hc fg%d fh%d" % (k, k), "cp%d" % k, T.cp[:, a:b], T.hc[:, a:b], T.fh[:, b - 1:b], A.is_equal,
+                                    T.fg[:, b - 1:b], A.mult))
+            each(lambda k, a, b: tt("rp%d cp%d" % (k, k), "rc%d" % k, T.rc[:, a:b], T.rp[:, a:b], T.cp[:, a:b], A.add))
+            each(lambda k, a, b, src=src: tt(src(k)[1] + " rc%d" % k, "Sp%d" % k, T.Sp[:, a:b], src(k)[0], T.rc[:, a:b], A.add))
+            if step in extra:
+                out.append(extra[step])
+        lo8, hi8 = lo // 8, hi // 8
+        each(lambda k, a, b: ts("hc fg%d fh%d" % (k, k), "t2%d" % k, T.t2[:, 8 * k:8 * k + 8], T.hc[:, 0:8], T.fh[:, b - 1:b], A.is_equal,
+                                T.fg[:, b - 1:b], A.mult))
+        out.append(lambda: tt(keys("t1") + " " + keys("t2"), keys("t3"), T.t3[:, lo8:hi8], T.t1[:, lo8:hi8], T.t2[:, lo8:hi8], A.add))
+        out.append(lambda: ts(keys("t3"), keys("t4"), T.t4[:, lo8:hi8], T.t3[:, lo8:hi8], -1.0 / PEN, A.mult, -27.5, A.add))
+        each(lambda k, a, b: red("t4%d" % k, "sg%d" % k, T.sg[:, k:k + 1], T.t4[:, 8 * k:8 * k + 8], A.add, True))
+        each(lambda k, a, b: ts("t4%d sg%d" % (k, k), "t5%d" % k, T.t5[:, 8 * k:8 * k + 8], T.t4[:, 8 * k:8 * k + 8], -11.5, A.is_equal,
+                                T.sg[:, k:k + 1], A.mult))
+        out.append(lambda: tt(keys("t4") + " " + keys("t5"), keys("t6"), T.t6[:, lo8:hi8], T.t4[:, lo8:hi8], T.t5[:, lo8:hi8], A.add))
+        each(lambda k, a, b: tt("t6%d offc mka" % k, "A%d" % k, T.At[:, k:512:4], T.t6[:, 8 * k:8 * k + 8].indirect(T.offc[:, 72:80]),
+                                T.mka[:], A.mult))
+        return out
+
+    def scores(k):
+        mm("T%d qu1c su1c" % k, "p%d" % k, k, 128, "T", 128 * k, "u1c", 0)
+
+    def merge(first, second):
+        for f in first[:LEAD]:
+            f()
+        rest = first[LEAD:]
+        for i in range(max(len(rest), len(second))):
+            if i < len(second):
+                second[i]()
+            if i < len(rest):
+                rest[i]()
+
+    def slot(c):
+        for a, n_, cs in CT:
+            if c in cs:
+                return T.Ct[:, 4 * a + cs.index(c):4 * (a + (256 if c == "d" else 16 * c)):4]
+
+    def compare(c):
+        ts("Rr Lt", "C%d" % c, slot(c), T.Rr[:, 0:16 * c], T.Lt[:, 16 * c + 15:16 * c + 16], A.is_lt)
+
+    def rowsum(c):
+        o = 8 * c * (c - 1)
+        act("C%d" % c, "rs%d" % c, T.junk[:, o:o + 16 * c], slot(c), AF.Copy, accum_out=T.rs[:, c:c + 1])
+
+    def sums(i):
+        a, n_, cs = CT[i]
+        quant(" ".join("C%s" % c for c in cs), "c%d" % i, "C", a, a + n_, T.Ct[:, 4 * a:4 * (a + n_)])
+        mm("K c%d" % i, "p1" if i == 0 else "", 1, n_, "K", 0, "C", a, i == 0, i == 3)
+
+    ka, kb = rank // 4, 1 - rank // 4
+    for t in range(R):
+        if t == 0:
+            quant("xin", "T0 T1", "T", 0, C, T.xin[:])
+            scores(0)
+            scores(1)
+            ts("gd0", "gd", T.gd[:, 0:128], T.gd0[:], -PEN, A.mult)
+            quant("Ez", "E3", "E", EW * 3, EW * 4, T.Ez[:, 0:4 * EW])
+            parts(0)
+            parts(1)
+            late_constants_g()
+            likings(0)
+            likings(1)
+            late_constants_s()
+            for f in matching([0, 1], {3: offsets_window}):
+                f()
+        else:
+            merge(state(t - 1, ka) + [lambda: (scores(ka), parts(ka))] + matching([ka], {}),
+                  state(t - 1, kb) + [lambda: (scores(kb), parts(kb), likings(ka), likings(kb))] + matching([kb], {}))
+        quant("A0 A1", "A", "A", 0, 128, T.At[:])
+        mm("A L", "p0", 0, 128, "A", 0, "L", 0)
+        if t == 0:
+            quant("Kb", "K", "K", 0, 128, T.Kb[:])
+        tt("p0 cl", "l1f", T.l1f[:], T.ps0[:, 0:16], T.cl[:], A.add)
+        cp("l1f", "l1", T.l1[:], T.l1f[:])
+        act(sw + " l1", "Rr", T.Rr[:], T.Sw[:].indirect(T.l1[:]), AF.Copy)
+        tt(sw + " l1 cap", "Rm", T.Rm[:], T.Sw[:].indirect(T.l1[:]), T.cap[:], A.max)
+        scan("rst Rm", "Lt", T.Lt[:], T.rst[:], T.Rm[:], A.max, A.min)
+        act(cw + " l1", "Pr", T.Pr[:], T.CW[:].indirect(T.l1[:]), AF.Copy)
+        for i, c in enumerate((15, 14, 13)):
+            act("Rr Lt", "sn%d" % i, T.sn[:, 256 * i:256 * i + 16 * c], T.Rr[:, 0:16 * c], AF.Sign,
+                bias=T.Lt[:, 16 * c + 15:16 * c + 16], scale=-1.0)
+        for i, c in enumerate((15, 14, 13)):
+            act("sn%d" % i, "C%d rs%d" % (c, c), slot(c), T.sn[:, 256 * i:256 * i + 16 * c], AF.Relu, accum_out=T.rs[:, c:c + 1])
+        for c in (12, 11, 10, 9):
+            compare(c)
+            rowsum(c)
+        tt("Rr Lt", "Cd", slot("d"), T.Lt[:], T.Rr[:], A.is_ge)
+        compare(8)
+        scan("keep Cd", "ds", T.ds[:], T.keep[:], slot("d"), A.mult, A.add)
+        sums(0)
+        sums(1)
+        for c in (7, 6, 5, 4):
+            compare(c)
+        sums(2)
+        for c in (3, 2, 1):
+            compare(c)
+        for c in range(8, 0, -1):
+            rowsum(c)
+        tt("cr ds", "u1", T.u1[:], T.cr[:], T.ds[:, 15:256:16], A.subtract)
+        sums(3)
+        wr["p1"] = ("ct", cnt["ct"])
+        scan("kap p1", "ex", T.ex[:], T.kap[:], T.ps1[:, 0:C], A.add, A.min)
+        tt("u1 " + " ".join("rs%d" % c for c in range(16)), "u2", T.u2[:], T.u1[:], T.rs[:], A.subtract)
+        tt("ex u2", "rkf", T.rkf[:], T.ex[:, 15:256:16], T.u2[:], A.add)
+        cp("rkf", "rk", T.rk[:], T.rkf[:])
+        cp("Pr rk", "Or", T.Or[:].indirect(T.rk[:]), T.Pr[:])
+        scan("kap Or", "ex2", T.ex2[:], T.kap[:], T.Or[:], A.add, A.min)
+        ts("ex2 cor", "l2", T.l2[:], T.ex2[:, 15:256:16], T.cor[:, 0:1], A.add)
+        Bn, Mn = "B%d" % t, "M%d" % t
+        for k in (ka, kb):
+            for b in range(4):
+                win = T.Wn[:, 128 * b:128 * b + 7808].indirect(T.l2[:, 8 * k:8 * k + 8])
+                out = T.Bt[:, 512 * k + b:512 * k + 512:4]
+                if b % 2:
+                    act(wall + " l2", "B%d%d" % (b, k), out, win, AF.Copy)
+                else:
+                    cp(wall + " l2", "B%d%d" % (b, k), out, win)
+            quant(" ".join("B%d%d" % (b, k) for b in range(4)), "qB%d" % k, Bn, 128 * k, 128 * k + 128, T.Bt[:, 512 * k:512 * k + 512])
+            need("g", ["qB%d" % k], [])
+            for codes in (True, False):
+                trs = []
+                for d, eng in deal(T, topo, rank, k):
+                    rid, pid = topo.addr(T.cores[d])[0:2]
+                    if codes:
+                        s_, d_ = bytes_of(Bn, L * d, L * d + L), bytes_of(Mn, L * rank, L * rank + L)
+                    else:
+                        s_, d_ = T["s" + Bn][:, L * d:L * d + L], T["s" + Mn][:, L * rank:L * rank + L]
+                    trs.append(RemoteDMATransfer(dst_ids=[DstId(rid=rid, pnc=pid)], dma_engine_mask=sum(1 << e for e in eng),
+                                                 remote_sem=T.sem["arr%d%d" % (t, ka)], src=s_, dst=d_))
+                    cnt["sent"] = cnt.get("sent", 0) + len(eng)
+                g.remote_dma_fused(trs, local_sem=T.sem.sent)
+        own = T.offc[:, 88:90]
+        cp("offc qB%d" % ka, "mq", words(Mn, L * rank, L * rank + L), words(Bn, L * rank, L * rank + L).indirect(own))
+        cp("offc qB%d" % ka, "ms", T["s" + Mn][:, L * rank:L * rank + L], T["s" + Bn][:, L * rank:L * rank + L].indirect(own))
+        for k in range(2):
+            arr = "arr%d%d" % (t, k)
+            cnt[arr] = sum(2 * len(e) for s in range(4 * k, 4 * k + 4) if s != rank for d, e in deal(T, topo, s, ka) if d == rank)
+            wr["M%d" % k] = (arr, cnt[arr])
+
+    quant("vin", "v", "v", 0, 128, T.vin[:])
+    cp("Or", "oi", T.oi[:], T.Or[:])
+    act("CG l1", "OLg", T.OL[:, 256:512], T.CG[:].indirect(T.l1[:]), AF.Copy)
+    ts("oi", "oj", T.oj[:], T.oi[:], 127, A.bitwise_and)
+    ts("oi", "oi", T.oi[:], T.oi[:], 5, A.arith_shift_right, 128, A.bitwise_and)
+    tt("oi oj", "OLo", T.OL[:, 0:256], T.oi[:], T.oj[:], A.add)
+    dma("y", "outs", "OLo OLg", "", T.ol[:], T.OL[0:128:16, :])
+    for k in (ka, kb):
+        a, b = 128 * k, 128 * k + 128
+        for f in state(R - 1, k):
+            f()
+        mm("T%d v" % k, "p%d" % k, k, 128, "v", 0, "T", a)
+        dma("y", "outs", "T%d" % k, "", T.oc[:, 4 * a:4 * b], bytes_of("T", a, b))
+        if k == kb:
+            for i in range(4):
+                dma("s" if i % 2 else "y", "outs", "T0 T1", "", T.osc[4 * i:4 * i + 4, :], T.sT[32 * i:32 * i + 4, :])
+        cp("p%d" % k, "ys%d" % k, T.ys[:, a:b], T["ps%d" % k][:, 0:128])
+        dma("s", "outs", "ys%d" % k, "", T.y[:, a:b], T.ys[:, a:b])
+    for sem in cnt:
+        if seen.get(("g", sem), 0) < cnt[sem]:
+            g.wait_ge(T.sem[sem], cnt[sem])

@@ -8,7 +8,7 @@ ROWPEN = 16 * PEN
 BIG = 2.0 ** 90
 KL = 8192.0
 EW = 144
-LEAD = 27
+LEAD = 15
 CT = [(0, 256, ["d", 15, 14, 13]), (256, 192, [12, 11, 10, 9]), (448, 128, [8, 7, 6, 5]), (576, 128, [4, 3, 2, 1])]
 
 SCRATCH = {}
@@ -199,20 +199,21 @@ def rank_program(g, core, T, topo):
 
     def late_constants_s():
         act("j16 pf", "ab", T.ab[:], T.j16[:], AF.Abs, bias=icol, scale=-1.0)
-        act("ab", "nq", T.nq[:], T.ab[:], AF.Sign)
         act("j16", "sgj", T.sgj[:], T.j16[:], AF.Sign)
-        act("nq", "mka", T.mka[:], T.nq[:, 0:128], AF.Identity, bias=1.0, scale=-1.0)
-        act("nq", "cap", T.cap[:], T.nq[:], AF.Identity, bias=-BIG, scale=2 * BIG)
-        act("nq", "kap", T.kap[:], T.nq[:], AF.Identity, bias=16 * KL, scale=-17 * KL)
+        act("pf", "cor", T.cor[:, 0:1], icol, AF.Identity, bias=15 * KL, scale=-KL)
+        act("ab", "nq", T.nq[:], T.ab[:], AF.Sign)
         act("sgj", "rst", T.rst[:], T.sgj[:], AF.Identity, bias=BIG, scale=-2 * BIG)
         act("sgj", "keep", T.keep[:], T.sgj[:], AF.Copy)
-        act("pf", "cor", T.cor[:, 0:1], icol, AF.Identity, bias=15 * KL, scale=-KL)
+        act("nq", "mka", T.mka[:], T.nq[:, 0:128], AF.Identity, bias=-1.0 / PEN, scale=1.0 / PEN)
+        act("nq", "cap", T.cap[:], T.nq[:], AF.Identity, bias=-BIG, scale=2 * BIG)
+        act("nq", "kap", T.kap[:], T.nq[:], AF.Identity, bias=16 * KL, scale=-17 * KL)
         act("s88", "cl", T.cl[:], T.stg[:, 88:104], AF.Identity, bias=896.0)
         act("s88 cor", "cr", T.cr[:], T.stg[:, 88:104], AF.Identity, bias=T.cor[:, 0:1])
 
     def offsets_window():
         ts("di", "dj", T.dj[:], T.di[:], 4, A.arith_shift_right, 7, A.bitwise_and)
         quant("Kl", "L", "L", 0, 128, T.Kl[:])
+        quant("Kb", "K", "K", 0, 128, T.Kb[:])
         ts("dj", "df", T.df[:], T.dj[:], 512.0, A.mult)
         for k in range(8):
             act("jr df", "CW%d" % k, T.CW[:, 256 * k:256 * k + 256], T.jr[:], AF.Identity, bias=T.df[:, k:k + 1])
@@ -252,46 +253,62 @@ def rank_program(g, core, T, topo):
     def matching(ks, extra):
         out = []
         lo, hi = 64 * ks[0], 64 * ks[-1] + 64
+        lo8, hi8 = lo // 8, hi // 8
 
-        def each(fn):
-            for k in ks:
-                out.append(lambda k=k: fn(k, 64 * k, 64 * k + 64))
+        def level(*fns):
+            out.append(lambda: [fn(k, 64 * k, 64 * k + 64) for fn in fns for k in (ks if fn not in once else ks[:1])])
 
         def keys(n):
             return " ".join(n + str(k) for k in ks)
 
+        def row(k, a, b):
+            scan(keys("ne") + " dg", keys("fg"), T.fg[:, lo:hi], T.ne[:, lo:hi], T.gd[:, 128 + lo:128 + hi], A.mult, A.add)
+
+        def col(k, a, b):
+            scan(keys("ne") + " dh", keys("fh"), T.fh[:, lo:hi], T.ne[:, lo:hi], T.dh[:, lo:hi], A.mult, A.add)
+
+        def centred(k, a, b):
+            ts(keys("t1"), keys("t4"), T.t4[:, lo8:hi8], T.t1[:, lo8:hi8], 27.5 * PEN, A.add)
+
+        def seventh(k, a, b):
+            tt(keys("t4") + " " + keys("t2"), keys("t3"), T.t3[:, lo8:hi8], T.t4[:, lo8:hi8], T.t2[:, lo8:hi8], A.add)
+
+        def eighth(k, a, b):
+            tt(keys("t3") + " " + keys("t5"), keys("t6"), T.t6[:, lo8:hi8], T.t3[:, lo8:hi8], T.t5[:, lo8:hi8], A.add)
+        once = [row, col, centred, seventh, eighth]
+
+        def two(k, a, b):
+            tt("Sp%d" % k, "t0%d" % k, T.t0[:, 8 * k:8 * k + 8], T.Sp[:, a:a + 8], T.Sp[:, a + 8:a + 16], A.min)
+
+        def three(k, a, b):
+            tt("Sp%d t0%d" % (k, k), "t1%d" % k, T.t1[:, 8 * k:8 * k + 8], T.t0[:, 8 * k:8 * k + 8], T.Sp[:, a + 16:a + 24], A.min)
+
         for step in range(7):
             def src(k, step=step):
                 return (T["ps%d" % k][:, 0:64], "p%d" % k) if step == 0 else (T.Sp[:, 64 * k:64 * k + 64], "Sp%d" % k)
-            each(lambda k, a, b, src=src: red(src(k)[1], "mm%d" % k, T.mm[:, k:k + 1], src(k)[0], A.max))
-            if step == 6:
-                each(lambda k, a, b: tt("Sp%d" % k, "t0%d" % k, T.t0[:, 8 * k:8 * k + 8], T.Sp[:, a:a + 8], T.Sp[:, a + 8:a + 16], A.min))
-            each(lambda k, a, b, src=src: ts(src(k)[1] + " mm%d" % k, "ne%d" % k, T.ne[:, a:b], src(k)[0], T.mm[:, k:k + 1], A.is_lt))
-            if step == 6:
-                each(lambda k, a, b: tt("Sp%d t0%d" % (k, k), "t1%d" % k, T.t1[:, 8 * k:8 * k + 8], T.t0[:, 8 * k:8 * k + 8],
-                                        T.Sp[:, a + 16:a + 24], A.min))
-            out.append(lambda: scan(keys("ne") + " dg", keys("fg"), T.fg[:, lo:hi], T.ne[:, lo:hi], T.gd[:, 128 + lo:128 + hi], A.mult, A.add))
-            out.append(lambda: scan(keys("ne") + " dh", keys("fh"), T.fh[:, lo:hi], T.ne[:, lo:hi], T.dh[:, lo:hi], A.mult, A.add))
-            if step == 6:
+            last = 1 if step == 6 else 0
+            level(*[lambda k, a, b, src=src: red(src(k)[1], "mm%d" % k, T.mm[:, k:k + 1], src(k)[0], A.max)] + [two] * last)
+            level(*[lambda k, a, b, src=src: ts(src(k)[1] + " mm%d" % k, "ne%d" % k, T.ne[:, a:b], src(k)[0], T.mm[:, k:k + 1],
+                                                A.is_lt)] + [three] * last)
+            level(*[row, col] + [centred] * last)
+            if last:
                 break
-            each(lambda k, a, b: ts("gd fg%d" % k, "rp%d" % k, T.rp[:, a:b], T.gd[:, a:b], T.fg[:, b - 1:b], A.is_equal, -ROWPEN, A.mult))
-            each(lambda k, a, b: ts("hc fg%d fh%d" % (k, k), "cp%d" % k, T.cp[:, a:b], T.hc[:, a:b], T.fh[:, b - 1:b], A.is_equal,
-                                    T.fg[:, b - 1:b], A.mult))
-            each(lambda k, a, b: tt("rp%d cp%d" % (k, k), "rc%d" % k, T.rc[:, a:b], T.rp[:, a:b], T.cp[:, a:b], A.add))
-            each(lambda k, a, b, src=src: tt(src(k)[1] + " rc%d" % k, "Sp%d" % k, T.Sp[:, a:b], src(k)[0], T.rc[:, a:b], A.add))
+            level(lambda k, a, b: ts("gd fg%d" % k, "rp%d" % k, T.rp[:, a:b], T.gd[:, a:b], T.fg[:, b - 1:b], A.is_equal, -ROWPEN, A.mult),
+                  lambda k, a, b: ts("hc fg%d fh%d" % (k, k), "cp%d" % k, T.cp[:, a:b], T.hc[:, a:b], T.fh[:, b - 1:b], A.is_equal,
+                                     T.fg[:, b - 1:b], A.mult))
+            level(lambda k, a, b: tt("rp%d cp%d" % (k, k), "rc%d" % k, T.rc[:, a:b], T.rp[:, a:b], T.cp[:, a:b], A.add))
+            level(lambda k, a, b, src=src: tt(src(k)[1] + " rc%d" % k, "Sp%d" % k, T.Sp[:, a:b], src(k)[0], T.rc[:, a:b], A.add))
             if step in extra:
                 out.append(extra[step])
-        lo8, hi8 = lo // 8, hi // 8
-        each(lambda k, a, b: ts("hc fg%d fh%d" % (k, k), "t2%d" % k, T.t2[:, 8 * k:8 * k + 8], T.hc[:, 0:8], T.fh[:, b - 1:b], A.is_equal,
-                                T.fg[:, b - 1:b], A.mult))
-        out.append(lambda: tt(keys("t1") + " " + keys("t2"), keys("t3"), T.t3[:, lo8:hi8], T.t1[:, lo8:hi8], T.t2[:, lo8:hi8], A.add))
-        out.append(lambda: ts(keys("t3"), keys("t4"), T.t4[:, lo8:hi8], T.t3[:, lo8:hi8], -1.0 / PEN, A.mult, -27.5, A.add))
-        each(lambda k, a, b: red("t4%d" % k, "sg%d" % k, T.sg[:, k:k + 1], T.t4[:, 8 * k:8 * k + 8], A.add, True))
-        each(lambda k, a, b: ts("t4%d sg%d" % (k, k), "t5%d" % k, T.t5[:, 8 * k:8 * k + 8], T.t4[:, 8 * k:8 * k + 8], -11.5, A.is_equal,
-                                T.sg[:, k:k + 1], A.mult))
-        out.append(lambda: tt(keys("t4") + " " + keys("t5"), keys("t6"), T.t6[:, lo8:hi8], T.t4[:, lo8:hi8], T.t5[:, lo8:hi8], A.add))
-        each(lambda k, a, b: tt("t6%d offc mka" % k, "A%d" % k, T.At[:, k:512:4], T.t6[:, 8 * k:8 * k + 8].indirect(T.offc[:, 72:80]),
-                                T.mka[:], A.mult))
+        level(lambda k, a, b: ts("hc fg%d fh%d" % (k, k), "t2%d" % k, T.t2[:, 8 * k:8 * k + 8], T.hc[:, 0:8], T.fh[:, b - 1:b], A.is_equal,
+                                 T.fg[:, b - 1:b], A.mult),
+              lambda k, a, b: red("t4%d" % k, "sg%d" % k, T.sg[:, k:k + 1], T.t4[:, 8 * k:8 * k + 8], A.add, True))
+        level(seventh, lambda k, a, b: ts("sg%d fg%d" % (k, k), "sx%d" % k, T.sg[:, 2 + k:3 + k], T.sg[:, k:k + 1], T.fg[:, b - 1:b], A.subtract))
+        level(lambda k, a, b: ts("t3%d sx%d" % (k, k), "t5%d" % k, T.t5[:, 8 * k:8 * k + 8], T.t3[:, 8 * k:8 * k + 8], 11.5 * PEN, A.is_equal,
+                                 T.sg[:, 2 + k:3 + k], A.mult))
+        level(eighth)
+        level(lambda k, a, b: tt("t6%d offc mka" % k, "A%d" % k, T.At[:, k:512:4], T.t6[:, 8 * k:8 * k + 8].indirect(T.offc[:, 72:80]),
+                                 T.mka[:], A.mult))
         return out
 
     def scores(k):
@@ -319,10 +336,12 @@ def rank_program(g, core, T, topo):
         o = 8 * c * (c - 1)
         act("C%d" % c, "rs%d" % c, T.junk[:, o:o + 16 * c], slot(c), AF.Copy, accum_out=T.rs[:, c:c + 1])
 
-    def sums(i):
+    def pack(i):
         a, n_, cs = CT[i]
         quant(" ".join("C%s" % c for c in cs), "c%d" % i, "C", a, a + n_, T.Ct[:, 4 * a:4 * (a + n_)])
-        mm("K c%d" % i, "p1" if i == 0 else "", 1, n_, "K", 0, "C", a, i == 0, i == 3)
+
+    def sums(i):
+        mm("K c%d" % i, "p1" if i == 0 else "", 1, CT[i][1], "K", 0, "C", CT[i][0], i == 0, i == 3)
 
     ka, kb = rank // 4, 1 - rank // 4
     for t in range(R):
@@ -345,8 +364,6 @@ def rank_program(g, core, T, topo):
                   state(t - 1, kb) + [lambda: (scores(kb), parts(kb), likings(ka), likings(kb))] + matching([kb], {}))
         quant("A0 A1", "A", "A", 0, 128, T.At[:])
         mm("A L", "p0", 0, 128, "A", 0, "L", 0)
-        if t == 0:
-            quant("Kb", "K", "K", 0, 128, T.Kb[:])
         tt("p0 cl", "l1f", T.l1f[:], T.ps0[:, 0:16], T.cl[:], A.add)
         cp("l1f", "l1", T.l1[:], T.l1f[:])
         act(sw + " l1", "Rr", T.Rr[:], T.Sw[:].indirect(T.l1[:]), AF.Copy)
@@ -360,21 +377,21 @@ def rank_program(g, core, T, topo):
             act("sn%d" % i, "C%d rs%d" % (c, c), slot(c), T.sn[:, 256 * i:256 * i + 16 * c], AF.Relu, accum_out=T.rs[:, c:c + 1])
         for c in (12, 11, 10, 9):
             compare(c)
-            rowsum(c)
         tt("Rr Lt", "Cd", slot("d"), T.Lt[:], T.Rr[:], A.is_ge)
-        compare(8)
+        for c in (8, 7, 6, 5):
+            compare(c)
+        pack(1)
         scan("keep Cd", "ds", T.ds[:], T.keep[:], slot("d"), A.mult, A.add)
-        sums(0)
-        sums(1)
-        for c in (7, 6, 5, 4):
+        for c in (4, 3, 2, 1):
             compare(c)
-        sums(2)
-        for c in (3, 2, 1):
-            compare(c)
-        for c in range(8, 0, -1):
+        for c in range(12, 0, -1):
             rowsum(c)
+        pack(0)
+        pack(2)
+        pack(3)
+        for i in range(4):
+            sums(i)
         tt("cr ds", "u1", T.u1[:], T.cr[:], T.ds[:, 15:256:16], A.subtract)
-        sums(3)
         wr["p1"] = ("ct", cnt["ct"])
         scan("kap p1", "ex", T.ex[:], T.kap[:], T.ps1[:, 0:C], A.add, A.min)
         tt("u1 " + " ".join("rs%d" % c for c in range(16)), "u2", T.u2[:], T.u1[:], T.rs[:], A.subtract)
@@ -429,8 +446,8 @@ def rank_program(g, core, T, topo):
         dma("y", "outs", "T%d" % k, "", T.oc[:, 4 * a:4 * b], bytes_of("T", a, b))
         if k == kb:
             for i in range(4):
-                dma("s" if i % 2 else "y", "outs", "T0 T1", "", T.osc[4 * i:4 * i + 4, :], T.sT[32 * i:32 * i + 4, :])
-        cp("p%d" % k, "ys%d" % k, T.ys[:, a:b], T["ps%d" % k][:, 0:128])
+                dma("y", "outs", "T0 T1", "", T.osc[4 * i:4 * i + 4, :], T.sT[32 * i:32 * i + 4, :])
+        act("p%d" % k, "ys%d" % k, T.ys[:, a:b], T["ps%d" % k][:, 0:128], AF.Copy)
         dma("s", "outs", "ys%d" % k, "", T.y[:, a:b], T.ys[:, a:b])
     for sem in cnt:
         if seen.get(("g", sem), 0) < cnt[sem]:

@@ -5,10 +5,11 @@ N, C, L, R = 8, 256, 32, 3
 F32, BF, I32, U16, Q8, U8 = "float32", "bfloat16", "int32", "uint16", "float8_e4m3fn_x4", "uint8"
 PEN = 2.0 ** 94
 ROWPEN = 16 * PEN
+LOW = -9e29
 BIG = 2.0 ** 90
 KL = 8192.0
 EW = 144
-LEAD = 15
+LEAD = 9
 CT = [(0, 256, ["d", 15, 14, 13]), (256, 192, [12, 11, 10, 9]), (448, 128, [8, 7, 6, 5]), (576, 128, [4, 3, 2, 1])]
 
 SCRATCH = {}
@@ -16,14 +17,14 @@ for _n, _w, _d in [("xin", 1024, BF), ("uin", 512, BF), ("vin", 512, BF), ("X", 
                    ("Ez", 4 * EW + 4, BF), ("Kb", 512, BF), ("Kl", 512, BF), ("At", 512, BF), ("Ct", 4 * 704, BF),
                    ("Wn", 8192, BF), ("Sw", 2048, F32), ("CW", 2048, F32), ("CG", 2048, F32), ("Rb", 1024, F32),
                    ("pi", 4, I32), ("pt", 4, I32), ("pf", 4, F32), ("stg", 104, F32), ("offc", 104, U16),
-                   ("gd0", 128, BF), ("gd", 256, BF), ("hc", 128, BF), ("dh", 128, BF),
+                   ("gd0", 64, BF), ("gd", 64, BF), ("dg", 64, BF), ("hc", 64, BF), ("dh", 64, BF), ("neg", 64, F32),
                    ("di", 8, I32), ("dj", 8, I32), ("df", 8, F32), ("j16", 256, F32), ("jr", 256, F32),
                    ("ab", 256, F32), ("nq", 256, F32), ("cap", 256, F32), ("kap", 256, F32), ("rst", 256, F32),
                    ("sgj", 256, F32), ("keep", 256, BF), ("mka", 128, BF), ("cl", 16, F32), ("cr", 16, F32), ("cor", 4, F32),
-                   ("Sp", 128, F32), ("mm", 4, F32), ("ne", 128, BF), ("fg", 128, BF), ("fh", 128, BF),
+                   ("Sp", 128, F32), ("pm", 128, F32), ("ne", 128, BF), ("fg", 128, BF), ("fh", 128, BF),
                    ("rp", 128, BF), ("cp", 128, BF), ("rc", 128, BF),
                    ("t0", 16, F32), ("t1", 16, F32), ("t2", 16, F32), ("t3", 16, F32), ("t4", 16, F32), ("t5", 16, F32),
-                   ("t6", 32, F32), ("sg", 4, F32),
+                   ("sg", 4, F32),
                    ("l1f", 16, F32), ("l1", 16, U16), ("Rr", 256, F32), ("Rm", 256, F32), ("Lt", 256, F32), ("Pr", 256, F32),
                    ("sn", 256 * 3, BF), ("junk", 1280, BF), ("rs", 16, F32), ("ds", 256, BF), ("u1", 16, F32), ("u2", 16, F32),
                    ("ex", 256, F32), ("rkf", 16, F32), ("rk", 16, U16), ("Or", 256, F32), ("ex2", 256, F32), ("l2", 16, U16),
@@ -105,11 +106,8 @@ def rank_program(g, core, T, topo):
     def cp(r, w, out, in_):
         op("v", r, w, lambda: V.tensor_copy(out, in_))
 
-    def scan(r, w, out, d0, d1, o0, o1):
-        op("v", r, w, lambda: V.tensor_tensor_scan(out, d0, d1, 0.0, o0, o1))
-
-    def red(r, w, out, in_, o, neg=False):
-        op("v", r, w, lambda: V.tensor_reduce(out, in_, AX, o, negate=neg))
+    def scan(r, w, out, d0, d1, o0, o1, first=0.0):
+        op("v", r, w, lambda: V.tensor_tensor_scan(out, d0, d1, first, o0, o1))
 
     def act(r, w, out, in_, f, **kw):
         op("s", r, w, lambda: S.activation(out, in_, f, **kw))
@@ -121,9 +119,10 @@ def rank_program(g, core, T, topo):
         op("t", r, w, lambda: P.matmul_mx(T["ps%d" % bank][:, 0:n], T["q" + l][:, la:la + 128], T["s" + l][:, la:la + 128],
                                           T["q" + m][:, ma:ma + n], T["s" + m][:, ma:ma + n], start, stop))
 
-    def prod(r, l, la, m, k):
-        bk = 2 + turn[0] % 6
-        turn[0] += 1
+    def prod(r, l, la, m, k, bk=None):
+        if bk is None:
+            bk = 2 + turn[0] % 6
+            turn[0] += 1
         mm(r, "p%d" % bk, bk, 128, l, la, m, 128 * k)
         return "p%d" % bk, T["ps%d" % bk][:, 0:128]
 
@@ -144,52 +143,58 @@ def rank_program(g, core, T, topo):
 
     dma("s", "ldu", "", "uin", T.uin[:], T.u[:])
     dma("y", "ldx", "", "xin", T.xin[:], T.x[:])
-    dma("y", "ldw", "", "qW", bytes_of("W", 0, 512), T.wc[:])
+    dma("y", "ldw", "xin", "qW", bytes_of("W", 0, 512), T.wc[:])
     dma("y", "ldw", "", "sW", T.sW[:], T.ws[:])
     dma("y", "ldv", "", "vin", T.vin[:], T.v[:])
 
     icol, c8col = T.pf[:, 0:1], T.pf[:, 1:2]
-    for key, ap, val in [("Ez", T.Ez[:], 0.0), ("dg", T.gd[:, 128:256], 0.0), ("dh", T.dh[:], 1.0), ("dg", T.gd[:, 135:256:8], -PEN),
-                         ("dh", T.dh[:, 7:128:8], -7.0), ("dg", T.gd[:, 191:256:64], -8 * PEN), ("dh", T.dh[:, 63:128:64], 0.0)]:
+    for key, ap, val in [("Ez", T.Ez[:], 0.0), ("dg", T.dg[:], 0.0), ("dh", T.dh[:], -1.0), ("neg", T.neg[:], LOW)]:
         op("v", "", key, lambda: V.memset(ap, val))
     iota("pi", T.pi[:, 0:1], [[0, 1]], 0, 1, small=False)
-    iota("s64", T.stg[:, 64:72], [[0, 2], [-32, 4]], 119)
+    iota("s64", T.stg[:, 64:72], [[0, 2], [32, 4]], 0)
     iota("s88", T.stg[:, 88:104], [[16, 16]], 0)
-    iota("s72", T.stg[:, 72:88], [[0, 2], [-1, 8]], 7)
+    iota("s72", T.stg[:, 72:88], [[0, 2], [1, 8]], 0)
     iota("s0", T.stg[:, 0:64], [[16, 8], [1, 8]], 0)
     ez = T.Ez[:, 3:4 * EW + 3:4]
     sel("Ez", ez, [[1, EW]], A.not_equal, 1.0, 0, -1)
+    iota("hc", T.hc[:], [[0, 8], [1, 8]], 0)
     sel("Ez", ez, [[1, EW]], A.not_equal, 1.0, -128, -1)
+    iota("gd0", T.gd0[:], [[1, 8], [0, 8]], 8)
     ts("pi", "pt0", T.pt[:, 0:1], T.pi[:, 0:1], 15, A.bitwise_and)
     ts("pi", "pt1", T.pt[:, 1:2], T.pi[:, 0:1], 8, A.bitwise_and)
+    op("v", "", "dg", lambda: V.memset(T.dg[:, 6:62:8], PEN))
+    op("v", "", "dh", lambda: V.memset(T.dh[:, 6:64:8], 7.0))
     cp("pt0 pt1", "pf", T.pf[:, 0:2], T.pt[:, 0:2])
-    ts("pf s64", "s64", T.stg[:, 64:72], T.stg[:, 64:72], icol, A.subtract, c8col, A.subtract)
+    op("v", "", "dg", lambda: V.memset(T.dg[:, 62:63], -15 * PEN))
+    op("v", "", "dh", lambda: V.memset(T.dh[:, 63:64], 0.0))
+    ts("pf s64", "s64", T.stg[:, 64:72], T.stg[:, 64:72], icol, A.add, c8col, A.add)
     ts("pf s88", "s88", T.stg[:, 88:104], T.stg[:, 88:104], icol, A.add)
     cp("s0 s64 s72 s88", "offc", T.offc[:], T.stg[:])
-    for b in range(3):
+
+    def unpacker(b):
         quant("Ez", "E%d" % b, "E", EW * b, EW * b + EW, T.Ez[:, 3 - b:3 - b + 4 * EW])
-    iota("gd0", T.gd0[:], [[0, 2], [-1, 8], [0, 8]], 15)
-    iota("hc", T.hc[:], [[0, 16], [-1, 8]], 7)
     quant("uin", "u", "u", 0, 128, T.uin[:])
+    unpacker(0)
     cp("u offc", "qu1c", words("u1c", 0, 128), words("u", 0, 128).indirect(T.offc[:, 64:72]))
     act("u offc", "su1c", T.su1c[:], T.su[:].indirect(T.offc[:, 64:72]), AF.Copy)
-    act("u offc", "suR", T.suR[:], T.su[:].indirect(T.offc[:, 0:64]), AF.Copy)
-    cp("u offc", "quR", words("uR", 0, 1024), words("u", 0, 128).indirect(T.offc[:, 0:64]))
+
+    def spread(i):
+        cp("u offc", "quR%d" % i, words("uR", 128 * i, 128 * i + 128), words("u", 0, 128).indirect(T.offc[:, 8 * i:8 * i + 8]))
+        act("u offc", "suR%d" % i, T.suR[:, 128 * i:128 * i + 128], T.su[:].indirect(T.offc[:, 8 * i:8 * i + 8]), AF.Copy)
 
     def late_constants_g():
         iota("j16", T.j16[:], [[0, 16], [1, 16]], 0)
         iota("di", T.di[:], [[16, 8]], 143, -1, small=False)
         iota("jr", T.jr[:], [[4096, 2], [1, 128]], 0)
-        iota("Kl", T.Kl[:, 64:512], [[0, 448]], 0)
+        iota("Kl2", T.Kl[:, 64:512], [[0, 448]], 0)
         kl = T.Kl[:, 0:64]
         iota("Kl", kl, [[0, 64]], 256)
-        sel("Kl", kl, [[-1, 2], [0, 8], [1, 4]], A.is_equal, 0.0, 0, 0)
-        sel("Kl", kl, [[0, 2], [-16, 8], [0, 4]], A.is_ge, 0.0, 0, 1)
-        sel("Kl", kl, [[0, 2], [16, 8], [0, 4]], A.is_ge, 0.0, 15, -1)
-        iota("A0 A1", T.At[:], [[0, 512]], 0)
         iota("Kb", T.Kb[:], [[0, 512]], 1)
+        sel("Kl", kl, [[-1, 2], [0, 16], [1, 2]], A.is_equal, 0.0, 0, 0)
         sel("Kb", T.Kb[:], [[-16, 8], [0, 64]], A.is_ge, 0.0, 0, 1)
+        sel("Kl", kl, [[0, 2], [-16, 8], [0, 4]], A.is_ge, 0.0, 0, 1)
         sel("Kb", T.Kb[:], [[16, 8], [0, 64]], A.is_ge, 0.0, 15, -1)
+        sel("Kl", kl, [[0, 2], [16, 8], [0, 4]], A.is_ge, 0.0, 15, -1)
         for a, n, cs in CT:
             lo = 4 * (a + 16 * cs[3])
             iota(" ".join("C%s" % c for c in cs), T.Ct[:, lo:4 * (a + n)], [[0, 4 * (a + n) - lo]], 0)
@@ -207,13 +212,10 @@ def rank_program(g, core, T, topo):
         act("nq", "mka", T.mka[:], T.nq[:, 0:128], AF.Identity, bias=-1.0 / PEN, scale=1.0 / PEN)
         act("nq", "cap", T.cap[:], T.nq[:], AF.Identity, bias=-BIG, scale=2 * BIG)
         act("nq", "kap", T.kap[:], T.nq[:], AF.Identity, bias=16 * KL, scale=-17 * KL)
-        act("s88", "cl", T.cl[:], T.stg[:, 88:104], AF.Identity, bias=896.0)
+        act("s88", "cl", T.cl[:], T.stg[:, 88:104], AF.Identity, bias=1024.0)
         act("s88 cor", "cr", T.cr[:], T.stg[:, 88:104], AF.Identity, bias=T.cor[:, 0:1])
 
     def offsets_window():
-        ts("di", "dj", T.dj[:], T.di[:], 4, A.arith_shift_right, 7, A.bitwise_and)
-        quant("Kl", "L", "L", 0, 128, T.Kl[:])
-        quant("Kb", "K", "K", 0, 128, T.Kb[:])
         ts("dj", "df", T.df[:], T.dj[:], 512.0, A.mult)
         for k in range(8):
             act("jr df", "CW%d" % k, T.CW[:, 256 * k:256 * k + 256], T.jr[:], AF.Identity, bias=T.df[:, k:k + 1])
@@ -234,95 +236,71 @@ def rank_program(g, core, T, topo):
 
     def likings(k):
         for i in range(8):
-            key, ps = prod("T%d quR suR" % k, "uR", 128 * i, "T", k)
+            key, ps = prod("T%d suR%d quR%d" % (k, i, i), "uR", 128 * i, "T", k)
             o = 256 * i + 128 * k
             act(key, "Sw%d%d" % (i, k), T.Sw[:, o:o + 128], ps, AF.Copy)
 
     def state(t, k):
-        Mn = "M%d" % t
+        Mn, got = "M%d" % t, {}
 
-        def one(b):
-            kw, pw = prod("M%d mq ms qW sW" % k, "W", 128 * b, Mn, k)
-            kd, pd = prod("M%d mq ms E%d" % (k, b), "E", EW * b, Mn, k)
-            rb = T.Rb[:, 256 * b + 128 * k:256 * b + 128 * k + 128]
-            act(kw, "R%d%d" % (b, k), rb, pw, AF.Relu, scale=0.03125)
-            tt(kd + " R%d%d" % (b, k), "X%d%d" % (b, k), T.X[:, 512 * k + b:512 * k + 512:4], pd, rb, A.add)
-        return [lambda b=b: one(b) for b in range(4)] + [lambda: quant(
+        def products():
+            for n, b in [("W", 0), ("W", 1), ("E", 0), ("W", 2), ("E", 1), ("W", 3), ("E", 2), ("E", 3)]:
+                if n == "W":
+                    kw, pw = prod("M%d mq ms qW sW" % k, "W", 128 * b, Mn, k, (k + b) % 2 if b < 2 else b + 4)
+                    act(kw, "R%d%d" % (b, k), T.Rb[:, 256 * b + 128 * k:256 * b + 128 * k + 128], pw, AF.Relu, scale=0.03125)
+                else:
+                    got[b] = prod("M%d mq ms E%d" % (k, b), "E", EW * b, Mn, k, 2 + b)
+            for b in range(4):
+                tt(got[b][0] + " R%d%d" % (b, k), "X%d%d" % (b, k), T.X[:, 512 * k + b:512 * k + 512:4], got[b][1],
+                   T.Rb[:, 256 * b + 128 * k:256 * b + 128 * k + 128], A.add)
+        return [products, lambda: quant(
             " ".join("X%d%d" % (b, k) for b in range(4)), "T%d" % k, "T", 128 * k, 128 * k + 128, T.X[:, 512 * k:512 * k + 512])]
 
-    def matching(ks, extra):
+    def matching(k):
+        a, b, e = 64 * k, 64 * k + 64, slice(8 * k, 8 * k + 8)
+        n = str(k)
+        top, fg, fh, run = T.pm[:, b - 1:b], T.fg[:, b - 1:b], T.fh[:, b - 1:b], T.pm[:, a:b]
         out = []
-        lo, hi = 64 * ks[0], 64 * ks[-1] + 64
-        lo8, hi8 = lo // 8, hi // 8
-
-        def level(*fns):
-            out.append(lambda: [fn(k, 64 * k, 64 * k + 64) for fn in fns for k in (ks if fn not in once else ks[:1])])
-
-        def keys(n):
-            return " ".join(n + str(k) for k in ks)
-
-        def row(k, a, b):
-            scan(keys("ne") + " dg", keys("fg"), T.fg[:, lo:hi], T.ne[:, lo:hi], T.gd[:, 128 + lo:128 + hi], A.mult, A.add)
-
-        def col(k, a, b):
-            scan(keys("ne") + " dh", keys("fh"), T.fh[:, lo:hi], T.ne[:, lo:hi], T.dh[:, lo:hi], A.mult, A.add)
-
-        def centred(k, a, b):
-            ts(keys("t1"), keys("t4"), T.t4[:, lo8:hi8], T.t1[:, lo8:hi8], 27.5 * PEN, A.add)
-
-        def seventh(k, a, b):
-            tt(keys("t4") + " " + keys("t2"), keys("t3"), T.t3[:, lo8:hi8], T.t4[:, lo8:hi8], T.t2[:, lo8:hi8], A.add)
-
-        def eighth(k, a, b):
-            tt(keys("t3") + " " + keys("t5"), keys("t6"), T.t6[:, lo8:hi8], T.t3[:, lo8:hi8], T.t5[:, lo8:hi8], A.add)
-        once = [row, col, centred, seventh, eighth]
-
-        def two(k, a, b):
-            tt("Sp%d" % k, "t0%d" % k, T.t0[:, 8 * k:8 * k + 8], T.Sp[:, a:a + 8], T.Sp[:, a + 8:a + 16], A.min)
-
-        def three(k, a, b):
-            tt("Sp%d t0%d" % (k, k), "t1%d" % k, T.t1[:, 8 * k:8 * k + 8], T.t0[:, 8 * k:8 * k + 8], T.Sp[:, a + 16:a + 24], A.min)
-
         for step in range(7):
-            def src(k, step=step):
-                return (T["ps%d" % k][:, 0:64], "p%d" % k) if step == 0 else (T.Sp[:, 64 * k:64 * k + 64], "Sp%d" % k)
-            last = 1 if step == 6 else 0
-            level(*[lambda k, a, b, src=src: red(src(k)[1], "mm%d" % k, T.mm[:, k:k + 1], src(k)[0], A.max)] + [two] * last)
-            level(*[lambda k, a, b, src=src: ts(src(k)[1] + " mm%d" % k, "ne%d" % k, T.ne[:, a:b], src(k)[0], T.mm[:, k:k + 1],
-                                                A.is_lt)] + [three] * last)
-            level(*[row, col] + [centred] * last)
-            if last:
+            src, sk = (T["ps" + n][:, 0:64], "p" + n) if step == 0 else (T.Sp[:, a:b], "Sp" + n)
+            one = [lambda src=src, sk=sk: scan(sk + " neg", "pm" + n, run, src, T.neg[:], A.max, A.max, LOW)]
+            two = [lambda: ts("pm" + n, "ne" + n, T.ne[:, a:b], run, top, A.is_ge)]
+            three = [lambda: scan("dg ne" + n, "fg" + n, T.fg[:, a:b], T.ne[:, a:b], T.dg[:], A.mult, A.add),
+                     lambda: scan("dh ne" + n, "fh" + n, T.fh[:, a:b], T.ne[:, a:b], T.dh[:], A.mult, A.add, -1.0)]
+            if step == 6:
+                one.append(lambda: tt("Sp" + n, "t0" + n, T.t0[:, e], T.Sp[:, a:a + 8], T.Sp[:, a + 8:a + 16], A.min))
+                two.append(lambda: tt("Sp%d t0%d" % (k, k), "t1" + n, T.t1[:, e], T.t0[:, e], T.Sp[:, a + 16:a + 24], A.min))
+                three.append(lambda: ts("t1" + n, "t4" + n, T.t4[:, e], T.t1[:, e], 28 * PEN, A.add))
+                out += [one, two, three]
                 break
-            level(lambda k, a, b: ts("gd fg%d" % k, "rp%d" % k, T.rp[:, a:b], T.gd[:, a:b], T.fg[:, b - 1:b], A.is_equal, -ROWPEN, A.mult),
-                  lambda k, a, b: ts("hc fg%d fh%d" % (k, k), "cp%d" % k, T.cp[:, a:b], T.hc[:, a:b], T.fh[:, b - 1:b], A.is_equal,
-                                     T.fg[:, b - 1:b], A.mult))
-            level(lambda k, a, b: tt("rp%d cp%d" % (k, k), "rc%d" % k, T.rc[:, a:b], T.rp[:, a:b], T.cp[:, a:b], A.add))
-            level(lambda k, a, b, src=src: tt(src(k)[1] + " rc%d" % k, "Sp%d" % k, T.Sp[:, a:b], src(k)[0], T.rc[:, a:b], A.add))
-            if step in extra:
-                out.append(extra[step])
-        level(lambda k, a, b: ts("hc fg%d fh%d" % (k, k), "t2%d" % k, T.t2[:, 8 * k:8 * k + 8], T.hc[:, 0:8], T.fh[:, b - 1:b], A.is_equal,
-                                 T.fg[:, b - 1:b], A.mult),
-              lambda k, a, b: red("t4%d" % k, "sg%d" % k, T.sg[:, k:k + 1], T.t4[:, 8 * k:8 * k + 8], A.add, True))
-        level(seventh, lambda k, a, b: ts("sg%d fg%d" % (k, k), "sx%d" % k, T.sg[:, 2 + k:3 + k], T.sg[:, k:k + 1], T.fg[:, b - 1:b], A.subtract))
-        level(lambda k, a, b: ts("t3%d sx%d" % (k, k), "t5%d" % k, T.t5[:, 8 * k:8 * k + 8], T.t3[:, 8 * k:8 * k + 8], 11.5 * PEN, A.is_equal,
-                                 T.sg[:, 2 + k:3 + k], A.mult))
-        level(eighth)
-        level(lambda k, a, b: tt("t6%d offc mka" % k, "A%d" % k, T.At[:, k:512:4], T.t6[:, 8 * k:8 * k + 8].indirect(T.offc[:, 72:80]),
-                                 T.mka[:], A.mult))
-        return out
+            out += [one, two, three,
+                    [lambda: ts("gd fg" + n, "rp" + n, T.rp[:, a:b], T.gd[:], fg, A.is_equal, -ROWPEN, A.mult),
+                     lambda: ts("hc fg%d fh%d" % (k, k), "cp" + n, T.cp[:, a:b], T.hc[:], fh, A.is_equal, fg, A.mult)],
+                    [lambda: tt("rp%d cp%d" % (k, k), "rc" + n, T.rc[:, a:b], T.rp[:, a:b], T.cp[:, a:b], A.add)],
+                    [lambda src=src, sk=sk: tt(sk + " rc" + n, "Sp" + n, T.Sp[:, a:b], src, T.rc[:, a:b], A.add)]]
+        out += [[lambda: ts("hc fg%d fh%d" % (k, k), "t2" + n, T.t2[:, e], T.hc[:, 0:8], fh, A.is_equal, fg, A.mult),
+                 lambda: op("v", "t4" + n, "sg" + n, lambda: V.tensor_reduce(T.sg[:, k:k + 1], T.t4[:, e], AX, A.add, negate=True))],
+                [lambda: tt("t4%d t2%d" % (k, k), "t3" + n, T.t3[:, e], T.t4[:, e], T.t2[:, e], A.add),
+                 lambda: ts("sg%d fg%d" % (k, k), "sx" + n, T.sg[:, 2 + k:3 + k], T.sg[:, k:k + 1], fg, A.subtract, 4 * PEN, A.add)],
+                [lambda: ts("t3%d sx%d" % (k, k), "t5" + n, T.t5[:, e], T.t3[:, e], 12 * PEN, A.is_equal, T.sg[:, 2 + k:3 + k], A.mult),
+                 lambda: tt("offc mka t3" + n, "A" + n, T.At[:, k:512:4], T.t3[:, e].indirect(T.offc[:, 72:80]), T.mka[:], A.mult)],
+                [lambda: tt("offc mka t5" + n, "A%d" % (2 + k), T.At[:, 2 + k:512:4], T.t5[:, e].indirect(T.offc[:, 72:80]), T.mka[:], A.mult)]]
+        return [lambda fs=fs: [f() for f in fs] for fs in out]
 
     def scores(k):
         mm("T%d qu1c su1c" % k, "p%d" % k, k, 128, "T", 128 * k, "u1c", 0)
 
-    def merge(first, second):
-        for f in first[:LEAD]:
+    def merge(first, second, lead, extra):
+        for f in first[:lead]:
             f()
-        rest = first[LEAD:]
+        rest = first[lead:]
         for i in range(max(len(rest), len(second))):
             if i < len(second):
                 second[i]()
             if i < len(rest):
                 rest[i]()
+            if i in extra:
+                extra[i]()
 
     def slot(c):
         for a, n_, cs in CT:
@@ -349,20 +327,22 @@ def rank_program(g, core, T, topo):
             quant("xin", "T0 T1", "T", 0, C, T.xin[:])
             scores(0)
             scores(1)
-            ts("gd0", "gd", T.gd[:, 0:128], T.gd0[:], -PEN, A.mult)
-            quant("Ez", "E3", "E", EW * 3, EW * 4, T.Ez[:, 0:4 * EW])
-            parts(0)
-            parts(1)
+            ts("gd0", "gd", T.gd[:], T.gd0[:], -PEN, A.mult)
+            unpacker(1)
             late_constants_g()
-            likings(0)
-            likings(1)
-            late_constants_s()
-            for f in matching([0, 1], {3: offsets_window}):
-                f()
+            extra = {i + 4: (lambda i=i: spread(i)) for i in range(8)}
+            extra[0] = lambda: unpacker(2)
+            extra[1] = lambda: (unpacker(3), parts(0), parts(1), late_constants_s())
+            extra[16] = lambda: (likings(0), likings(1))
+            extra[19] = lambda: ts("di", "dj", T.dj[:], T.di[:], 4, A.arith_shift_right, 7, A.bitwise_and)
+            extra[20] = offsets_window
+            extra[30] = lambda: quant("Kl Kl2", "L", "L", 0, 128, T.Kl[:])
+            extra[31] = lambda: quant("Kb", "K", "K", 0, 128, T.Kb[:])
+            merge(matching(0), matching(1), 0, extra)
         else:
-            merge(state(t - 1, ka) + [lambda: (scores(ka), parts(ka))] + matching([ka], {}),
-                  state(t - 1, kb) + [lambda: (scores(kb), parts(kb), likings(ka), likings(kb))] + matching([kb], {}))
-        quant("A0 A1", "A", "A", 0, 128, T.At[:])
+            merge(state(t - 1, ka) + [lambda: (scores(ka), parts(ka))] + matching(ka),
+                  state(t - 1, kb) + [lambda: (scores(kb), parts(kb), likings(ka), likings(kb))] + matching(kb), LEAD, {})
+        quant("A0 A1 A2 A3", "A", "A", 0, 128, T.At[:])
         mm("A L", "p0", 0, 128, "A", 0, "L", 0)
         tt("p0 cl", "l1f", T.l1f[:], T.ps0[:, 0:16], T.cl[:], A.add)
         cp("l1f", "l1", T.l1[:], T.l1f[:])
@@ -381,20 +361,20 @@ def rank_program(g, core, T, topo):
         for c in (8, 7, 6, 5):
             compare(c)
         pack(1)
-        scan("keep Cd", "ds", T.ds[:], T.keep[:], slot("d"), A.mult, A.add)
+        pack(0)
         for c in (4, 3, 2, 1):
             compare(c)
         for c in range(12, 0, -1):
             rowsum(c)
-        pack(0)
+        scan("keep Cd", "ds", T.ds[:], T.keep[:], slot("d"), A.mult, A.add)
         pack(2)
         pack(3)
         for i in range(4):
             sums(i)
         tt("cr ds", "u1", T.u1[:], T.cr[:], T.ds[:, 15:256:16], A.subtract)
         wr["p1"] = ("ct", cnt["ct"])
-        scan("kap p1", "ex", T.ex[:], T.kap[:], T.ps1[:, 0:C], A.add, A.min)
         tt("u1 " + " ".join("rs%d" % c for c in range(16)), "u2", T.u2[:], T.u1[:], T.rs[:], A.subtract)
+        scan("kap p1", "ex", T.ex[:], T.kap[:], T.ps1[:, 0:C], A.add, A.min)
         tt("ex u2", "rkf", T.rkf[:], T.ex[:, 15:256:16], T.u2[:], A.add)
         cp("rkf", "rk", T.rk[:], T.rkf[:])
         cp("Pr rk", "Or", T.Or[:].indirect(T.rk[:]), T.Pr[:])
@@ -442,13 +422,13 @@ def rank_program(g, core, T, topo):
         a, b = 128 * k, 128 * k + 128
         for f in state(R - 1, k):
             f()
-        mm("T%d v" % k, "p%d" % k, k, 128, "v", 0, "T", a)
-        dma("y", "outs", "T%d" % k, "", T.oc[:, 4 * a:4 * b], bytes_of("T", a, b))
         if k == kb:
-            for i in range(4):
-                dma("y", "outs", "T0 T1", "", T.osc[4 * i:4 * i + 4, :], T.sT[32 * i:32 * i + 4, :])
-        act("p%d" % k, "ys%d" % k, T.ys[:, a:b], T["ps%d" % k][:, 0:128], AF.Copy)
-        dma("s", "outs", "ys%d" % k, "", T.y[:, a:b], T.ys[:, a:b])
+            mm("T0 T1 v", "p0", 0, C, "v", 0, "T", 0)
+        dma("y", "outs", "T%d" % k, "", T.oc[:, 4 * a:4 * b], bytes_of("T", a, b))
+    for i in range(4):
+        dma("y", "outs", "T0 T1", "", T.osc[4 * i:4 * i + 4, :], T.sT[32 * i:32 * i + 4, :])
+    act("p0", "ys", T.ys[:], T.ps0[:, 0:C], AF.Copy)
+    dma("s", "outs", "ys", "", T.y[:], T.ys[:])
     for sem in cnt:
         if seen.get(("g", sem), 0) < cnt[sem]:
             g.wait_ge(T.sem[sem], cnt[sem])

@@ -1,43 +1,43 @@
 from concourse.bass import DstId, RemoteDMATransfer
-from concourse.mybir import dt, AluOpType, AxisListType, ActivationFunctionType
+from concourse.mybir import dt, AluOpType, ActivationFunctionType
 
 N, C, L, R = 8, 256, 32, 3
 F32, BF, I32, U16, Q8, U8 = "float32", "bfloat16", "int32", "uint16", "float8_e4m3fn_x4", "uint8"
-PEN = 2.0 ** 94
-ROWPEN = 16 * PEN
+PEN = 2.0 ** 92
+KC = 128.0
 LOW = -9e29
 BIG = 2.0 ** 90
 KL = 8192.0
-EW = 144
-LEAD = 9
-CT = [(0, 256, ["d", 15, 14, 13]), (256, 192, [12, 11, 10, 9]), (448, 128, [8, 7, 6, 5]), (576, 128, [4, 3, 2, 1])]
+NA = 3
+TRI = [["d", 7, 6, 5], [4, 3, 2, 1]]
+CYC, WAIT, DMA, FLY = 1.04, 120, 2500, (2600, 4200)
+SLACK = 30
+ANY, SIDE = list(range(8)), [6, 7]
 
 SCRATCH = {}
 for _n, _w, _d in [("xin", 1024, BF), ("uin", 512, BF), ("vin", 512, BF), ("X", 1024, BF), ("Bt", 1024, BF),
-                   ("Ez", 4 * EW + 4, BF), ("Kb", 512, BF), ("Kl", 512, BF), ("At", 512, BF), ("Ct", 4 * 704, BF),
-                   ("Wn", 8192, BF), ("Sw", 2048, F32), ("CW", 2048, F32), ("CG", 2048, F32), ("Rb", 1024, F32),
-                   ("pi", 4, I32), ("pt", 4, I32), ("pf", 4, F32), ("stg", 104, F32), ("offc", 104, U16),
-                   ("gd0", 64, BF), ("gd", 64, BF), ("dg", 64, BF), ("hc", 64, BF), ("dh", 64, BF), ("neg", 64, F32),
-                   ("di", 8, I32), ("dj", 8, I32), ("df", 8, F32), ("j16", 256, F32), ("jr", 256, F32),
-                   ("ab", 256, F32), ("nq", 256, F32), ("cap", 256, F32), ("kap", 256, F32), ("rst", 256, F32),
-                   ("sgj", 256, F32), ("keep", 256, BF), ("mka", 128, BF), ("cl", 16, F32), ("cr", 16, F32), ("cor", 4, F32),
-                   ("Sp", 128, F32), ("pm", 128, F32), ("ne", 128, BF), ("fg", 128, BF), ("fh", 128, BF),
-                   ("rp", 128, BF), ("cp", 128, BF), ("rc", 128, BF),
-                   ("t0", 16, F32), ("t1", 16, F32), ("t2", 16, F32), ("t3", 16, F32), ("t4", 16, F32), ("t5", 16, F32),
-                   ("sg", 4, F32),
+                   ("Ez", 516, BF), ("Kb", 512, BF), ("Kp", 512, BF), ("Kl", 512, BF), ("At", 1024, BF), ("Ct", 3072, BF),
+                   ("Wn", 8192, BF), ("Sw", 2048, F32), ("CW", 1024, F32), ("CG", 1024, F32), ("Rb", 1024, F32),
+                   ("pi", 4, I32), ("pt", 4, I32), ("pf", 8, F32), ("stg", 104, F32), ("offc", 104, U16),
+                   ("h8", 64, F32), ("g7", 64, F32), ("neg", 64, F32), ("d0", 192, F32), ("sa", 64, F32), ("zz", 16, F32),
+                   ("di", 8, I32), ("dj", 8, I32), ("df", 8, F32), ("j16", 144, F32), ("jr", 128, F32),
+                   ("ab", 144, F32), ("nq", 144, F32), ("cap", 128, F32), ("kq", 384, F32), ("rst", 128, F32),
+                   ("sgj", 128, F32), ("keep", 128, BF), ("mka", 128, BF), ("cl", 8, F32), ("cr", 16, F32), ("cor", 4, F32),
+                   ("Z0", 384, F32), ("Z1", 384, F32), ("pm", 160, F32), ("cn", 32, F32), ("jx", 128, BF), ("jh", 128, BF),
+                   ("seg", 128, F32), ("tmp", 256, BF), ("alt", 32, F32), ("sc", 8, F32),
                    ("l1f", 16, F32), ("l1", 16, U16), ("Rr", 256, F32), ("Rm", 256, F32), ("Lt", 256, F32), ("Pr", 256, F32),
-                   ("sn", 256 * 3, BF), ("junk", 1280, BF), ("rs", 16, F32), ("ds", 256, BF), ("u1", 16, F32), ("u2", 16, F32),
-                   ("ex", 256, F32), ("rkf", 16, F32), ("rk", 16, U16), ("Or", 256, F32), ("ex2", 256, F32), ("l2", 16, U16),
+                   ("sn", 1024, BF), ("junk", 2048, BF), ("rs", 24, F32), ("ds", 256, BF), ("u1", 16, F32),
+                   ("ex", 256, F32), ("rkf", 8, F32), ("rk", 16, U16), ("Or", 256, F32), ("ex2", 256, F32), ("l2", 16, U16),
                    ("oi", 256, I32), ("oj", 256, I32), ("OL", 512, F32), ("ys", 256, F32)]:
     SCRATCH[_n] = ("sbuf", [128, _w], _d)
-for _n, _w in [("u", 128), ("u1c", 128), ("uR", 1024), ("v", 128), ("W", 512), ("T", 256), ("E", 4 * EW), ("K", 128),
-               ("L", 128), ("A", 128), ("C", 704)] + [("B%d" % _t, 256) for _t in range(R)] + [("M%d" % _t, 256) for _t in range(R)]:
+for _n, _w in [("u", 128), ("u1c", 128), ("uR", 1024), ("v", 128), ("W", 512), ("T", 256), ("E", 512), ("K", 256),
+               ("L", 128), ("A", 256), ("C", 768)] + [("B%d" % _t, 256) for _t in range(R)] + [("M%d" % _t, 256) for _t in range(R)]:
     SCRATCH["q" + _n] = ("sbuf", [128, _w], Q8)
     SCRATCH["s" + _n] = ("sbuf", [128, _w], U8)
 for _b in range(8):
     SCRATCH["ps%d" % _b] = ("psum", [128, 512], F32)
 
-SEMAPHORES = (["cv", "cs", "ct", "cg", "ldx", "ldu", "ldw", "ldv", "rot0", "rot1", "outs", "sent"]
+SEMAPHORES = (["cv", "cs", "ct", "cg", "ldx0", "ldx1", "ldu", "ldw", "ldv", "rot0", "rot1", "outs", "sent"]
               + ["arr%d%d" % (_t, _k) for _t in range(R) for _k in range(2)])
 
 
@@ -51,89 +51,142 @@ def deal(T, topo, s, k):
     return out + [(d, [e for e in topo.engines(src, T.cores[d]) if e not in eng]) for d in others if d not in far]
 
 
+def issue_order(calls):
+    for c in reversed(calls):
+        c["way"] += c["cost"] + c["lat"]
+        for d in c["deps"]:
+            d["way"] = max(d["way"], c["way"] + (-d["lat"] if d is c["sums"] else WAIT))
+            d["users"].append(c)
+    ready, free, held, order = {q: [] for q in "vstgya"}, {q: 0.0 for q in "vstgya"}, [None] * 8, []
+
+    def enter(c):
+        c["at"] = max([d["end"] + (-d["lat"] if d is c["sums"] else WAIT) for d in c["deps"]] + [0.0])
+        ready[c["q"]].append(c)
+
+    def bank_time(b):
+        if held[b] is None:
+            return 0.0
+        return max(u["end"] for u in held[b]["uses"]) + WAIT if all("end" in u for u in held[b]["uses"]) else None
+
+    for c in calls:
+        c["left"] = len(c["deps"])
+        if not c["deps"]:
+            enter(c)
+    while len(order) < len(calls):
+        best, times = None, [bank_time(b) for b in range(8)]
+        for q, cs in ready.items():
+            can = []
+            for c in cs:
+                open_ = [(times[b], b) for b in c["banks"] if times[b] is not None]
+                if open_ or not c["banks"]:
+                    can.append((max(c["at"], free[q], min(open_)[0] if open_ else 0.0), c, min(open_)[1] if open_ else None))
+            if can:
+                now = min(x[0] for x in can)
+                pick = max((x for x in can if x[0] == now), key=lambda x: x[1]["way"])
+                soon = [x for x in can if x[0] < now + pick[1]["cost"] - SLACK and x[1]["way"] > pick[1]["way"]]
+                if soon:
+                    pick = max(soon, key=lambda x: x[1]["way"])
+                if best is None or pick[0] < best[0]:
+                    best = pick
+        at, c, b = best
+        if b is not None:
+            c["deps"] += held[b]["uses"] if held[b] else []
+            held[b], c["bank"] = c, b
+        ready[c["q"]].remove(c)
+        free[c["q"]], c["end"] = at + c["cost"], at + c["cost"] + c["lat"]
+        order.append(c)
+        for u in c["users"]:
+            u["left"] -= 1
+            if not u["left"]:
+                enter(u)
+    return order
+
+
 def rank_program(g, core, T, topo):
     rank = T.rank_of(core)
     if rank is None:
         return
-    A, AF, AX = AluOpType, ActivationFunctionType, AxisListType.X
+    A, AF = AluOpType, ActivationFunctionType
     Q = {"v": g.vector, "s": g.scalar, "t": g.tensor, "g": g, "y": g.sync}
     V, S, P = g.vector, g.scalar, g.tensor
-    cnt, seen, wr, rd, turn = {}, {}, {}, {}, [0]
+    calls, wr, rd = [], {}, {}
+    line, tail = {}, {}
+    ka, kb = rank // 4, 1 - rank // 4
 
-    def need(q, reads, writes, skip=None):
-        want = {}
-        toks = [wr[k] for k in reads + writes if k in wr]
-        for k in writes:
-            toks += rd.get(k, [])
-        for sem, val in toks:
-            want[sem] = max(want.get(sem, 0), cnt[sem] if val is None else val)
-        for sem, val in want.items():
-            if sem != skip and seen.get((q, sem), 0) < val:
-                Q[q].wait_ge(T.sem[sem], val)
-                seen[(q, sem)] = val
-
-    def note(tok, reads, writes):
+    def op(q, reads, writes, fn, cost, lat=0.0, sem=None, inc=1, banks=(), sums=None):
+        reads, writes = reads.split(), writes.split()
+        deps = [wr[k] for k in reads + writes if k in wr] + [d for k in writes for d in rd.get(k, [])]
+        if line.get(q) in tail and tail[line[q]] not in deps:
+            sums = tail[line[q]]
+            deps.append(sums)
+        c = {"q": q, "fn": fn, "cost": cost, "lat": lat, "sem": sem or "c" + q, "inc": inc, "banks": banks, "sums": sums,
+             "deps": list({d["n"]: d for d in deps}.values()), "n": len(calls), "way": 0.0, "users": [], "uses": []}
         for k in reads:
-            rd.setdefault(k, []).append(tok)
+            rd.setdefault(k, []).append(c)
+            if k in wr and "start" in wr[k]:
+                wr[k]["start"]["uses"].append(c)
         for k in writes:
-            wr[k] = tok
-            rd[k] = []
+            wr[k], rd[k] = c, []
+        calls.append(c)
+        if q in line:
+            tail[line[q]] = c
+        return c
 
-    def op(q, reads, writes, fn):
-        reads, writes = reads.split(), writes.split()
-        need(q, reads, writes)
-        sem = "c" + q
-        fn().then_inc(T.sem[sem], 1)
-        cnt[sem] = cnt.get(sem, 0) + 1
-        note((sem, cnt[sem]), reads, writes)
+    def ap(x):
+        return T["ps%d" % x[0]["bank"]][:, 0:x[1]] if isinstance(x, tuple) else x
 
-    def dma(q, sem, reads, writes, out, in_):
-        reads, writes = reads.split(), writes.split()
-        need(q, reads, writes, sem)
-        Q[q].dma_start(out, in_).then_inc(T.sem[sem], 16)
-        cnt[sem] = cnt.get(sem, 0) + 16
-        note((sem, None), reads, writes)
+    def cycles(n):
+        return max(64, n) * CYC
 
-    def ts(r, w, out, in0, s1, o0, s2=None, o1=None):
-        if o1 is None:
-            op("v", r, w, lambda: V.tensor_scalar(out, in0, s1, None, o0))
-        else:
-            op("v", r, w, lambda: V.tensor_scalar(out, in0, s1, s2, o0, o1))
+    def picks(n, per=1.6):
+        return 55 + n * per * CYC
 
-    def tt(r, w, out, in0, in1, o):
-        op("v", r, w, lambda: V.tensor_tensor(out, in0, in1, o))
+    def dma(q, sem, reads, writes, out, in_, lat=DMA):
+        op(q, reads, writes, lambda: Q[q].dma_start(out, in_), 50, lat, sem, 16)
 
-    def cp(r, w, out, in_):
-        op("v", r, w, lambda: V.tensor_copy(out, in_))
+    def ts(r, w, out, in0, s1, o0, s2=None, o1=None, n=64):
+        more = () if o1 is None else (o1,)
+        op("v", r, w, lambda: V.tensor_scalar(out, ap(in0), s1, s2, o0, *more), cycles(n))
 
-    def scan(r, w, out, d0, d1, o0, o1, first=0.0):
-        op("v", r, w, lambda: V.tensor_tensor_scan(out, d0, d1, first, o0, o1))
+    def tt(r, w, out, in0, in1, o, cost=cycles(64)):
+        op("v", r, w, lambda: V.tensor_tensor(out, ap(in0), in1, o), cost)
 
-    def act(r, w, out, in_, f, **kw):
-        op("s", r, w, lambda: S.activation(out, in_, f, **kw))
+    def cp(r, w, out, in_, cost=cycles(64)):
+        op("v", r, w, lambda: V.tensor_copy(out, in_), cost)
 
-    def quant(r, w, n, a, b, in_):
-        op("v", r, w, lambda: V.quantize_mx(T["q" + n][:, a:b], T["s" + n][:, a:b], in_))
+    def scan(r, w, out, d0, d1, o0, o1, first=0.0, n=64):
+        op("v", r, w, lambda: V.tensor_tensor_scan(out, ap(d0), d1, first, o0, o1), cycles(n))
 
-    def mm(r, w, bank, n, l, la, m, ma, start=True, stop=True):
-        op("t", r, w, lambda: P.matmul_mx(T["ps%d" % bank][:, 0:n], T["q" + l][:, la:la + 128], T["s" + l][:, la:la + 128],
-                                          T["q" + m][:, ma:ma + n], T["s" + m][:, ma:ma + n], start, stop))
+    def act(r, w, out, in_, f, cost=cycles(128), **kw):
+        op("s", r, w, lambda: S.activation(out, ap(in_), f, **kw), cost + (20 if "accum_out" in kw else 0))
 
-    def prod(r, l, la, m, k, bk=None):
-        if bk is None:
-            bk = 2 + turn[0] % 6
-            turn[0] += 1
-        mm(r, "p%d" % bk, bk, 128, l, la, m, 128 * k)
-        return "p%d" % bk, T["ps%d" % bk][:, 0:128]
+    def fix(w, out, val, n=64):
+        op("v", "", w, lambda: V.memset(out, val), cycles(n))
+
+    def quant(r, w, n, a, in_, cols=128):
+        op("v", r, w, lambda: V.quantize_mx(T["q" + n][:, a:a + cols], T["s" + n][:, a:a + cols], in_), 15 + 1.1 * cols)
+
+    def prod(r, terms, banks=ANY):
+        key, first, last = "p%d" % len(calls), None, None
+        for i, (l, la, m, ma) in enumerate(terms):
+            def fn(i=i, l=l, la=la, m=m, ma=ma):
+                return P.matmul_mx(ap((wr0[0], 128)), T["q" + l][:, la:la + 128], T["s" + l][:, la:la + 128],
+                                   T["q" + m][:, ma:ma + 128], T["s" + m][:, ma:ma + 128], i == 0, i == len(terms) - 1)
+            last = op("t", r[i], key, fn, 90, 50, banks=() if i else banks, sums=last)
+            first = first or last
+            last["start"] = first
+        wr0 = [first]
+        return key, first
 
     def iota(w, out, pat, base, cm=0, small=True):
-        if small:
-            op("g", "", w, lambda: g.iota(out, pat, base, cm, allow_small_or_imprecise_dtypes=True))
-        else:
-            op("g", "", w, lambda: g.iota(out, pat, base, cm))
+        n = 1
+        for step, count in pat:
+            n *= count
+        kw = {"allow_small_or_imprecise_dtypes": True} if small else {}
+        op("g", "", w, lambda: g.iota(out, pat, base, cm, **kw), 160 + 2 * CYC * n)
 
-    def sel(k, ap, pat, cmp, fill, base, cm):
-        op("g", k, k, lambda: g.affine_select(ap, ap, pat, cmp, fill, base, cm))
+    def sel(k, out, pat, cmp, fill, base, cm, n):
+        op("g", k, k, lambda: g.affine_select(out, out, pat, cmp, fill, base, cm), 210 + 2 * CYC * n)
 
     def words(n, a, b):
         return T["q" + n][:, a:b].bitcast(dt.uint32)
@@ -141,294 +194,311 @@ def rank_program(g, core, T, topo):
     def bytes_of(n, a, b):
         return T["q" + n][:, a:b].bitcast(dt.uint8)
 
-    dma("s", "ldu", "", "uin", T.uin[:], T.u[:])
-    dma("y", "ldx", "", "xin", T.xin[:], T.x[:])
-    dma("y", "ldw", "xin", "qW", bytes_of("W", 0, 512), T.wc[:])
-    dma("y", "ldw", "", "sW", T.sW[:], T.ws[:])
-    dma("y", "ldv", "", "vin", T.vin[:], T.v[:])
+    def keys(pre, items, post=""):
+        return " ".join("%s%s%s" % (pre, i, post) for i in items)
 
-    icol, c8col = T.pf[:, 0:1], T.pf[:, 1:2]
-    for key, ap, val in [("Ez", T.Ez[:], 0.0), ("dg", T.dg[:], 0.0), ("dh", T.dh[:], -1.0), ("neg", T.neg[:], LOW)]:
-        op("v", "", key, lambda: V.memset(ap, val))
+    def half(x, k, w=128):
+        return x[:, w * k:w * k + w]
+
+    def ends(x, k):
+        return x[:, 128 * k + 15:128 * k + 128:16]
+
+    dma("s", "ldu", "", "uin", T.uin[:], T.u[:], 2000)
+    for k in (ka, kb):
+        dma("y", "ldx%d" % k, "", "xin%d" % k, half(T.xin, k, 512), half(T.x, k, 512), 2200 + 400 * (k == kb))
+    dma("y", "ldw", "xin0 xin1", "qW", bytes_of("W", 0, 512), T.wc[:])
+    dma("y", "ldw", "xin0 xin1", "sW", T.sW[:], T.ws[:])
+    dma("y", "ldv", "xin0 xin1", "vin", T.vin[:], T.v[:])
+
+    icol, i8col, ucol = T.pf[:, 0:1], T.pf[:, 1:2], T.pf[:, 4:5]
+    small = cycles(64)
+    line.update(g="g")
     iota("pi", T.pi[:, 0:1], [[0, 1]], 0, 1, small=False)
-    iota("s64", T.stg[:, 64:72], [[0, 2], [32, 4]], 0)
-    iota("s88", T.stg[:, 88:104], [[16, 16]], 0)
-    iota("s72", T.stg[:, 72:88], [[0, 2], [1, 8]], 0)
+    iota("s64", T.stg[:, 64:72], [[0, 2], [2, 4]], 0)
     iota("s0", T.stg[:, 0:64], [[16, 8], [1, 8]], 0)
-    ez = T.Ez[:, 3:4 * EW + 3:4]
-    sel("Ez", ez, [[1, EW]], A.not_equal, 1.0, 0, -1)
-    iota("hc", T.hc[:], [[0, 8], [1, 8]], 0)
-    sel("Ez", ez, [[1, EW]], A.not_equal, 1.0, -128, -1)
-    iota("gd0", T.gd0[:], [[1, 8], [0, 8]], 8)
-    ts("pi", "pt0", T.pt[:, 0:1], T.pi[:, 0:1], 15, A.bitwise_and)
-    ts("pi", "pt1", T.pt[:, 1:2], T.pi[:, 0:1], 8, A.bitwise_and)
-    op("v", "", "dg", lambda: V.memset(T.dg[:, 6:62:8], PEN))
-    op("v", "", "dh", lambda: V.memset(T.dh[:, 6:64:8], 7.0))
-    cp("pt0 pt1", "pf", T.pf[:, 0:2], T.pt[:, 0:2])
-    op("v", "", "dg", lambda: V.memset(T.dg[:, 62:63], -15 * PEN))
-    op("v", "", "dh", lambda: V.memset(T.dh[:, 63:64], 0.0))
-    ts("pf s64", "s64", T.stg[:, 64:72], T.stg[:, 64:72], icol, A.add, c8col, A.add)
+    iota("j16", T.j16[:], [[0, 9], [1, 16]], 0)
+    iota("s80", T.stg[:, 80:88], [[16, 8]], 7)
+    iota("di", T.di[:], [[16, 8]], 143, -1, small=False)
+    iota("jr", T.jr[:], [[1, 128]], 0)
+    fix("Ez", T.Ez[:], 0.0, 258)
+    sel("Ez", T.Ez[:, 3:515:4], [[1, 128]], A.not_equal, 1.0, 0, -1, 128)
+    iota("h8", T.h8[:], [[8, 8], [0, 8]], 8)
+    iota("g7", T.g7[:], [[0, 8], [1, 8]], -7)
+    iota("s88", T.stg[:, 88:104], [[16, 16]], 0)
+    iota("s72", T.stg[:, 72:80], [[8, 8]], 7)
+    fix("neg", T.neg[:], LOW)
+    fix("pm0 pm1", T.pm[:], LOW, 160)
+    fix("sa", T.sa[:], 0.0)
+    fix("zz", T.zz[:], 0.0)
+    fix("A0 A1", T.At[:, 0:1024:4], 0.0, 128)
+    for j, m in enumerate((15, 8, 7)):
+        ts("pi", "pt%d" % j, T.pt[:, j:j + 1], T.pi[:, 0:1], m, A.bitwise_and)
+    for j, val in enumerate((0.0, KC, -PEN)):
+        fix("d0%d" % j, T.d0[:, j:192:3], val)
+    cp("pt0 pt1 pt2", "pf", T.pf[:, 0:3], T.pt[:, 0:3])
+    ts("pf", "p3", T.pf[:, 3:4], T.pf[:, 2:3], 16.0, A.mult)
+    ts("pf p3", "p4", ucol, i8col, 0.125, A.mult, T.pf[:, 3:4], A.add)
+    ts("p4 s64", "o64", T.offc[:, 64:72], T.stg[:, 64:72], ucol, A.add)
+    ts("pf s80", "o80", T.offc[:, 80:88], T.stg[:, 80:88], i8col, A.add)
     ts("pf s88", "s88", T.stg[:, 88:104], T.stg[:, 88:104], icol, A.add)
-    cp("s0 s64 s72 s88", "offc", T.offc[:], T.stg[:])
+    cp("s0", "o0", T.offc[:, 0:64], T.stg[:, 0:64])
+    cp("s72", "o72", T.offc[:, 72:80], T.stg[:, 72:80])
+    cp("s88", "o88", T.offc[:, 88:104], T.stg[:, 88:104])
+    for b in range(4):
+        quant("Ez", "E%d" % b, "E", 128 * b, T.Ez[:, 3 - b:515 - b])
+    quant("uin", "u", "u", 0, T.uin[:])
+    quant("vin", "v", "v", 0, T.vin[:])
+    line.update(v="spread", s="side")
+    for n, a, o, key in [("u1c", 0, 64, "o64")] + [("uR", 128 * i, 8 * i, "o0") for i in range(8)]:
+        cp("u " + key, "q%s%d" % (n, a), words(n, a, a + 128), words("u", 0, 128).indirect(T.offc[:, o:o + 8]), picks(128))
+        act("u " + key, "s%s%d" % (n, a), T["s" + n][:, a:a + 128], T.su[:].indirect(T.offc[:, o:o + 8]), AF.Copy, picks(128))
+    del line["v"], line["s"]
+    iota("Kl2", T.Kl[:, 32:512], [[0, 480]], 0)
+    kl = T.Kl[:, 0:32]
+    iota("Kl", kl, [[0, 8], [-128, 2], [-128, 2]], 0)
+    sel("Kl", kl, [[-16, 8], [0, 4]], A.is_ge, 0.0, 0, 1, 32)
+    sel("Kl", kl, [[16, 8], [0, 4]], A.is_ge, 0.0, 15, -1, 32)
+    quant("Kl Kl2", "L", "L", 0, T.Kl[:])
+    iota("rs0", T.rs[:, 0:9:8], [[0, 2]], 0)
+    for j, (key, x, val) in enumerate([("Kb", T.Kb[:], 1), ("Kp", T.Kp[:], 2 * ka - 1)]):
+        k = (ka, kb)[j]
+        iota(keys("C", TRI[0] + TRI[1], k), half(T.Ct, k, 1024), [[0, 1024]], 0)
+        iota(key, x, [[0, 512]], val)
+        sel(key, x, [[-16, 8], [0, 64]], A.is_ge, 0.0, 0, 1, 512)
+        sel(key, x, [[16, 8], [0, 64]], A.is_ge, 0.0, 15, -1, 512)
+        quant(key, "K%d" % j, "K", 128 * j, x)
+    iota("Or", T.Or[:], [[0, 256]], 0)
+    iota("CG", T.CG[:], [[1, 8], [0, 128]], 0)
+    line.clear()
+    s8, last = T.stg[:, 88:96], T.kq[:, 271:272]
+    act("h8 sa", "sa", T.sa[:, 7:64:8], T.h8[:, 7:64:8], AF.Identity, small, bias=KC * PEN, scale=PEN)
+    act("j16 pf", "ab", T.ab[:], T.j16[:], AF.Abs, bias=icol, scale=-1.0)
+    act("j16", "sgj", T.sgj[:], T.j16[:, 0:128], AF.Sign)
+    act("ab", "nq", T.nq[:], T.ab[:], AF.Sign)
+    act("sgj", "rst", T.rst[:], T.sgj[:], AF.Identity, bias=BIG, scale=-2 * BIG)
+    act("sgj", "keep", T.keep[:], T.sgj[:], AF.Copy)
+    act("nq", "mka", T.mka[:], T.nq[:, 0:128], AF.Identity, bias=1.0 / PEN, scale=-1.0 / PEN)
+    act("nq", "cap", T.cap[:], T.nq[:, 0:128], AF.Identity, bias=-BIG, scale=2 * BIG)
+    for j in range(3):
+        act("nq", "kq%d" % j, half(T.kq, j), T.nq[:, 1:129], AF.Identity, bias=17 * KL, scale=-18 * KL)
+    act("s88", "cl", T.cl[:], s8, AF.Identity, small, bias=896.0)
+    act("kq2 pf", "c1", T.cor[:, 1:2], icol, AF.Identity, small, bias=last, scale=KL)
+    act("c1", "cor", T.cor[:, 0:1], T.cor[:, 1:2], AF.Identity, small, bias=15 * KL, scale=-1.0)
+    act("kq2", "c2", T.cor[:, 2:3], last, AF.Identity, small, bias=128.0)
+    act("s88 kq2", "cr0", T.cr[:, 0:8], s8, AF.Identity, small, bias=last)
+    act("s88 c2", "cr1", T.cr[:, 8:16], s8, AF.Identity, small, bias=T.cor[:, 2:3])
+    ts("di", "dj", T.dj[:], T.di[:], 4, A.arith_shift_right, 7, A.bitwise_and)
+    ts("dj", "df", T.df[:], T.dj[:], 512.0, A.mult)
+    for k in range(8):
+        act("jr df", "CW%d" % k, half(T.CW, k), T.jr[:], AF.Identity, bias=T.df[:, k:k + 1])
 
-    def unpacker(b):
-        quant("Ez", "E%d" % b, "E", EW * b, EW * b + EW, T.Ez[:, 3 - b:3 - b + 4 * EW])
-    quant("uin", "u", "u", 0, 128, T.uin[:])
-    unpacker(0)
-    cp("u offc", "qu1c", words("u1c", 0, 128), words("u", 0, 128).indirect(T.offc[:, 64:72]))
-    act("u offc", "su1c", T.su1c[:], T.su[:].indirect(T.offc[:, 64:72]), AF.Copy)
-
-    def spread(i):
-        cp("u offc", "quR%d" % i, words("uR", 128 * i, 128 * i + 128), words("u", 0, 128).indirect(T.offc[:, 8 * i:8 * i + 8]))
-        act("u offc", "suR%d" % i, T.suR[:, 128 * i:128 * i + 128], T.su[:].indirect(T.offc[:, 8 * i:8 * i + 8]), AF.Copy)
-
-    def late_constants_g():
-        iota("j16", T.j16[:], [[0, 16], [1, 16]], 0)
-        iota("di", T.di[:], [[16, 8]], 143, -1, small=False)
-        iota("jr", T.jr[:], [[4096, 2], [1, 128]], 0)
-        iota("Kl2", T.Kl[:, 64:512], [[0, 448]], 0)
-        kl = T.Kl[:, 0:64]
-        iota("Kl", kl, [[0, 64]], 256)
-        iota("Kb", T.Kb[:], [[0, 512]], 1)
-        sel("Kl", kl, [[-1, 2], [0, 16], [1, 2]], A.is_equal, 0.0, 0, 0)
-        sel("Kb", T.Kb[:], [[-16, 8], [0, 64]], A.is_ge, 0.0, 0, 1)
-        sel("Kl", kl, [[0, 2], [-16, 8], [0, 4]], A.is_ge, 0.0, 0, 1)
-        sel("Kb", T.Kb[:], [[16, 8], [0, 64]], A.is_ge, 0.0, 15, -1)
-        sel("Kl", kl, [[0, 2], [16, 8], [0, 4]], A.is_ge, 0.0, 15, -1)
-        for a, n, cs in CT:
-            lo = 4 * (a + 16 * cs[3])
-            iota(" ".join("C%s" % c for c in cs), T.Ct[:, lo:4 * (a + n)], [[0, 4 * (a + n) - lo]], 0)
-        iota("rs0", T.rs[:, 0:1], [[0, 1]], 0)
-        iota("Or", T.Or[:], [[0, 256]], 0)
-        iota("CG", T.CG[:], [[1, 8], [0, 256]], 0)
-
-    def late_constants_s():
-        act("j16 pf", "ab", T.ab[:], T.j16[:], AF.Abs, bias=icol, scale=-1.0)
-        act("j16", "sgj", T.sgj[:], T.j16[:], AF.Sign)
-        act("pf", "cor", T.cor[:, 0:1], icol, AF.Identity, bias=15 * KL, scale=-KL)
-        act("ab", "nq", T.nq[:], T.ab[:], AF.Sign)
-        act("sgj", "rst", T.rst[:], T.sgj[:], AF.Identity, bias=BIG, scale=-2 * BIG)
-        act("sgj", "keep", T.keep[:], T.sgj[:], AF.Copy)
-        act("nq", "mka", T.mka[:], T.nq[:, 0:128], AF.Identity, bias=-1.0 / PEN, scale=1.0 / PEN)
-        act("nq", "cap", T.cap[:], T.nq[:], AF.Identity, bias=-BIG, scale=2 * BIG)
-        act("nq", "kap", T.kap[:], T.nq[:], AF.Identity, bias=16 * KL, scale=-17 * KL)
-        act("s88", "cl", T.cl[:], T.stg[:, 88:104], AF.Identity, bias=1024.0)
-        act("s88 cor", "cr", T.cr[:], T.stg[:, 88:104], AF.Identity, bias=T.cor[:, 0:1])
-
-    def offsets_window():
-        ts("dj", "df", T.df[:], T.dj[:], 512.0, A.mult)
-        for k in range(8):
-            act("jr df", "CW%d" % k, T.CW[:, 256 * k:256 * k + 256], T.jr[:], AF.Identity, bias=T.df[:, k:k + 1])
-
-    wall = " ".join(n + str(k) for k in range(2) for n in ["W0_%d" % i for i in range(8)] + ["W1a", "W1b", "W2a", "W2b", "W3a", "W3b"])
-    sw = " ".join("Sw%d%d" % (i, k) for i in range(8) for k in range(2))
-    cw = " ".join("CW%d" % i for i in range(8))
+    wall = " ".join(keys(n, r, k) for k in range(2) for n, r in [("W0", range(4)), ("Wa", range(1, 8)), ("Wb", range(1, 8))])
 
     def parts(k):
-        w0, o = " ".join("W0_%d%d" % (i, k) for i in range(8)), 4096 * k
-        for i in range(8):
-            key, ps = prod("T%d E%d" % (k, i % 4), "E", EW * (i % 4) + 16 * (i // 4), "T", k)
-            act(key, "W0_%d%d" % (i, k), T.Wn[:, o + 128 * i:o + 128 * i + 128], ps, AF.Copy)
-        for q in range(1, 4):
-            n, rot = 32 * q, "rot%d" % k
-            dma("y", rot, w0, "W%da%d" % (q, k), T.Wn[0:128 - n, o + 1024 * q:o + 1024 * q + 1024], T.Wn[n:128, o:o + 1024])
-            dma("y", rot, w0, "W%db%d" % (q, k), T.Wn[128 - n:128, o + 1024 * q:o + 1024 * q + 1024], T.Wn[0:n, o:o + 1024])
+        w0, o = keys("W0", range(4), k), 4096 * k
+        for b in range(4):
+            key, c = prod(["T%d E%d" % (k, b)], [("E", 128 * b, "T", 128 * k)], SIDE)
+            act(key, "W0%d%d" % (b, k), T.Wn[:, o + 128 * b:o + 128 * b + 128], (c, 128), AF.Copy)
+        for q in range(1, 8):
+            n, rot = 16 * q, "rot%d" % k
+            dma("y", rot, w0, "Wa%d%d" % (q, k), T.Wn[0:128 - n, o + 512 * q:o + 512 * q + 512], T.Wn[n:128, o:o + 512], 4500)
+            dma("y", rot, w0, "Wb%d%d" % (q, k), T.Wn[128 - n:128, o + 512 * q:o + 512 * q + 512], T.Wn[0:n, o:o + 512], 4500)
 
     def likings(k):
         for i in range(8):
-            key, ps = prod("T%d suR%d quR%d" % (k, i, i), "uR", 128 * i, "T", k)
-            o = 256 * i + 128 * k
-            act(key, "Sw%d%d" % (i, k), T.Sw[:, o:o + 128], ps, AF.Copy)
+            key, c = prod(["T%d suR%d quR%d" % (k, 128 * i, 128 * i)], [("uR", 128 * i, "T", 128 * k)], SIDE)
+            act(key, "Sw%d%d" % (i, k), half(T.Sw, 8 * k + i), (c, 128), AF.Copy)
 
     def state(t, k):
-        Mn, got = "M%d" % t, {}
-
-        def products():
-            for n, b in [("W", 0), ("W", 1), ("E", 0), ("W", 2), ("E", 1), ("W", 3), ("E", 2), ("E", 3)]:
-                if n == "W":
-                    kw, pw = prod("M%d mq ms qW sW" % k, "W", 128 * b, Mn, k, (k + b) % 2 if b < 2 else b + 4)
-                    act(kw, "R%d%d" % (b, k), T.Rb[:, 256 * b + 128 * k:256 * b + 128 * k + 128], pw, AF.Relu, scale=0.03125)
-                else:
-                    got[b] = prod("M%d mq ms E%d" % (k, b), "E", EW * b, Mn, k, 2 + b)
-            for b in range(4):
-                tt(got[b][0] + " R%d%d" % (b, k), "X%d%d" % (b, k), T.X[:, 512 * k + b:512 * k + 512:4], got[b][1],
-                   T.Rb[:, 256 * b + 128 * k:256 * b + 128 * k + 128], A.add)
-        return [products, lambda: quant(
-            " ".join("X%d%d" % (b, k) for b in range(4)), "T%d" % k, "T", 128 * k, 128 * k + 128, T.X[:, 512 * k:512 * k + 512])]
+        Mn, got, m = "M%d" % t, {}, "M%d" % k + (" mq ms" if k == ka else "")
+        for b in range(4):
+            key, c = prod([m + " qW sW"], [("W", 128 * b, Mn, 128 * k)])
+            act(key, "R%d%d" % (b, k), half(T.Rb, 2 * b + k), (c, 128), AF.Relu, scale=0.03125)
+        for b in range(4):
+            key, c = prod([m + " E%d" % b], [("E", 128 * b, Mn, 128 * k)])
+            tt(key + " R%d%d" % (b, k), "X%d%d" % (b, k), T.X[:, 512 * k + b:512 * k + 512:4], (c, 128), half(T.Rb, 2 * b + k), A.add, cycles(128))
+        quant(keys("X", range(4), k), "T%d" % k, "T", 128 * k, half(T.X, k, 512))
 
     def matching(k):
-        a, b, e = 64 * k, 64 * k + 64, slice(8 * k, 8 * k + 8)
-        n = str(k)
-        top, fg, fh, run = T.pm[:, b - 1:b], T.fg[:, b - 1:b], T.fh[:, b - 1:b], T.pm[:, a:b]
-        out = []
+        n, a, o = str(k), 80 * k + 8, 192 * k
+        run, top = T.pm[:, a:a + 64], T.pm[:, a + 63:a + 64]
+        n1, (n2, sa, sb) = T.alt[:, 16 * k + 11:16 * k + 12], [T.sc[:, 4 * k + j:4 * k + j + 1] for j in range(3)]
+        pk, c = prod(["T%d qu1c0 su1c0" % k], [("T", 128 * k, "u1c", 0)])
         for step in range(7):
-            src, sk = (T["ps" + n][:, 0:64], "p" + n) if step == 0 else (T.Sp[:, a:b], "Sp" + n)
-            one = [lambda src=src, sk=sk: scan(sk + " neg", "pm" + n, run, src, T.neg[:], A.max, A.max, LOW)]
-            two = [lambda: ts("pm" + n, "ne" + n, T.ne[:, a:b], run, top, A.is_ge)]
-            three = [lambda: scan("dg ne" + n, "fg" + n, T.fg[:, a:b], T.ne[:, a:b], T.dg[:], A.mult, A.add),
-                     lambda: scan("dh ne" + n, "fh" + n, T.fh[:, a:b], T.ne[:, a:b], T.dh[:], A.mult, A.add, -1.0)]
-            if step == 6:
-                one.append(lambda: tt("Sp" + n, "t0" + n, T.t0[:, e], T.Sp[:, a:a + 8], T.Sp[:, a + 8:a + 16], A.min))
-                two.append(lambda: tt("Sp%d t0%d" % (k, k), "t1" + n, T.t1[:, e], T.t0[:, e], T.Sp[:, a + 16:a + 24], A.min))
-                three.append(lambda: ts("t1" + n, "t4" + n, T.t4[:, e], T.t1[:, e], 28 * PEN, A.add))
-                out += [one, two, three]
-                break
-            out += [one, two, three,
-                    [lambda: ts("gd fg" + n, "rp" + n, T.rp[:, a:b], T.gd[:], fg, A.is_equal, -ROWPEN, A.mult),
-                     lambda: ts("hc fg%d fh%d" % (k, k), "cp" + n, T.cp[:, a:b], T.hc[:], fh, A.is_equal, fg, A.mult)],
-                    [lambda: tt("rp%d cp%d" % (k, k), "rc" + n, T.rc[:, a:b], T.rp[:, a:b], T.cp[:, a:b], A.add)],
-                    [lambda src=src, sk=sk: tt(sk + " rc" + n, "Sp" + n, T.Sp[:, a:b], src, T.rc[:, a:b], A.add)]]
-        out += [[lambda: ts("hc fg%d fh%d" % (k, k), "t2" + n, T.t2[:, e], T.hc[:, 0:8], fh, A.is_equal, fg, A.mult),
-                 lambda: op("v", "t4" + n, "sg" + n, lambda: V.tensor_reduce(T.sg[:, k:k + 1], T.t4[:, e], AX, A.add, negate=True))],
-                [lambda: tt("t4%d t2%d" % (k, k), "t3" + n, T.t3[:, e], T.t4[:, e], T.t2[:, e], A.add),
-                 lambda: ts("sg%d fg%d" % (k, k), "sx" + n, T.sg[:, 2 + k:3 + k], T.sg[:, k:k + 1], fg, A.subtract, 4 * PEN, A.add)],
-                [lambda: ts("t3%d sx%d" % (k, k), "t5" + n, T.t5[:, e], T.t3[:, e], 12 * PEN, A.is_equal, T.sg[:, 2 + k:3 + k], A.mult),
-                 lambda: tt("offc mka t3" + n, "A" + n, T.At[:, k:512:4], T.t3[:, e].indirect(T.offc[:, 72:80]), T.mka[:], A.mult)],
-                [lambda: tt("offc mka t5" + n, "A%d" % (2 + k), T.At[:, 2 + k:512:4], T.t5[:, e].indirect(T.offc[:, 72:80]), T.mka[:], A.mult)]]
-        return [lambda fs=fs: [f() for f in fs] for fs in out]
+            z, zn, zk, znk = T["Z%d" % (step % 2)], T["Z%d" % (1 - step % 2)], "%d%d" % (step % 2, k), "%d%d" % (1 - step % 2, k)
+            src, sk = ((c, 64), pk) if step == 0 else (z[:, o + 2:o + 192:3], "S" + zk)
+            x1, r8 = [T.cn[:, 16 * k + 2 * step + j:16 * k + 2 * step + j + 1] for j in range(2)]
+            xk, rk = "x%d%d" % (step, k), "r%d%d" % (step, k)
+            both = " %s %s" % (xk, rk)
+            scan(sk + " neg", "pm" + n, run, src, T.neg[:], A.max, A.max, LOW)
+            act("pm%d o80" % k, rk + " jh" + n, half(T.jh, k, 64), T.pm[:, a - 8:a + 56].indirect(T.offc[:, 80:84]), AF.Sign, picks(64),
+                bias=top, scale=-1.0, accum_out=r8)
+            act("pm" + n, xk + " jx" + n, half(T.jx, k, 64), T.pm[:, a - 1:a + 63], AF.Sign, small, bias=top, scale=-1.0, accum_out=x1)
+            if step == 0:
+                act("%s pm%d" % (pk, k), "S" + zk, z[:, o + 2:o + 192:3], src, AF.Copy, small)
+            if step < 6:
+                ts("h8" + both, "r" + zk, z[:, o + 1:o + 192:3], T.h8[:], r8, A.is_equal, x1, A.mult)
+                ts("g7" + both, "c" + zk, z[:, o:o + 192:3], T.g7[:], r8, A.add, x1, A.is_equal)
+                scan("c%s r%s S%s d00 d01 d02" % (zk, zk, zk), "c%s r%s S%s" % (znk, znk, znk), zn[:, o:o + 192], T.d0[:], z[:, o:o + 192],
+                     A.mult, A.add, n=192)
+        scan("zz " + keys("x", range(6), k) + " " + keys("r", range(6), k), "n1" + n, T.alt[:, 16 * k:16 * k + 12],
+             T.cn[:, 16 * k:16 * k + 12], T.zz[:, 0:12], A.subtract, A.add, -20.0)
+        ts("n1" + n, "n2" + n, n2, n1, 0.5, A.mult, -4.0, A.add)
+        scan(sk + " sa", "seg" + n, half(T.seg, k, 64), src, T.sa[:], A.min, A.add)
+        tmp = half(T.tmp, k)
+        tt("seg%d o72 mka" % k, "tmp" + n, tmp, half(T.seg, k, 64).indirect(T.offc[:, 72:80]), T.mka[:], A.mult, picks(128))
+        ts("n1" + n + both, "sa" + n, sa, x1, r8, A.subtract, n1, A.subtract)
+        ts("n2" + n + both, "sb" + n, sb, r8, x1, A.subtract, n2, A.add)
+        ts("tmp%d A%d" % (k, k), "A0" + n, T.At[:, 512 * k + 1:512 * k + 512:4], tmp, 8.0, A.min)
+        ts("tmp%d sa%d A%d" % (k, k, k), "A1" + n, T.At[:, 512 * k + 2:512 * k + 512:4], tmp, 8.0, A.is_ge, sa, A.mult)
+        ts("tmp%d sb%d A%d %s" % (k, k, k, rk), "A2" + n, T.At[:, 512 * k + 3:512 * k + 512:4], tmp, r8, A.is_equal, sb, A.mult)
 
-    def scores(k):
-        mm("T%d qu1c su1c" % k, "p%d" % k, k, 128, "T", 128 * k, "u1c", 0)
+    def listing(k):
+        n, e = str(k), slice(8 * k, 8 * k + 8)
+        sw, win = keys("Sw", range(8), k) + " l1" + n, half(T.Sw, k, 1024).indirect(T.l1[:, e])
+        quant(keys("A", range(3), k), "qA" + n, "A", 128 * k, half(T.At, k, 512))
+        key, c = prod(["qA%d L" % k], [("A", 128 * k, "L", 0)])
+        tt("cl " + key, "l1f" + n, T.l1f[:, e], (c, 8), T.cl[:], A.add)
+        cp("l1f" + n, "l1" + n, T.l1[:, e], T.l1f[:, e])
+        act(sw, "Rr" + n, half(T.Rr, k), win, AF.Copy, picks(128))
+        tt(sw + " cap", "Rm" + n, half(T.Rm, k), win, T.cap[:], A.max, picks(128))
+        scan("rst Rm" + n, "Lt" + n, half(T.Lt, k), T.rst[:], half(T.Rm, k), A.max, A.min, n=128)
+        act(keys("CW", range(8)) + " l1" + n, "Pr" + n, half(T.Pr, k), T.CW[:].indirect(T.l1[:, e]), AF.Identity, picks(128), bias=4096.0 * k)
 
-    def merge(first, second, lead, extra):
-        for f in first[:lead]:
-            f()
-        rest = first[lead:]
-        for i in range(max(len(rest), len(second))):
-            if i < len(second):
-                second[i]()
-            if i < len(rest):
-                rest[i]()
-            if i in extra:
-                extra[i]()
+    def mine(k, c):
+        return T.Lt[:, 128 * k + 16 * c + 15:128 * k + 16 * c + 16]
 
-    def slot(c):
-        for a, n_, cs in CT:
-            if c in cs:
-                return T.Ct[:, 4 * a + cs.index(c):4 * (a + (256 if c == "d" else 16 * c)):4]
+    def pack(i, r):
+        quant(r, "c%d" % i, "C", 128 * i, half(T.Ct, i, 512))
 
-    def compare(c):
-        ts("Rr Lt", "C%d" % c, slot(c), T.Rr[:, 0:16 * c], T.Lt[:, 16 * c + 15:16 * c + 16], A.is_lt)
+    def inside(k):
+        n, e, both = str(k), slice(8 * k, 8 * k + 8), "Rr%d Lt%d" % (k, k)
+        diag = T.Ct[:, 1024 * k:1024 * k + 512:4]
+        tt(both, "Cd" + n, diag, half(T.Lt, k), half(T.Rr, k), A.is_ge, cycles(256))
+        for i in range(2):
+            for j, c in enumerate(TRI[i]):
+                if c != "d":
+                    o = 1024 * k + 512 * i
+                    slot, key = T.Ct[:, o + j:o + 64 * c:4], "C%d%d" % (c, k)
+                    ts(both, key, slot, T.Rr[:, 128 * k:128 * k + 16 * c], mine(k, c), A.is_lt, n=16 * c)
+                    o = 512 * k + 8 * c * (c - 1)
+                    act(key, "rs%d%d" % (c, k), T.junk[:, o:o + 16 * c], slot, AF.Copy, cycles(16 * c), accum_out=T.rs[:, 8 * k + c:8 * k + c + 1])
+            pack(2 * k + i, keys("C", TRI[i], k))
+        scan("keep Cd" + n, "ds" + n, half(T.ds, k), T.keep[:], diag, A.mult, A.add)
+        tt("ds%d cr%d" % (k, k), "u1" + n, T.u1[:, e], T.cr[:, e], ends(T.ds, k), A.subtract)
+        tt("u1%d rs0 " % k + keys("rs", range(1, 8), k), "kq" + n, ends(T.kq, k), T.u1[:, e], T.rs[:, e], A.subtract)
 
-    def rowsum(c):
-        o = 8 * c * (c - 1)
-        act("C%d" % c, "rs%d" % c, T.junk[:, o:o + 16 * c], slot(c), AF.Copy, accum_out=T.rs[:, c:c + 1])
+    def across():
+        both = "Rr%d Lt%d" % (kb, ka)
+        for c in range(8):
+            slot, key, acc = T.Ct[:, 2048 + 512 * (c // 4) + c % 4:2560 + 512 * (c // 4):4], "Cx%d" % c, T.rs[:, 16 + c:17 + c]
+            if c >= 8 - NA:
+                act(both, "sn%d" % c, half(T.sn, c), half(T.Rr, kb), AF.Sign, bias=mine(ka, c), scale=-1.0)
+                act("sn%d" % c, "%s rq%d" % (key, c), slot, half(T.sn, c), AF.Relu, scale=2.0 * ka - 1, accum_out=acc)
+            else:
+                ts(both, key, slot, half(T.Rr, kb), mine(ka, c), A.is_lt if ka else A.is_gt, n=128)
+                act(key, "rq%d" % c, half(T.junk, 8 + c), slot, AF.Copy, accum_out=acc)
+        for i in range(2):
+            pack(4 + i, keys("Cx", range(4 * i, 4 * i + 4)))
 
-    def pack(i):
-        a, n_, cs = CT[i]
-        quant(" ".join("C%s" % c for c in cs), "c%d" % i, "C", a, a + n_, T.Ct[:, 4 * a:4 * (a + n_)])
+    def ranks(k):
+        tiles, e = [2 * k, 2 * k + 1] + ([4, 5] if k == kb else []), slice(8 * k, 8 * k + 8)
+        tiles = tiles[2:] + tiles[:2]
+        key, c = prod(["K0 K1 c%d" % i for i in tiles], [("K", 128 * (i // 4), "C", 128 * i) for i in tiles])
+        scan("kq%d %s" % (k, key), "ex%d" % k, half(T.ex, k), (c, 128), half(T.kq, k), A.min, A.add, 17 * KL, n=128)
+        if k == ka:
+            tt("ex%d " % k + keys("rq", range(8)), "rkf", T.rkf[:], ends(T.ex, k), T.rs[:, 16:24], A.subtract if ka else A.add)
+        ts("rkf cor ex%d" % k if k == ka else "cor ex%d" % k, "rk%d" % k, T.rk[:, e], T.rkf[:] if k == ka else ends(T.ex, k), T.cor[:, 0:1], A.add)
+        cp("Pr%d rk%d" % (k, k), "Or", T.Or[:].indirect(T.rk[:, e]), half(T.Pr, k), picks(128, 3.8))
 
-    def sums(i):
-        mm("K c%d" % i, "p1" if i == 0 else "", 1, CT[i][1], "K", 0, "C", CT[i][0], i == 0, i == 3)
+    def order(k):
+        scan("kq2 Or", "ex2%d" % k, half(T.ex2, k), half(T.Or, k), half(T.kq, 2), A.min, A.add, 17 * KL, n=128)
+        ts("ex2%d cor" % k, "l2%d" % k, T.l2[:, 8 * k:8 * k + 8], ends(T.ex2, k), T.cor[:, 0:1], A.add)
 
-    ka, kb = rank // 4, 1 - rank // 4
-    for t in range(R):
-        if t == 0:
-            quant("xin", "T0 T1", "T", 0, C, T.xin[:])
-            scores(0)
-            scores(1)
-            ts("gd0", "gd", T.gd[:], T.gd0[:], -PEN, A.mult)
-            unpacker(1)
-            late_constants_g()
-            extra = {i + 4: (lambda i=i: spread(i)) for i in range(8)}
-            extra[0] = lambda: unpacker(2)
-            extra[1] = lambda: (unpacker(3), parts(0), parts(1), late_constants_s())
-            extra[16] = lambda: (likings(0), likings(1))
-            extra[19] = lambda: ts("di", "dj", T.dj[:], T.di[:], 4, A.arith_shift_right, 7, A.bitwise_and)
-            extra[20] = offsets_window
-            extra[30] = lambda: quant("Kl Kl2", "L", "L", 0, 128, T.Kl[:])
-            extra[31] = lambda: quant("Kb", "K", "K", 0, 128, T.Kb[:])
-            merge(matching(0), matching(1), 0, extra)
-        else:
-            merge(state(t - 1, ka) + [lambda: (scores(ka), parts(ka))] + matching(ka),
-                  state(t - 1, kb) + [lambda: (scores(kb), parts(kb), likings(ka), likings(kb))] + matching(kb), LEAD, {})
-        quant("A0 A1 A2 A3", "A", "A", 0, 128, T.At[:])
-        mm("A L", "p0", 0, 128, "A", 0, "L", 0)
-        tt("p0 cl", "l1f", T.l1f[:], T.ps0[:, 0:16], T.cl[:], A.add)
-        cp("l1f", "l1", T.l1[:], T.l1f[:])
-        act(sw + " l1", "Rr", T.Rr[:], T.Sw[:].indirect(T.l1[:]), AF.Copy)
-        tt(sw + " l1 cap", "Rm", T.Rm[:], T.Sw[:].indirect(T.l1[:]), T.cap[:], A.max)
-        scan("rst Rm", "Lt", T.Lt[:], T.rst[:], T.Rm[:], A.max, A.min)
-        act(cw + " l1", "Pr", T.Pr[:], T.CW[:].indirect(T.l1[:]), AF.Copy)
-        for i, c in enumerate((15, 14, 13)):
-            act("Rr Lt", "sn%d" % i, T.sn[:, 256 * i:256 * i + 16 * c], T.Rr[:, 0:16 * c], AF.Sign,
-                bias=T.Lt[:, 16 * c + 15:16 * c + 16], scale=-1.0)
-        for i, c in enumerate((15, 14, 13)):
-            act("sn%d" % i, "C%d rs%d" % (c, c), slot(c), T.sn[:, 256 * i:256 * i + 16 * c], AF.Relu, accum_out=T.rs[:, c:c + 1])
-        for c in (12, 11, 10, 9):
-            compare(c)
-        tt("Rr Lt", "Cd", slot("d"), T.Lt[:], T.Rr[:], A.is_ge)
-        for c in (8, 7, 6, 5):
-            compare(c)
-        pack(1)
-        pack(0)
-        for c in (4, 3, 2, 1):
-            compare(c)
-        for c in range(12, 0, -1):
-            rowsum(c)
-        scan("keep Cd", "ds", T.ds[:], T.keep[:], slot("d"), A.mult, A.add)
-        pack(2)
-        pack(3)
-        for i in range(4):
-            sums(i)
-        tt("cr ds", "u1", T.u1[:], T.cr[:], T.ds[:, 15:256:16], A.subtract)
-        wr["p1"] = ("ct", cnt["ct"])
-        tt("u1 " + " ".join("rs%d" % c for c in range(16)), "u2", T.u2[:], T.u1[:], T.rs[:], A.subtract)
-        scan("kap p1", "ex", T.ex[:], T.kap[:], T.ps1[:, 0:C], A.add, A.min)
-        tt("ex u2", "rkf", T.rkf[:], T.ex[:, 15:256:16], T.u2[:], A.add)
-        cp("rkf", "rk", T.rk[:], T.rkf[:])
-        cp("Pr rk", "Or", T.Or[:].indirect(T.rk[:]), T.Pr[:])
-        scan("kap Or", "ex2", T.ex2[:], T.kap[:], T.Or[:], A.add, A.min)
-        ts("ex2 cor", "l2", T.l2[:], T.ex2[:, 15:256:16], T.cor[:, 0:1], A.add)
+    def send(t, k):
         Bn, Mn = "B%d" % t, "M%d" % t
-        for k in (ka, kb):
-            for b in range(4):
-                win = T.Wn[:, 128 * b:128 * b + 7808].indirect(T.l2[:, 8 * k:8 * k + 8])
-                out = T.Bt[:, 512 * k + b:512 * k + 512:4]
-                if b % 2:
-                    act(wall + " l2", "B%d%d" % (b, k), out, win, AF.Copy)
+        for b in range(4):
+            win = T.Wn[:, 128 * b:128 * b + 7808].indirect(T.l2[:, 8 * k:8 * k + 8])
+            out = T.Bt[:, 512 * k + b:512 * k + 512:4]
+            if b % 2:
+                act(wall + " l2%d" % k, "B%d%d" % (b, k), out, win, AF.Copy, picks(128))
+            else:
+                cp(wall + " l2%d" % k, "B%d%d" % (b, k), out, win, picks(128))
+        quant(keys("B", range(4), k), "qB%d" % k, Bn, 128 * k, half(T.Bt, k, 512))
+        for codes in (True, False):
+            trs = []
+            for d, eng in deal(T, topo, rank, k):
+                rid, pid = topo.addr(T.cores[d])[0:2]
+                if codes:
+                    s_, d_ = bytes_of(Bn, L * d, L * d + L), bytes_of(Mn, L * rank, L * rank + L)
                 else:
-                    cp(wall + " l2", "B%d%d" % (b, k), out, win)
-            quant(" ".join("B%d%d" % (b, k) for b in range(4)), "qB%d" % k, Bn, 128 * k, 128 * k + 128, T.Bt[:, 512 * k:512 * k + 512])
-            need("g", ["qB%d" % k], [])
-            for codes in (True, False):
-                trs = []
-                for d, eng in deal(T, topo, rank, k):
-                    rid, pid = topo.addr(T.cores[d])[0:2]
-                    if codes:
-                        s_, d_ = bytes_of(Bn, L * d, L * d + L), bytes_of(Mn, L * rank, L * rank + L)
-                    else:
-                        s_, d_ = T["s" + Bn][:, L * d:L * d + L], T["s" + Mn][:, L * rank:L * rank + L]
-                    trs.append(RemoteDMATransfer(dst_ids=[DstId(rid=rid, pnc=pid)], dma_engine_mask=sum(1 << e for e in eng),
-                                                 remote_sem=T.sem["arr%d%d" % (t, ka)], src=s_, dst=d_))
-                    cnt["sent"] = cnt.get("sent", 0) + len(eng)
-                g.remote_dma_fused(trs, local_sem=T.sem.sent)
-        own = T.offc[:, 88:90]
-        cp("offc qB%d" % ka, "mq", words(Mn, L * rank, L * rank + L), words(Bn, L * rank, L * rank + L).indirect(own))
-        cp("offc qB%d" % ka, "ms", T["s" + Mn][:, L * rank:L * rank + L], T["s" + Bn][:, L * rank:L * rank + L].indirect(own))
-        for k in range(2):
-            arr = "arr%d%d" % (t, k)
-            cnt[arr] = sum(2 * len(e) for s in range(4 * k, 4 * k + 4) if s != rank for d, e in deal(T, topo, s, ka) if d == rank)
-            wr["M%d" % k] = (arr, cnt[arr])
+                    s_, d_ = T["s" + Bn][:, L * d:L * d + L], T["s" + Mn][:, L * rank:L * rank + L]
+                trs.append(RemoteDMATransfer(dst_ids=[DstId(rid=rid, pnc=pid)], dma_engine_mask=sum(1 << e for e in eng),
+                                             remote_sem=T.sem["arr%d%d" % (t, ka)], src=s_, dst=d_))
+            op("g", "qB%d" % k, "gone%d%d%d" % (t, k, codes), lambda trs=trs: g.remote_dma_fused(trs, local_sem=T.sem.sent), 150, 0, "sent",
+               sum(len(eng) for d, eng in deal(T, topo, rank, k)))
+        got = sum(2 * len(e) for s in range(4 * k, 4 * k + 4) if s != rank for d, e in deal(T, topo, s, ka) if d == rank)
+        op("a", keys("gone%d%d" % (t, k), (0, 1)), "M%d" % k, None, 0, FLY[k != ka], "arr%d%d" % (t, k), got)
+        if k == kb:
+            own = T.offc[:, 88:90]
+            cp("o88 qB%d" % ka, "mq", words(Mn, L * rank, L * rank + L), words(Bn, L * rank, L * rank + L).indirect(own), picks(32))
+            cp("o88 qB%d" % ka, "ms", T["s" + Mn][:, L * rank:L * rank + L], T["s" + Bn][:, L * rank:L * rank + L].indirect(own), picks(32))
 
-    quant("vin", "v", "v", 0, 128, T.vin[:])
-    cp("Or", "oi", T.oi[:], T.Or[:])
-    act("CG l1", "OLg", T.OL[:, 256:512], T.CG[:].indirect(T.l1[:]), AF.Copy)
-    ts("oi", "oj", T.oj[:], T.oi[:], 127, A.bitwise_and)
-    ts("oi", "oi", T.oi[:], T.oi[:], 5, A.arith_shift_right, 128, A.bitwise_and)
-    tt("oi oj", "OLo", T.OL[:, 0:256], T.oi[:], T.oj[:], A.add)
-    dma("y", "outs", "OLo OLg", "", T.ol[:], T.OL[0:128:16, :])
+    for t in range(R):
+        for k in (ka, kb):
+            if t == 0:
+                quant("xin%d" % k, "T%d" % k, "T", 128 * k, half(T.xin, k, 512))
+            else:
+                state(t - 1, k)
+            matching(k)
+            line.update(s="side", t="sidet")
+            parts(k)
+            likings(k)
+            line.clear()
+            listing(k)
+            inside(k)
+        across()
+        for k in (ka, kb):
+            ranks(k)
+        for k in (ka, kb):
+            order(k)
+        line.update(v="sendv%d" % t, s="sends%d" % t, g="g")
+        for k in (ka, kb):
+            send(t, k)
+        line.clear()
+
+    cp("Or", "oi", T.oi[:], T.Or[:], cycles(256))
+    for k in range(2):
+        act("CG l1%d" % k, "OLg%d" % k, half(T.OL, 2 + k), T.CG[:].indirect(T.l1[:, 8 * k:8 * k + 8]), AF.Copy, picks(128))
+    ts("oi", "oj", T.oj[:], T.oi[:], 127, A.bitwise_and, n=256)
+    ts("oi", "oi", T.oi[:], T.oi[:], 5, A.arith_shift_right, 128, A.bitwise_and, n=256)
+    tt("oi oj", "OLo", T.OL[:, 0:256], T.oi[:], T.oj[:], A.add, cycles(512))
+    dma("y", "outs", "OLo OLg0 OLg1", "", T.ol[:], T.OL[0:128:16, :])
     for k in (ka, kb):
         a, b = 128 * k, 128 * k + 128
-        for f in state(R - 1, k):
-            f()
-        if k == kb:
-            mm("T0 T1 v", "p0", 0, C, "v", 0, "T", 0)
+        state(R - 1, k)
+        key, c = prod(["T%d v" % k], [("v", 0, "T", a)])
         dma("y", "outs", "T%d" % k, "", T.oc[:, 4 * a:4 * b], bytes_of("T", a, b))
-    for i in range(4):
-        dma("y", "outs", "T0 T1", "", T.osc[4 * i:4 * i + 4, :], T.sT[32 * i:32 * i + 4, :])
-    act("p0", "ys", T.ys[:], T.ps0[:, 0:C], AF.Copy)
-    dma("s", "outs", "ys", "", T.y[:], T.ys[:])
+        for i in range(4):
+            dma("y", "outs", "T%d" % k, "", T.osc[4 * i:4 * i + 4, a:b], T.sT[32 * i:32 * i + 4, a:b])
+        act(key, "ys%d" % k, half(T.ys, k), (c, 128), AF.Copy)
+        dma("s", "outs", "ys%d" % k, "", T.y[:, a:b], half(T.ys, k))
+
+    cnt, seen = {}, {}
+    for c in issue_order(calls):
+        q, want = c["q"], {}
+        for d in c["deps"]:
+            if q != "a" and d is not c["sums"] and d["sem"] != "sent" and not (d["inc"] == 16 and d["sem"] == c["sem"]):
+                want[d["sem"]] = max(want.get(d["sem"], 0), d["count"] if d["inc"] == 1 else cnt[d["sem"]])
+        for sem, val in want.items():
+            if seen.get((q, sem), 0) < val:
+                Q[q].wait_ge(T.sem[sem], val)
+                seen[(q, sem)] = val
+        if q in "vstgy":
+            done = c["fn"]()
+            if c["sem"] != "sent":
+                done.then_inc(T.sem[c["sem"]], c["inc"])
+        c["count"] = cnt[c["sem"]] = cnt.get(c["sem"], 0) + c["inc"]
     for sem in cnt:
         if seen.get(("g", sem), 0) < cnt[sem]:
             g.wait_ge(T.sem[sem], cnt[sem])

@@ -8,10 +8,13 @@ KC = 128.0
 LOW = -9e29
 BIG = 2.0 ** 90
 KL = 8192.0
-NA = 3
+NA = 4
+ON_SCALAR = [(7, 6, 5, 4), ()]
 TRI = [["d", 7, 6, 5], [4, 3, 2, 1]]
-CYC, WAIT, DMA, FLY = 1.04, 120, 2500, (2600, 4200)
-SLACK = 30
+CYC, WAIT, DMA, FLY = 1.0, 140, 4000, (2800, 4400)
+SLACK, GAP = 30, 2.0
+TURNS = 4
+ORDERS = {}
 ANY, SIDE = list(range(8)), [6, 7]
 
 SCRATCH = {}
@@ -20,7 +23,7 @@ for _n, _w, _d in [("xin", 1024, BF), ("uin", 512, BF), ("vin", 512, BF), ("X", 
                    ("Wn", 8192, BF), ("Sw", 2048, F32), ("CW", 1024, F32), ("CG", 1024, F32), ("Rb", 1024, F32),
                    ("pi", 4, I32), ("pt", 4, I32), ("pf", 8, F32), ("stg", 104, F32), ("offc", 104, U16),
                    ("h8", 64, F32), ("g7", 64, F32), ("neg", 64, F32), ("d0", 192, F32), ("sa", 64, F32), ("zz", 16, F32),
-                   ("di", 8, I32), ("dj", 8, I32), ("df", 8, F32), ("j16", 144, F32), ("jr", 128, F32),
+                   ("j16", 144, F32), ("W0", 1024, BF), ("S0", 256, F32),
                    ("ab", 144, F32), ("nq", 144, F32), ("cap", 128, F32), ("kq", 384, F32), ("rst", 128, F32),
                    ("sgj", 128, F32), ("keep", 128, BF), ("mka", 128, BF), ("cl", 8, F32), ("cr", 16, F32), ("cor", 4, F32),
                    ("Z0", 384, F32), ("Z1", 384, F32), ("pm", 160, F32), ("cn", 32, F32), ("jx", 128, BF), ("jh", 128, BF),
@@ -30,14 +33,18 @@ for _n, _w, _d in [("xin", 1024, BF), ("uin", 512, BF), ("vin", 512, BF), ("X", 
                    ("ex", 256, F32), ("rkf", 8, F32), ("rk", 16, U16), ("Or", 256, F32), ("ex2", 256, F32), ("l2", 16, U16),
                    ("oi", 256, I32), ("oj", 256, I32), ("OL", 512, F32), ("ys", 256, F32)]:
     SCRATCH[_n] = ("sbuf", [128, _w], _d)
-for _n, _w in [("u", 128), ("u1c", 128), ("uR", 1024), ("v", 128), ("W", 512), ("T", 256), ("E", 512), ("K", 256),
+for _n, _w in [("u", 128), ("u1c", 128), ("v", 128), ("W", 512), ("T", 256), ("E", 512), ("K", 256),
                ("L", 128), ("A", 256), ("C", 768)] + [("B%d" % _t, 256) for _t in range(R)] + [("M%d" % _t, 256) for _t in range(R)]:
     SCRATCH["q" + _n] = ("sbuf", [128, _w], Q8)
     SCRATCH["s" + _n] = ("sbuf", [128, _w], U8)
 for _b in range(8):
     SCRATCH["ps%d" % _b] = ("psum", [128, 512], F32)
+for _k in range(2):
+    SCRATCH["Dw%d" % _k] = ("dram", [16, 4096], BF)
+    SCRATCH["Ds%d" % _k] = ("dram", [8, 4096], F32)
 
-SEMAPHORES = (["cv", "cs", "ct", "cg", "ldx0", "ldx1", "ldu", "ldw", "ldv", "rot0", "rot1", "outs", "sent"]
+SEMAPHORES = (["cv", "cs", "ct", "cg", "ldx0", "ldx1", "ldu", "ldw", "ldv", "outs", "sent"]
+              + [_n + str(_k) for _n in ("pw", "pr", "sw", "sr") for _k in range(2)]
               + ["arr%d%d" % (_t, _k) for _t in range(R) for _k in range(2)])
 
 
@@ -52,54 +59,63 @@ def deal(T, topo, s, k):
 
 
 def issue_order(calls):
-    for c in reversed(calls):
-        c["way"] += c["cost"] + c["lat"]
-        for d in c["deps"]:
-            d["way"] = max(d["way"], c["way"] + (-d["lat"] if d is c["sums"] else WAIT))
-            d["users"].append(c)
-    ready, free, held, order = {q: [] for q in "vstgya"}, {q: 0.0 for q in "vstgya"}, [None] * 8, []
+    n, cost = len(calls), [c["cost"] for c in calls]
+    before = [[(d["n"], 0 if d is c["sums"] else d["lat"] + WAIT) for d in c["deps"]] for c in calls]
+    after = [[] for c in calls]
+    for i in range(n):
+        for j, gap in before[i]:
+            after[j].append((i, gap))
 
-    def enter(c):
-        c["at"] = max([d["end"] + (-d["lat"] if d is c["sums"] else WAIT) for d in c["deps"]] + [0.0])
-        ready[c["q"]].append(c)
+    def one_pass(first, then, at, way, banks):
+        ready, free, held, order = {q: [] for q in "vstgya"}, {q: 0.0 for q in "vstgya"}, [None] * 8, []
+        left, end = [len(x) for x in first], [None] * n
+        for i in range(n):
+            if not left[i]:
+                ready[calls[i]["q"]].append(i)
+        while len(order) < n:
+            best, times = None, [0.0] * 8
+            for b in range(8):
+                if held[b] is not None:
+                    ends = [end[u["n"]] for u in calls[held[b]]["uses"]]
+                    times[b] = None if None in ends else max(ends) + WAIT
+            for q, cs in ready.items():
+                can = []
+                for i in cs:
+                    open_ = [(times[b], b) for b in banks[i] if times[b] is not None]
+                    if open_ or not banks[i]:
+                        can.append((max(at[i], free[q], min(open_)[0] if open_ else 0.0), i, min(open_)[1] if open_ else None))
+                if can:
+                    now = min(x[0] for x in can)
+                    pick = max((x for x in can if x[0] == now), key=lambda x: way[x[1]])
+                    soon = [x for x in can if now + cost[pick[1]] - x[0] > SLACK + GAP * (x[0] - now) and way[x[1]] > way[pick[1]]]
+                    if soon:
+                        pick = max(soon, key=lambda x: way[x[1]])
+                    if best is None or pick[0] < best[0]:
+                        best = pick
+            start, i, b = best
+            order.append((i, b, None if b is None else held[b]))
+            if b is not None:
+                held[b] = i
+            ready[calls[i]["q"]].remove(i)
+            free[calls[i]["q"]] = end[i] = start + cost[i]
+            for j, gap in then[i]:
+                at[j], left[j] = max(at[j], end[i] + gap), left[j] - 1
+                if not left[j]:
+                    ready[calls[j]["q"]].append(j)
+        return order, end
 
-    def bank_time(b):
-        if held[b] is None:
-            return 0.0
-        return max(u["end"] for u in held[b]["uses"]) + WAIT if all("end" in u for u in held[b]["uses"]) else None
-
-    for c in calls:
-        c["left"] = len(c["deps"])
-        if not c["deps"]:
-            enter(c)
-    while len(order) < len(calls):
-        best, times = None, [bank_time(b) for b in range(8)]
-        for q, cs in ready.items():
-            can = []
-            for c in cs:
-                open_ = [(times[b], b) for b in c["banks"] if times[b] is not None]
-                if open_ or not c["banks"]:
-                    can.append((max(c["at"], free[q], min(open_)[0] if open_ else 0.0), c, min(open_)[1] if open_ else None))
-            if can:
-                now = min(x[0] for x in can)
-                pick = max((x for x in can if x[0] == now), key=lambda x: x[1]["way"])
-                soon = [x for x in can if x[0] < now + pick[1]["cost"] - SLACK and x[1]["way"] > pick[1]["way"]]
-                if soon:
-                    pick = max(soon, key=lambda x: x[1]["way"])
-                if best is None or pick[0] < best[0]:
-                    best = pick
-        at, c, b = best
-        if b is not None:
-            c["deps"] += held[b]["uses"] if held[b] else []
-            held[b], c["bank"] = c, b
-        ready[c["q"]].remove(c)
-        free[c["q"]], c["end"] = at + c["cost"], at + c["cost"] + c["lat"]
-        order.append(c)
-        for u in c["users"]:
-            u["left"] -= 1
-            if not u["left"]:
-                enter(u)
-    return order
+    way = [c["lat"] + c["cost"] for c in calls]
+    for i in reversed(range(n)):
+        for j, gap in before[i]:
+            way[j] = max(way[j], way[i] + gap + cost[j])
+    best = None
+    for turn in range(TURNS):
+        order, end = one_pass(before, after, [0.0] * n, way, [c["banks"] for c in calls])
+        total = max(end[i] + calls[i]["lat"] for i in range(n))
+        if best is None or total < best[0]:
+            best = (total, order)
+        way = one_pass(after, before, [c["lat"] for c in calls], end, [()] * n)[1]
+    return best[1]
 
 
 def rank_program(g, core, T, topo):
@@ -215,13 +231,10 @@ def rank_program(g, core, T, topo):
     line.update(g="g")
     iota("pi", T.pi[:, 0:1], [[0, 1]], 0, 1, small=False)
     iota("s64", T.stg[:, 64:72], [[0, 2], [2, 4]], 0)
-    iota("s0", T.stg[:, 0:64], [[16, 8], [1, 8]], 0)
-    iota("j16", T.j16[:], [[0, 9], [1, 16]], 0)
-    iota("s80", T.stg[:, 80:88], [[16, 8]], 7)
-    iota("di", T.di[:], [[16, 8]], 143, -1, small=False)
-    iota("jr", T.jr[:], [[1, 128]], 0)
     fix("Ez", T.Ez[:], 0.0, 258)
     sel("Ez", T.Ez[:, 3:515:4], [[1, 128]], A.not_equal, 1.0, 0, -1, 128)
+    iota("j16", T.j16[:], [[0, 9], [1, 16]], 0)
+    iota("s80", T.stg[:, 80:88], [[16, 8]], 7)
     iota("h8", T.h8[:], [[8, 8], [0, 8]], 8)
     iota("g7", T.g7[:], [[0, 8], [1, 8]], -7)
     iota("s88", T.stg[:, 88:104], [[16, 16]], 0)
@@ -241,18 +254,14 @@ def rank_program(g, core, T, topo):
     ts("p4 s64", "o64", T.offc[:, 64:72], T.stg[:, 64:72], ucol, A.add)
     ts("pf s80", "o80", T.offc[:, 80:88], T.stg[:, 80:88], i8col, A.add)
     ts("pf s88", "s88", T.stg[:, 88:104], T.stg[:, 88:104], icol, A.add)
-    cp("s0", "o0", T.offc[:, 0:64], T.stg[:, 0:64])
     cp("s72", "o72", T.offc[:, 72:80], T.stg[:, 72:80])
     cp("s88", "o88", T.offc[:, 88:104], T.stg[:, 88:104])
     for b in range(4):
         quant("Ez", "E%d" % b, "E", 128 * b, T.Ez[:, 3 - b:515 - b])
     quant("uin", "u", "u", 0, T.uin[:])
     quant("vin", "v", "v", 0, T.vin[:])
-    line.update(v="spread", s="side")
-    for n, a, o, key in [("u1c", 0, 64, "o64")] + [("uR", 128 * i, 8 * i, "o0") for i in range(8)]:
-        cp("u " + key, "q%s%d" % (n, a), words(n, a, a + 128), words("u", 0, 128).indirect(T.offc[:, o:o + 8]), picks(128))
-        act("u " + key, "s%s%d" % (n, a), T["s" + n][:, a:a + 128], T.su[:].indirect(T.offc[:, o:o + 8]), AF.Copy, picks(128))
-    del line["v"], line["s"]
+    cp("u o64", "qu1c", words("u1c", 0, 128), words("u", 0, 128).indirect(T.offc[:, 64:72]), picks(128))
+    act("u o64", "su1c", T.su1c[:], T.su[:].indirect(T.offc[:, 64:72]), AF.Copy, picks(128))
     iota("Kl2", T.Kl[:, 32:512], [[0, 480]], 0)
     kl = T.Kl[:, 0:32]
     iota("Kl", kl, [[0, 8], [-128, 2], [-128, 2]], 0)
@@ -260,13 +269,17 @@ def rank_program(g, core, T, topo):
     sel("Kl", kl, [[16, 8], [0, 4]], A.is_ge, 0.0, 15, -1, 32)
     quant("Kl Kl2", "L", "L", 0, T.Kl[:])
     iota("rs0", T.rs[:, 0:9:8], [[0, 2]], 0)
-    for j, (key, x, val) in enumerate([("Kb", T.Kb[:], 1), ("Kp", T.Kp[:], 2 * ka - 1)]):
-        k = (ka, kb)[j]
-        iota(keys("C", TRI[0] + TRI[1], k), half(T.Ct, k, 1024), [[0, 1024]], 0)
-        iota(key, x, [[0, 512]], val)
-        sel(key, x, [[-16, 8], [0, 64]], A.is_ge, 0.0, 0, 1, 512)
-        sel(key, x, [[16, 8], [0, 64]], A.is_ge, 0.0, 15, -1, 512)
-        quant(key, "K%d" % j, "K", 128 * j, x)
+    iota("Kb", T.Kb[:], [[0, 512]], 1)
+    sel("Kb", T.Kb[:], [[-16, 8], [0, 64]], A.is_ge, 0.0, 0, 1, 512)
+    sel("Kb", T.Kb[:], [[16, 8], [0, 64]], A.is_ge, 0.0, 15, -1, 512)
+    for j in range(4):
+        act("Kb", "Kp%d" % j, half(T.Kp, j), half(T.Kb, j), AF.Copy, scale=2.0 * ka - 1)
+    quant("Kb", "K0", "K", 0, T.Kb[:])
+    quant(keys("Kp", range(4)), "K1", "K", 128, T.Kp[:])
+    for k in (ka, kb):
+        iota(keys("C", TRI[0] + TRI[1], k), T.Ct[:, 1024 * k + 320:1024 * k + 1024], [[0, 704]], 0)
+        if k == ka:
+            iota("CW", T.CW[:], [[512, 8], [1, 128]], 0)
     iota("Or", T.Or[:], [[0, 256]], 0)
     iota("CG", T.CG[:], [[1, 8], [0, 128]], 0)
     line.clear()
@@ -287,27 +300,27 @@ def rank_program(g, core, T, topo):
     act("kq2", "c2", T.cor[:, 2:3], last, AF.Identity, small, bias=128.0)
     act("s88 kq2", "cr0", T.cr[:, 0:8], s8, AF.Identity, small, bias=last)
     act("s88 c2", "cr1", T.cr[:, 8:16], s8, AF.Identity, small, bias=T.cor[:, 2:3])
-    ts("di", "dj", T.dj[:], T.di[:], 4, A.arith_shift_right, 7, A.bitwise_and)
-    ts("dj", "df", T.df[:], T.dj[:], 512.0, A.mult)
-    for k in range(8):
-        act("jr df", "CW%d" % k, half(T.CW, k), T.jr[:], AF.Identity, bias=T.df[:, k:k + 1])
 
-    wall = " ".join(keys(n, r, k) for k in range(2) for n, r in [("W0", range(4)), ("Wa", range(1, 8)), ("Wb", range(1, 8))])
+    wall = keys("Wn", range(8), 0) + " " + keys("Wn", range(8), 1)
 
     def parts(k):
-        w0, o = keys("W0", range(4), k), 4096 * k
+        d = T["Dw%d" % k]
         for b in range(4):
             key, c = prod(["T%d E%d" % (k, b)], [("E", 128 * b, "T", 128 * k)], SIDE)
-            act(key, "W0%d%d" % (b, k), T.Wn[:, o + 128 * b:o + 128 * b + 128], (c, 128), AF.Copy)
-        for q in range(1, 8):
-            n, rot = 16 * q, "rot%d" % k
-            dma("y", rot, w0, "Wa%d%d" % (q, k), T.Wn[0:128 - n, o + 512 * q:o + 512 * q + 512], T.Wn[n:128, o:o + 512], 4500)
-            dma("y", rot, w0, "Wb%d%d" % (q, k), T.Wn[128 - n:128, o + 512 * q:o + 512 * q + 512], T.Wn[0:n, o:o + 512], 4500)
+            act(key, "W0%d%d" % (b, k), half(T.W0, 4 * k + b), (c, 128), AF.Copy)
+        for i in range(8):
+            dma("y", "pw%d" % k, keys("W0", range(4), k), "Dw%d%d" % (i, k), half(d, i, 512), T.W0[16 * i:16 * i + 16, 512 * k:512 * k + 512])
+        for i in range(8):
+            dma("y", "pr%d" % k, keys("Dw", range(8), k), "Wn%d%d" % (i, k), T.Wn[16 * i:16 * i + 16, 4096 * k:4096 * k + 4096], d[:], 4000)
 
     def likings(k):
-        for i in range(8):
-            key, c = prod(["T%d suR%d quR%d" % (k, 128 * i, 128 * i)], [("uR", 128 * i, "T", 128 * k)], SIDE)
-            act(key, "Sw%d%d" % (i, k), half(T.Sw, 8 * k + i), (c, 128), AF.Copy)
+        d = T["Ds%d" % k]
+        key, c = prod(["T%d qu1c su1c" % k], [("u1c", 0, "T", 128 * k)], SIDE)
+        act(key, "St%d" % k, half(T.S0, k), (c, 128), AF.Copy)
+        for i in range(4):
+            dma("y", "sw%d" % k, "St%d" % k, "Ds%d%d" % (i, k), half(d, i, 1024), T.S0[64 * (i % 2):64 * (i % 2) + 64, 128 * k:128 * k + 128])
+        for i in range(4):
+            dma("y", "sr%d" % k, keys("Ds", range(4), k), "Sw%d%d" % (i, k), T.Sw[i:128:4, 1024 * k:1024 * k + 1024], d[:], 3000)
 
     def state(t, k):
         Mn, got, m = "M%d" % t, {}, "M%d" % k + (" mq ms" if k == ka else "")
@@ -323,7 +336,7 @@ def rank_program(g, core, T, topo):
         n, a, o = str(k), 80 * k + 8, 192 * k
         run, top = T.pm[:, a:a + 64], T.pm[:, a + 63:a + 64]
         n1, (n2, sa, sb) = T.alt[:, 16 * k + 11:16 * k + 12], [T.sc[:, 4 * k + j:4 * k + j + 1] for j in range(3)]
-        pk, c = prod(["T%d qu1c0 su1c0" % k], [("T", 128 * k, "u1c", 0)])
+        pk, c = prod(["T%d qu1c su1c" % k], [("T", 128 * k, "u1c", 0)])
         for step in range(7):
             z, zn, zk, znk = T["Z%d" % (step % 2)], T["Z%d" % (1 - step % 2)], "%d%d" % (step % 2, k), "%d%d" % (1 - step % 2, k)
             src, sk = ((c, 64), pk) if step == 0 else (z[:, o + 2:o + 192:3], "S" + zk)
@@ -337,13 +350,13 @@ def rank_program(g, core, T, topo):
             if step == 0:
                 act("%s pm%d" % (pk, k), "S" + zk, z[:, o + 2:o + 192:3], src, AF.Copy, small)
             if step < 6:
-                ts("h8" + both, "r" + zk, z[:, o + 1:o + 192:3], T.h8[:], r8, A.is_equal, x1, A.mult)
-                ts("g7" + both, "c" + zk, z[:, o:o + 192:3], T.g7[:], r8, A.add, x1, A.is_equal)
-                scan("c%s r%s S%s d00 d01 d02" % (zk, zk, zk), "c%s r%s S%s" % (znk, znk, znk), zn[:, o:o + 192], T.d0[:], z[:, o:o + 192],
+                ts("h8" + both, "zr" + zk, z[:, o + 1:o + 192:3], T.h8[:], r8, A.is_equal, x1, A.mult)
+                ts("g7" + both, "zc" + zk, z[:, o:o + 192:3], T.g7[:], r8, A.add, x1, A.is_equal)
+                scan("zc%s zr%s S%s d00 d01 d02" % (zk, zk, zk), "S%s zc%s zr%s" % (znk, znk, znk), zn[:, o:o + 192], T.d0[:], z[:, o:o + 192],
                      A.mult, A.add, n=192)
         scan("zz " + keys("x", range(6), k) + " " + keys("r", range(6), k), "n1" + n, T.alt[:, 16 * k:16 * k + 12],
              T.cn[:, 16 * k:16 * k + 12], T.zz[:, 0:12], A.subtract, A.add, -20.0)
-        ts("n1" + n, "n2" + n, n2, n1, 0.5, A.mult, -4.0, A.add)
+        act("n1" + n, "n2" + n, n2, n1, AF.Identity, small, bias=-4.0, scale=0.5)
         scan(sk + " sa", "seg" + n, half(T.seg, k, 64), src, T.sa[:], A.min, A.add)
         tmp = half(T.tmp, k)
         tt("seg%d o72 mka" % k, "tmp" + n, tmp, half(T.seg, k, 64).indirect(T.offc[:, 72:80]), T.mka[:], A.mult, picks(128))
@@ -355,7 +368,7 @@ def rank_program(g, core, T, topo):
 
     def listing(k):
         n, e = str(k), slice(8 * k, 8 * k + 8)
-        sw, win = keys("Sw", range(8), k) + " l1" + n, half(T.Sw, k, 1024).indirect(T.l1[:, e])
+        sw, win = keys("Sw", range(4), k) + " l1" + n, half(T.Sw, k, 1024).indirect(T.l1[:, e])
         quant(keys("A", range(3), k), "qA" + n, "A", 128 * k, half(T.At, k, 512))
         key, c = prod(["qA%d L" % k], [("A", 128 * k, "L", 0)])
         tt("cl " + key, "l1f" + n, T.l1f[:, e], (c, 8), T.cl[:], A.add)
@@ -363,7 +376,7 @@ def rank_program(g, core, T, topo):
         act(sw, "Rr" + n, half(T.Rr, k), win, AF.Copy, picks(128))
         tt(sw + " cap", "Rm" + n, half(T.Rm, k), win, T.cap[:], A.max, picks(128))
         scan("rst Rm" + n, "Lt" + n, half(T.Lt, k), T.rst[:], half(T.Rm, k), A.max, A.min, n=128)
-        act(keys("CW", range(8)) + " l1" + n, "Pr" + n, half(T.Pr, k), T.CW[:].indirect(T.l1[:, e]), AF.Identity, picks(128), bias=4096.0 * k)
+        act("CW l1" + n, "Pr" + n, half(T.Pr, k), T.CW[:].indirect(T.l1[:, e]), AF.Identity, picks(128), bias=4096.0 * k)
 
     def mine(k, c):
         return T.Lt[:, 128 * k + 16 * c + 15:128 * k + 16 * c + 16]
@@ -380,9 +393,14 @@ def rank_program(g, core, T, topo):
                 if c != "d":
                     o = 1024 * k + 512 * i
                     slot, key = T.Ct[:, o + j:o + 64 * c:4], "C%d%d" % (c, k)
-                    ts(both, key, slot, T.Rr[:, 128 * k:128 * k + 16 * c], mine(k, c), A.is_lt, n=16 * c)
-                    o = 512 * k + 8 * c * (c - 1)
-                    act(key, "rs%d%d" % (c, k), T.junk[:, o:o + 16 * c], slot, AF.Copy, cycles(16 * c), accum_out=T.rs[:, 8 * k + c:8 * k + c + 1])
+                    row, o, acc = T.Rr[:, 128 * k:128 * k + 16 * c], 512 * k + 8 * c * (c - 1), T.rs[:, 8 * k + c:8 * k + c + 1]
+                    spare = T.junk[:, o:o + 16 * c]
+                    if c in ON_SCALAR[k != ka]:
+                        act(both, "j" + key, spare, row, AF.Sign, cycles(16 * c), bias=mine(k, c), scale=-1.0)
+                        act("j" + key, "%s rs%d%d" % (key, c, k), slot, spare, AF.Relu, cycles(16 * c), accum_out=acc)
+                    else:
+                        ts(both, key, slot, row, mine(k, c), A.is_lt, n=16 * c)
+                        act(key, "rs%d%d j%s" % (c, k, key), spare, slot, AF.Copy, cycles(16 * c), accum_out=acc)
             pack(2 * k + i, keys("C", TRI[i], k))
         scan("keep Cd" + n, "ds" + n, half(T.ds, k), T.keep[:], diag, A.mult, A.add)
         tt("ds%d cr%d" % (k, k), "u1" + n, T.u1[:, e], T.cr[:, e], ends(T.ds, k), A.subtract)
@@ -451,10 +469,8 @@ def rank_program(g, core, T, topo):
             else:
                 state(t - 1, k)
             matching(k)
-            line.update(s="side", t="sidet")
-            parts(k)
             likings(k)
-            line.clear()
+            parts(k)
             listing(k)
             inside(k)
         across()
@@ -485,8 +501,13 @@ def rank_program(g, core, T, topo):
         dma("s", "outs", "ys%d" % k, "", T.y[:, a:b], half(T.ys, k))
 
     cnt, seen = {}, {}
-    for c in issue_order(calls):
-        q, want = c["q"], {}
+    if ka not in ORDERS:
+        ORDERS[ka] = issue_order(calls)
+    for i, bank, holder in ORDERS[ka]:
+        c = calls[i]
+        q, want, c["bank"] = c["q"], {}, bank
+        if holder is not None:
+            c["deps"] += calls[holder]["uses"]
         for d in c["deps"]:
             if q != "a" and d is not c["sums"] and d["sem"] != "sent" and not (d["inc"] == 16 and d["sem"] == c["sem"]):
                 want[d["sem"]] = max(want.get(d["sem"], 0), d["count"] if d["inc"] == 1 else cnt[d["sem"]])

from concourse.bass import DstId, RemoteDMATransfer
from concourse.mybir import dt, AluOpType, ActivationFunctionType

N, C, L, R = 8, 256, 32, 3
F32, BF, I32, U16, Q8, U8 = "float32", "bfloat16", "int32", "uint16", "float8_e4m3fn_x4", "uint8"
PEN = 2.0 ** 92
KC = 128.0
LOW = -9e29
BIG = 2.0 ** 90
KL = 8192.0
NA = 4
ON_SCALAR = [(7, 6, 5, 4), ()]
TRI = [["d", 7, 6, 5], [4, 3, 2, 1]]
CYC, WAIT, DMA, FLY = 1.0, 140, 4000, (2800, 4400)
SLACK, GAP = 30, 2.0
TURNS = 4
ORDERS = {}
ANY, SIDE = list(range(8)), [6, 7]

SCRATCH = {}
for _n, _w, _d in [("xin", 1024, BF), ("uin", 512, BF), ("vin", 512, BF), ("X", 1024, BF), ("Bt", 1024, BF),
                   ("Ez", 516, BF), ("Kb", 512, BF), ("Kp", 512, BF), ("Kl", 512, BF), ("At", 1024, BF), ("Ct", 3072, BF),
                   ("Wn", 8192, BF), ("Sw", 2048, F32), ("CW", 1024, F32), ("CG", 1024, F32), ("Rb", 1024, F32),
                   ("pi", 4, I32), ("pt", 4, I32), ("pf", 8, F32), ("stg", 104, F32), ("offc", 104, U16),
                   ("h8", 64, F32), ("g7", 64, F32), ("neg", 64, F32), ("d0", 192, F32), ("sa", 64, F32), ("zz", 16, F32),
                   ("j16", 144, F32), ("W0", 1024, BF), ("S0", 256, F32),
                   ("ab", 144, F32), ("nq", 144, F32), ("cap", 128, F32), ("kq", 384, F32), ("rst", 128, F32),
                   ("sgj", 128, F32), ("keep", 128, BF), ("mka", 128, BF), ("cl", 8, F32), ("cr", 16, F32), ("cor", 4, F32),
                   ("Z0", 384, F32), ("Z1", 384, F32), ("pm", 160, F32), ("cn", 32, F32), ("jx", 128, BF), ("jh", 128, BF),
                   ("seg", 128, F32), ("tmp", 256, BF), ("alt", 32, F32), ("sc", 8, F32),
                   ("l1f", 16, F32), ("l1", 16, U16), ("Rr", 256, F32), ("Rm", 256, F32), ("Lt", 256, F32), ("Pr", 256, F32),
                   ("sn", 1024, BF), ("junk", 2048, BF), ("rs", 24, F32), ("ds", 256, BF), ("u1", 16, F32),
                   ("ex", 256, F32), ("rkf", 8, F32), ("rk", 16, U16), ("Or", 256, F32), ("ex2", 256, F32), ("l2", 16, U16),
                   ("oi", 256, I32), ("oj", 256, I32), ("OL", 512, F32), ("ys", 256, F32)]:
    SCRATCH[_n] = ("sbuf", [128, _w], _d)
for _n, _w in [("u", 128), ("u1c", 128), ("v", 128), ("W", 512), ("T", 256), ("E", 512), ("K", 256),
               ("L", 128), ("A", 256), ("C", 768)] + [("B%d" % _t, 256) for _t in range(R)] + [("M%d" % _t, 256) for _t in range(R)]:
    SCRATCH["q" + _n] = ("sbuf", [128, _w], Q8)
    SCRATCH["s" + _n] = ("sbuf", [128, _w], U8)
for _b in range(8):
    SCRATCH["ps%d" % _b] = ("psum", [128, 512], F32)
for _k in range(2):
    SCRATCH["Dw%d" % _k] = ("dram", [16, 4096], BF)
    SCRATCH["Ds%d" % _k] = ("dram", [8, 4096], F32)

SEMAPHORES = (["cv", "cs", "ct", "cg", "ldx0", "ldx1", "ldu", "ldw", "ldv", "outs", "sent"]
              + [_n + str(_k) for _n in ("pw", "pr", "sw", "sr") for _k in range(2)]
              + ["arr%d%d" % (_t, _k) for _t in range(R) for _k in range(2)])


def deal(T, topo, s, k):
    src = T.cores[s]
    others = [d for d in [(s + i) % N for i in range(1, N)] if d // 4 == k]
    far = [d for d in others if topo.chip(T.cores[d]) != topo.chip(src)]
    eng = topo.engines(src, T.cores[far[0]])
    each = len(eng) // len(far)
    out = [(d, eng[each * i:each * i + each]) for i, d in enumerate(far)]
    return out + [(d, [e for e in topo.engines(src, T.cores[d]) if e not in eng]) for d in others if d not in far]


def issue_order(calls):
    n, cost = len(calls), [c["cost"] for c in calls]
    before = [[(d["n"], 0 if d is c["sums"] else d["lat"] + WAIT) for d in c["deps"]] for c in calls]
    after = [[] for c in calls]
    for i in range(n):
        for j, gap in before[i]:
            after[j].append((i, gap))

    def one_pass(first, then, at, way, banks):
        ready, free, held, order = {q: [] for q in "vstgya"}, {q: 0.0 for q in "vstgya"}, [None] * 8, []
        left, end = [len(x) for x in first], [None] * n
        for i in range(n):
            if not left[i]:
                ready[calls[i]["q"]].append(i)
        while len(order) < n:
            best, times = None, [0.0] * 8
            for b in range(8):
                if held[b] is not None:
                    ends = [end[u["n"]] for u in calls[held[b]]["uses"]]
                    times[b] = None if None in ends else max(ends) + WAIT
            for q, cs in ready.items():
                can = []
                for i in cs:
                    open_ = [(times[b], b) for b in banks[i] if times[b] is not None]
                    if open_ or not banks[i]:
                        can.append((max(at[i], free[q], min(open_)[0] if open_ else 0.0), i, min(open_)[1] if open_ else None))
                if can:
                    now = min(x[0] for x in can)
                    pick = max((x for x in can if x[0] == now), key=lambda x: way[x[1]])
                    soon = [x for x in can if now + cost[pick[1]] - x[0] > SLACK + GAP * (x[0] - now) and way[x[1]] > way[pick[1]]]
                    if soon:
                        pick = max(soon, key=lambda x: way[x[1]])
                    if best is None or pick[0] < best[0]:
                        best = pick
            start, i, b = best
            order.append((i, b, None if b is None else held[b]))
            if b is not None:
                held[b] = i
            ready[calls[i]["q"]].remove(i)
            free[calls[i]["q"]] = end[i] = start + cost[i]
            for j, gap in then[i]:
                at[j], left[j] = max(at[j], end[i] + gap), left[j] - 1
                if not left[j]:
                    ready[calls[j]["q"]].append(j)
        return order, end

    way = [c["lat"] + c["cost"] for c in calls]
    for i in reversed(range(n)):
        for j, gap in before[i]:
            way[j] = max(way[j], way[i] + gap + cost[j])
    best = None
    for turn in range(TURNS):
        order, end = one_pass(before, after, [0.0] * n, way, [c["banks"] for c in calls])
        total = max(end[i] + calls[i]["lat"] for i in range(n))
        if best is None or total < best[0]:
            best = (total, order)
        way = one_pass(after, before, [c["lat"] for c in calls], end, [()] * n)[1]
    return best[1]


def rank_program(g, core, T, topo):
    rank = T.rank_of(core)
    if rank is None:
        return
    A, AF = AluOpType, ActivationFunctionType
    Q = {"v": g.vector, "s": g.scalar, "t": g.tensor, "g": g, "y": g.sync}
    V, S, P = g.vector, g.scalar, g.tensor
    calls, wr, rd = [], {}, {}
    line, tail = {}, {}
    ka, kb = rank // 4, 1 - rank // 4

    def op(q, reads, writes, fn, cost, lat=0.0, sem=None, inc=1, banks=(), sums=None):
        reads, writes = reads.split(), writes.split()
        deps = [wr[k] for k in reads + writes if k in wr] + [d for k in writes for d in rd.get(k, [])]
        if line.get(q) in tail and tail[line[q]] not in deps:
            sums = tail[line[q]]
            deps.append(sums)
        c = {"q": q, "fn": fn, "cost": cost, "lat": lat, "sem": sem or "c" + q, "inc": inc, "banks": banks, "sums": sums,
             "deps": list({d["n"]: d for d in deps}.values()), "n": len(calls), "way": 0.0, "users": [], "uses": []}
        for k in reads:
            rd.setdefault(k, []).append(c)
            if k in wr and "start" in wr[k]:
                wr[k]["start"]["uses"].append(c)
        for k in writes:
            wr[k], rd[k] = c, []
        calls.append(c)
        if q in line:
            tail[line[q]] = c
        return c

    def ap(x):
        return T["ps%d" % x[0]["bank"]][:, 0:x[1]] if isinstance(x, tuple) else x

    def cycles(n):
        return max(64, n) * CYC

    def picks(n, per=1.6):
        return 55 + n * per * CYC

    def dma(q, sem, reads, writes, out, in_, lat=DMA):
        op(q, reads, writes, lambda: Q[q].dma_start(out, in_), 50, lat, sem, 16)

    def ts(r, w, out, in0, s1, o0, s2=None, o1=None, n=64):
        more = () if o1 is None else (o1,)
        op("v", r, w, lambda: V.tensor_scalar(out, ap(in0), s1, s2, o0, *more), cycles(n))

    def tt(r, w, out, in0, in1, o, cost=cycles(64)):
        op("v", r, w, lambda: V.tensor_tensor(out, ap(in0), in1, o), cost)

    def cp(r, w, out, in_, cost=cycles(64)):
        op("v", r, w, lambda: V.tensor_copy(out, in_), cost)

    def scan(r, w, out, d0, d1, o0, o1, first=0.0, n=64):
        op("v", r, w, lambda: V.tensor_tensor_scan(out, ap(d0), d1, first, o0, o1), cycles(n))

    def act(r, w, out, in_, f, cost=cycles(128), **kw):
        op("s", r, w, lambda: S.activation(out, ap(in_), f, **kw), cost + (20 if "accum_out" in kw else 0))

    def fix(w, out, val, n=64):
        op("v", "", w, lambda: V.memset(out, val), cycles(n))

    def quant(r, w, n, a, in_, cols=128):
        op("v", r, w, lambda: V.quantize_mx(T["q" + n][:, a:a + cols], T["s" + n][:, a:a + cols], in_), 15 + 1.1 * cols)

    def prod(r, terms, banks=ANY):
        key, first, last = "p%d" % len(calls), None, None
        for i, (l, la, m, ma) in enumerate(terms):
            def fn(i=i, l=l, la=la, m=m, ma=ma):
                return P.matmul_mx(ap((wr0[0], 128)), T["q" + l][:, la:la + 128], T["s" + l][:, la:la + 128],
                                   T["q" + m][:, ma:ma + 128], T["s" + m][:, ma:ma + 128], i == 0, i == len(terms) - 1)
            last = op("t", r[i], key, fn, 90, 50, banks=() if i else banks, sums=last)
            first = first or last
            last["start"] = first
        wr0 = [first]
        return key, first

    def iota(w, out, pat, base, cm=0, small=True):
        n = 1
        for step, count in pat:
            n *= count
        kw = {"allow_small_or_imprecise_dtypes": True} if small else {}
        op("g", "", w, lambda: g.iota(out, pat, base, cm, **kw), 160 + 2 * CYC * n)

    def sel(k, out, pat, cmp, fill, base, cm, n):
        op("g", k, k, lambda: g.affine_select(out, out, pat, cmp, fill, base, cm), 210 + 2 * CYC * n)

    def words(n, a, b):
        return T["q" + n][:, a:b].bitcast(dt.uint32)

    def bytes_of(n, a, b):
        return T["q" + n][:, a:b].bitcast(dt.uint8)

    def keys(pre, items, post=""):
        return " ".join("%s%s%s" % (pre, i, post) for i in items)

    def half(x, k, w=128):
        return x[:, w * k:w * k + w]

    def ends(x, k):
        return x[:, 128 * k + 15:128 * k + 128:16]

    dma("s", "ldu", "", "uin", T.uin[:], T.u[:], 2000)
    for k in (ka, kb):
        dma("y", "ldx%d" % k, "", "xin%d" % k, half(T.xin, k, 512), half(T.x, k, 512), 2200 + 400 * (k == kb))
    dma("y", "ldw", "xin0 xin1", "qW", bytes_of("W", 0, 512), T.wc[:])
    dma("y", "ldw", "xin0 xin1", "sW", T.sW[:], T.ws[:])
    dma("y", "ldv", "xin0 xin1", "vin", T.vin[:], T.v[:])

    icol, i8col, ucol = T.pf[:, 0:1], T.pf[:, 1:2], T.pf[:, 4:5]
    small = cycles(64)
    line.update(g="g")
    iota("pi", T.pi[:, 0:1], [[0, 1]], 0, 1, small=False)
    iota("s64", T.stg[:, 64:72], [[0, 2], [2, 4]], 0)
    fix("Ez", T.Ez[:], 0.0, 258)
    sel("Ez", T.Ez[:, 3:515:4], [[1, 128]], A.not_equal, 1.0, 0, -1, 128)
    iota("j16", T.j16[:], [[0, 9], [1, 16]], 0)
    iota("s80", T.stg[:, 80:88], [[16, 8]], 7)
    iota("h8", T.h8[:], [[8, 8], [0, 8]], 8)
    iota("g7", T.g7[:], [[0, 8], [1, 8]], -7)
    iota("s88", T.stg[:, 88:104], [[16, 16]], 0)
    iota("s72", T.stg[:, 72:80], [[8, 8]], 7)
    fix("neg", T.neg[:], LOW)
    fix("pm0 pm1", T.pm[:], LOW, 160)
    fix("sa", T.sa[:], 0.0)
    fix("zz", T.zz[:], 0.0)
    fix("A0 A1", T.At[:, 0:1024:4], 0.0, 128)
    for j, m in enumerate((15, 8, 7)):
        ts("pi", "pt%d" % j, T.pt[:, j:j + 1], T.pi[:, 0:1], m, A.bitwise_and)
    for j, val in enumerate((0.0, KC, -PEN)):
        fix("d0%d" % j, T.d0[:, j:192:3], val)
    cp("pt0 pt1 pt2", "pf", T.pf[:, 0:3], T.pt[:, 0:3])
    ts("pf", "p3", T.pf[:, 3:4], T.pf[:, 2:3], 16.0, A.mult)
    ts("pf p3", "p4", ucol, i8col, 0.125, A.mult, T.pf[:, 3:4], A.add)
    ts("p4 s64", "o64", T.offc[:, 64:72], T.stg[:, 64:72], ucol, A.add)
    ts("pf s80", "o80", T.offc[:, 80:88], T.stg[:, 80:88], i8col, A.add)
    ts("pf s88", "s88", T.stg[:, 88:104], T.stg[:, 88:104], icol, A.add)
    cp("s72", "o72", T.offc[:, 72:80], T.stg[:, 72:80])
    cp("s88", "o88", T.offc[:, 88:104], T.stg[:, 88:104])
    for b in range(4):
        quant("Ez", "E%d" % b, "E", 128 * b, T.Ez[:, 3 - b:515 - b])
    quant("uin", "u", "u", 0, T.uin[:])
    quant("vin", "v", "v", 0, T.vin[:])
    cp("u o64", "qu1c", words("u1c", 0, 128), words("u", 0, 128).indirect(T.offc[:, 64:72]), picks(128))
    act("u o64", "su1c", T.su1c[:], T.su[:].indirect(T.offc[:, 64:72]), AF.Copy, picks(128))
    iota("Kl2", T.Kl[:, 32:512], [[0, 480]], 0)
    kl = T.Kl[:, 0:32]
    iota("Kl", kl, [[0, 8], [-128, 2], [-128, 2]], 0)
    sel("Kl", kl, [[-16, 8], [0, 4]], A.is_ge, 0.0, 0, 1, 32)
    sel("Kl", kl, [[16, 8], [0, 4]], A.is_ge, 0.0, 15, -1, 32)
    quant("Kl Kl2", "L", "L", 0, T.Kl[:])
    iota("rs0", T.rs[:, 0:9:8], [[0, 2]], 0)
    iota("Kb", T.Kb[:], [[0, 512]], 1)
    sel("Kb", T.Kb[:], [[-16, 8], [0, 64]], A.is_ge, 0.0, 0, 1, 512)
    sel("Kb", T.Kb[:], [[16, 8], [0, 64]], A.is_ge, 0.0, 15, -1, 512)
    for j in range(4):
        act("Kb", "Kp%d" % j, half(T.Kp, j), half(T.Kb, j), AF.Copy, scale=2.0 * ka - 1)
    quant("Kb", "K0", "K", 0, T.Kb[:])
    quant(keys("Kp", range(4)), "K1", "K", 128, T.Kp[:])
    for k in (ka, kb):
        iota(keys("C", TRI[0] + TRI[1], k), T.Ct[:, 1024 * k + 320:1024 * k + 1024], [[0, 704]], 0)
        if k == ka:
            iota("CW", T.CW[:], [[512, 8], [1, 128]], 0)
    iota("Or", T.Or[:], [[0, 256]], 0)
    iota("CG", T.CG[:], [[1, 8], [0, 128]], 0)
    line.clear()
    s8, last = T.stg[:, 88:96], T.kq[:, 271:272]
    act("h8 sa", "sa", T.sa[:, 7:64:8], T.h8[:, 7:64:8], AF.Identity, small, bias=KC * PEN, scale=PEN)
    act("j16 pf", "ab", T.ab[:], T.j16[:], AF.Abs, bias=icol, scale=-1.0)
    act("j16", "sgj", T.sgj[:], T.j16[:, 0:128], AF.Sign)
    act("ab", "nq", T.nq[:], T.ab[:], AF.Sign)
    act("sgj", "rst", T.rst[:], T.sgj[:], AF.Identity, bias=BIG, scale=-2 * BIG)
    act("sgj", "keep", T.keep[:], T.sgj[:], AF.Copy)
    act("nq", "mka", T.mka[:], T.nq[:, 0:128], AF.Identity, bias=1.0 / PEN, scale=-1.0 / PEN)
    act("nq", "cap", T.cap[:], T.nq[:, 0:128], AF.Identity, bias=-BIG, scale=2 * BIG)
    for j in range(3):
        act("nq", "kq%d" % j, half(T.kq, j), T.nq[:, 1:129], AF.Identity, bias=17 * KL, scale=-18 * KL)
    act("s88", "cl", T.cl[:], s8, AF.Identity, small, bias=896.0)
    act("kq2 pf", "c1", T.cor[:, 1:2], icol, AF.Identity, small, bias=last, scale=KL)
    act("c1", "cor", T.cor[:, 0:1], T.cor[:, 1:2], AF.Identity, small, bias=15 * KL, scale=-1.0)
    act("kq2", "c2", T.cor[:, 2:3], last, AF.Identity, small, bias=128.0)
    act("s88 kq2", "cr0", T.cr[:, 0:8], s8, AF.Identity, small, bias=last)
    act("s88 c2", "cr1", T.cr[:, 8:16], s8, AF.Identity, small, bias=T.cor[:, 2:3])

    wall = keys("Wn", range(8), 0) + " " + keys("Wn", range(8), 1)

    def parts(k):
        d = T["Dw%d" % k]
        for b in range(4):
            key, c = prod(["T%d E%d" % (k, b)], [("E", 128 * b, "T", 128 * k)], SIDE)
            act(key, "W0%d%d" % (b, k), half(T.W0, 4 * k + b), (c, 128), AF.Copy)
        for i in range(8):
            dma("y", "pw%d" % k, keys("W0", range(4), k), "Dw%d%d" % (i, k), half(d, i, 512), T.W0[16 * i:16 * i + 16, 512 * k:512 * k + 512])
        for i in range(8):
            dma("y", "pr%d" % k, keys("Dw", range(8), k), "Wn%d%d" % (i, k), T.Wn[16 * i:16 * i + 16, 4096 * k:4096 * k + 4096], d[:], 4000)

    def likings(k):
        d = T["Ds%d" % k]
        key, c = prod(["T%d qu1c su1c" % k], [("u1c", 0, "T", 128 * k)], SIDE)
        act(key, "St%d" % k, half(T.S0, k), (c, 128), AF.Copy)
        for i in range(4):
            dma("y", "sw%d" % k, "St%d" % k, "Ds%d%d" % (i, k), half(d, i, 1024), T.S0[64 * (i % 2):64 * (i % 2) + 64, 128 * k:128 * k + 128])
        for i in range(4):
            dma("y", "sr%d" % k, keys("Ds", range(4), k), "Sw%d%d" % (i, k), T.Sw[i:128:4, 1024 * k:1024 * k + 1024], d[:], 3000)

    def state(t, k):
        Mn, got, m = "M%d" % t, {}, "M%d" % k + (" mq ms" if k == ka else "")
        for b in range(4):
            key, c = prod([m + " qW sW"], [("W", 128 * b, Mn, 128 * k)])
            act(key, "R%d%d" % (b, k), half(T.Rb, 2 * b + k), (c, 128), AF.Relu, scale=0.03125)
        for b in range(4):
            key, c = prod([m + " E%d" % b], [("E", 128 * b, Mn, 128 * k)])
            tt(key + " R%d%d" % (b, k), "X%d%d" % (b, k), T.X[:, 512 * k + b:512 * k + 512:4], (c, 128), half(T.Rb, 2 * b + k), A.add, cycles(128))
        quant(keys("X", range(4), k), "T%d" % k, "T", 128 * k, half(T.X, k, 512))

    def matching(k):
        n, a, o = str(k), 80 * k + 8, 192 * k
        run, top = T.pm[:, a:a + 64], T.pm[:, a + 63:a + 64]
        n1, (n2, sa, sb) = T.alt[:, 16 * k + 11:16 * k + 12], [T.sc[:, 4 * k + j:4 * k + j + 1] for j in range(3)]
        pk, c = prod(["T%d qu1c su1c" % k], [("T", 128 * k, "u1c", 0)])
        for step in range(7):
            z, zn, zk, znk = T["Z%d" % (step % 2)], T["Z%d" % (1 - step % 2)], "%d%d" % (step % 2, k), "%d%d" % (1 - step % 2, k)
            src, sk = ((c, 64), pk) if step == 0 else (z[:, o + 2:o + 192:3], "S" + zk)
            x1, r8 = [T.cn[:, 16 * k + 2 * step + j:16 * k + 2 * step + j + 1] for j in range(2)]
            xk, rk = "x%d%d" % (step, k), "r%d%d" % (step, k)
            both = " %s %s" % (xk, rk)
            scan(sk + " neg", "pm" + n, run, src, T.neg[:], A.max, A.max, LOW)
            act("pm%d o80" % k, rk + " jh" + n, half(T.jh, k, 64), T.pm[:, a - 8:a + 56].indirect(T.offc[:, 80:84]), AF.Sign, picks(64),
                bias=top, scale=-1.0, accum_out=r8)
            act("pm" + n, xk + " jx" + n, half(T.jx, k, 64), T.pm[:, a - 1:a + 63], AF.Sign, small, bias=top, scale=-1.0, accum_out=x1)
            if step == 0:
                act("%s pm%d" % (pk, k), "S" + zk, z[:, o + 2:o + 192:3], src, AF.Copy, small)
            if step < 6:
                ts("h8" + both, "zr" + zk, z[:, o + 1:o + 192:3], T.h8[:], r8, A.is_equal, x1, A.mult)
                ts("g7" + both, "zc" + zk, z[:, o:o + 192:3], T.g7[:], r8, A.add, x1, A.is_equal)
                scan("zc%s zr%s S%s d00 d01 d02" % (zk, zk, zk), "S%s zc%s zr%s" % (znk, znk, znk), zn[:, o:o + 192], T.d0[:], z[:, o:o + 192],
                     A.mult, A.add, n=192)
        scan("zz " + keys("x", range(6), k) + " " + keys("r", range(6), k), "n1" + n, T.alt[:, 16 * k:16 * k + 12],
             T.cn[:, 16 * k:16 * k + 12], T.zz[:, 0:12], A.subtract, A.add, -20.0)
        act("n1" + n, "n2" + n, n2, n1, AF.Identity, small, bias=-4.0, scale=0.5)
        scan(sk + " sa", "seg" + n, half(T.seg, k, 64), src, T.sa[:], A.min, A.add)
        tmp = half(T.tmp, k)
        tt("seg%d o72 mka" % k, "tmp" + n, tmp, half(T.seg, k, 64).indirect(T.offc[:, 72:80]), T.mka[:], A.mult, picks(128))
        ts("n1" + n + both, "sa" + n, sa, x1, r8, A.subtract, n1, A.subtract)
        ts("n2" + n + both, "sb" + n, sb, r8, x1, A.subtract, n2, A.add)
        ts("tmp%d A%d" % (k, k), "A0" + n, T.At[:, 512 * k + 1:512 * k + 512:4], tmp, 8.0, A.min)
        ts("tmp%d sa%d A%d" % (k, k, k), "A1" + n, T.At[:, 512 * k + 2:512 * k + 512:4], tmp, 8.0, A.is_ge, sa, A.mult)
        ts("tmp%d sb%d A%d %s" % (k, k, k, rk), "A2" + n, T.At[:, 512 * k + 3:512 * k + 512:4], tmp, r8, A.is_equal, sb, A.mult)

    def listing(k):
        n, e = str(k), slice(8 * k, 8 * k + 8)
        sw, win = keys("Sw", range(4), k) + " l1" + n, half(T.Sw, k, 1024).indirect(T.l1[:, e])
        quant(keys("A", range(3), k), "qA" + n, "A", 128 * k, half(T.At, k, 512))
        key, c = prod(["qA%d L" % k], [("A", 128 * k, "L", 0)])
        tt("cl " + key, "l1f" + n, T.l1f[:, e], (c, 8), T.cl[:], A.add)
        cp("l1f" + n, "l1" + n, T.l1[:, e], T.l1f[:, e])
        act(sw, "Rr" + n, half(T.Rr, k), win, AF.Copy, picks(128))
        tt(sw + " cap", "Rm" + n, half(T.Rm, k), win, T.cap[:], A.max, picks(128))
        scan("rst Rm" + n, "Lt" + n, half(T.Lt, k), T.rst[:], half(T.Rm, k), A.max, A.min, n=128)
        act("CW l1" + n, "Pr" + n, half(T.Pr, k), T.CW[:].indirect(T.l1[:, e]), AF.Identity, picks(128), bias=4096.0 * k)

    def mine(k, c):
        return T.Lt[:, 128 * k + 16 * c + 15:128 * k + 16 * c + 16]

    def pack(i, r):
        quant(r, "c%d" % i, "C", 128 * i, half(T.Ct, i, 512))

    def inside(k):
        n, e, both = str(k), slice(8 * k, 8 * k + 8), "Rr%d Lt%d" % (k, k)
        diag = T.Ct[:, 1024 * k:1024 * k + 512:4]
        tt(both, "Cd" + n, diag, half(T.Lt, k), half(T.Rr, k), A.is_ge, cycles(256))
        for i in range(2):
            for j, c in enumerate(TRI[i]):
                if c != "d":
                    o = 1024 * k + 512 * i
                    slot, key = T.Ct[:, o + j:o + 64 * c:4], "C%d%d" % (c, k)
                    row, o, acc = T.Rr[:, 128 * k:128 * k + 16 * c], 512 * k + 8 * c * (c - 1), T.rs[:, 8 * k + c:8 * k + c + 1]
                    spare = T.junk[:, o:o + 16 * c]
                    if c in ON_SCALAR[k != ka]:
                        act(both, "j" + key, spare, row, AF.Sign, cycles(16 * c), bias=mine(k, c), scale=-1.0)
                        act("j" + key, "%s rs%d%d" % (key, c, k), slot, spare, AF.Relu, cycles(16 * c), accum_out=acc)
                    else:
                        ts(both, key, slot, row, mine(k, c), A.is_lt, n=16 * c)
                        act(key, "rs%d%d j%s" % (c, k, key), spare, slot, AF.Copy, cycles(16 * c), accum_out=acc)
            pack(2 * k + i, keys("C", TRI[i], k))
        scan("keep Cd" + n, "ds" + n, half(T.ds, k), T.keep[:], diag, A.mult, A.add)
        tt("ds%d cr%d" % (k, k), "u1" + n, T.u1[:, e], T.cr[:, e], ends(T.ds, k), A.subtract)
        tt("u1%d rs0 " % k + keys("rs", range(1, 8), k), "kq" + n, ends(T.kq, k), T.u1[:, e], T.rs[:, e], A.subtract)

    def across():
        both = "Rr%d Lt%d" % (kb, ka)
        for c in range(8):
            slot, key, acc = T.Ct[:, 2048 + 512 * (c // 4) + c % 4:2560 + 512 * (c // 4):4], "Cx%d" % c, T.rs[:, 16 + c:17 + c]
            if c >= 8 - NA:
                act(both, "sn%d" % c, half(T.sn, c), half(T.Rr, kb), AF.Sign, bias=mine(ka, c), scale=-1.0)
                act("sn%d" % c, "%s rq%d" % (key, c), slot, half(T.sn, c), AF.Relu, scale=2.0 * ka - 1, accum_out=acc)
            else:
                ts(both, key, slot, half(T.Rr, kb), mine(ka, c), A.is_lt if ka else A.is_gt, n=128)
                act(key, "rq%d" % c, half(T.junk, 8 + c), slot, AF.Copy, accum_out=acc)
        for i in range(2):
            pack(4 + i, keys("Cx", range(4 * i, 4 * i + 4)))

    def ranks(k):
        tiles, e = [2 * k, 2 * k + 1] + ([4, 5] if k == kb else []), slice(8 * k, 8 * k + 8)
        tiles = tiles[2:] + tiles[:2]
        key, c = prod(["K0 K1 c%d" % i for i in tiles], [("K", 128 * (i // 4), "C", 128 * i) for i in tiles])
        scan("kq%d %s" % (k, key), "ex%d" % k, half(T.ex, k), (c, 128), half(T.kq, k), A.min, A.add, 17 * KL, n=128)
        if k == ka:
            tt("ex%d " % k + keys("rq", range(8)), "rkf", T.rkf[:], ends(T.ex, k), T.rs[:, 16:24], A.subtract if ka else A.add)
        ts("rkf cor ex%d" % k if k == ka else "cor ex%d" % k, "rk%d" % k, T.rk[:, e], T.rkf[:] if k == ka else ends(T.ex, k), T.cor[:, 0:1], A.add)
        cp("Pr%d rk%d" % (k, k), "Or", T.Or[:].indirect(T.rk[:, e]), half(T.Pr, k), picks(128, 3.8))

    def order(k):
        scan("kq2 Or", "ex2%d" % k, half(T.ex2, k), half(T.Or, k), half(T.kq, 2), A.min, A.add, 17 * KL, n=128)
        ts("ex2%d cor" % k, "l2%d" % k, T.l2[:, 8 * k:8 * k + 8], ends(T.ex2, k), T.cor[:, 0:1], A.add)

    def send(t, k):
        Bn, Mn = "B%d" % t, "M%d" % t
        for b in range(4):
            win = T.Wn[:, 128 * b:128 * b + 7808].indirect(T.l2[:, 8 * k:8 * k + 8])
            out = T.Bt[:, 512 * k + b:512 * k + 512:4]
            if b % 2:
                act(wall + " l2%d" % k, "B%d%d" % (b, k), out, win, AF.Copy, picks(128))
            else:
                cp(wall + " l2%d" % k, "B%d%d" % (b, k), out, win, picks(128))
        quant(keys("B", range(4), k), "qB%d" % k, Bn, 128 * k, half(T.Bt, k, 512))
        for codes in (True, False):
            trs = []
            for d, eng in deal(T, topo, rank, k):
                rid, pid = topo.addr(T.cores[d])[0:2]
                if codes:
                    s_, d_ = bytes_of(Bn, L * d, L * d + L), bytes_of(Mn, L * rank, L * rank + L)
                else:
                    s_, d_ = T["s" + Bn][:, L * d:L * d + L], T["s" + Mn][:, L * rank:L * rank + L]
                trs.append(RemoteDMATransfer(dst_ids=[DstId(rid=rid, pnc=pid)], dma_engine_mask=sum(1 << e for e in eng),
                                             remote_sem=T.sem["arr%d%d" % (t, ka)], src=s_, dst=d_))
            op("g", "qB%d" % k, "gone%d%d%d" % (t, k, codes), lambda trs=trs: g.remote_dma_fused(trs, local_sem=T.sem.sent), 150, 0, "sent",
               sum(len(eng) for d, eng in deal(T, topo, rank, k)))
        got = sum(2 * len(e) for s in range(4 * k, 4 * k + 4) if s != rank for d, e in deal(T, topo, s, ka) if d == rank)
        op("a", keys("gone%d%d" % (t, k), (0, 1)), "M%d" % k, None, 0, FLY[k != ka], "arr%d%d" % (t, k), got)
        if k == kb:
            own = T.offc[:, 88:90]
            cp("o88 qB%d" % ka, "mq", words(Mn, L * rank, L * rank + L), words(Bn, L * rank, L * rank + L).indirect(own), picks(32))
            cp("o88 qB%d" % ka, "ms", T["s" + Mn][:, L * rank:L * rank + L], T["s" + Bn][:, L * rank:L * rank + L].indirect(own), picks(32))

    for t in range(R):
        for k in (ka, kb):
            if t == 0:
                quant("xin%d" % k, "T%d" % k, "T", 128 * k, half(T.xin, k, 512))
            else:
                state(t - 1, k)
            matching(k)
            likings(k)
            parts(k)
            listing(k)
            inside(k)
        across()
        for k in (ka, kb):
            ranks(k)
        for k in (ka, kb):
            order(k)
        line.update(v="sendv%d" % t, s="sends%d" % t, g="g")
        for k in (ka, kb):
            send(t, k)
        line.clear()

    cp("Or", "oi", T.oi[:], T.Or[:], cycles(256))
    for k in range(2):
        act("CG l1%d" % k, "OLg%d" % k, half(T.OL, 2 + k), T.CG[:].indirect(T.l1[:, 8 * k:8 * k + 8]), AF.Copy, picks(128))
    ts("oi", "oj", T.oj[:], T.oi[:], 127, A.bitwise_and, n=256)
    ts("oi", "oi", T.oi[:], T.oi[:], 5, A.arith_shift_right, 128, A.bitwise_and, n=256)
    tt("oi oj", "OLo", T.OL[:, 0:256], T.oi[:], T.oj[:], A.add, cycles(512))
    dma("y", "outs", "OLo OLg0 OLg1", "", T.ol[:], T.OL[0:128:16, :])
    for k in (ka, kb):
        a, b = 128 * k, 128 * k + 128
        state(R - 1, k)
        key, c = prod(["T%d v" % k], [("v", 0, "T", a)])
        dma("y", "outs", "T%d" % k, "", T.oc[:, 4 * a:4 * b], bytes_of("T", a, b))
        for i in range(4):
            dma("y", "outs", "T%d" % k, "", T.osc[4 * i:4 * i + 4, a:b], T.sT[32 * i:32 * i + 4, a:b])
        act(key, "ys%d" % k, half(T.ys, k), (c, 128), AF.Copy)
        dma("s", "outs", "ys%d" % k, "", T.y[:, a:b], half(T.ys, k))

    cnt, seen = {}, {}
    if ka not in ORDERS:
        ORDERS[ka] = issue_order(calls)
    for i, bank, holder in ORDERS[ka]:
        c = calls[i]
        q, want, c["bank"] = c["q"], {}, bank
        if holder is not None:
            c["deps"] += calls[holder]["uses"]
        for d in c["deps"]:
            if q != "a" and d is not c["sums"] and d["sem"] != "sent" and not (d["inc"] == 16 and d["sem"] == c["sem"]):
                want[d["sem"]] = max(want.get(d["sem"], 0), d["count"] if d["inc"] == 1 else cnt[d["sem"]])
        for sem, val in want.items():
            if seen.get((q, sem), 0) < val:
                Q[q].wait_ge(T.sem[sem], val)
                seen[(q, sem)] = val
        if q in "vstgy":
            done = c["fn"]()
            if c["sem"] != "sent":
                done.then_inc(T.sem[c["sem"]], c["inc"])
        c["count"] = cnt[c["sem"]] = cnt.get(c["sem"], 0) + c["inc"]
    for sem in cnt:
        if seen.get(("g", sem), 0) < cnt[sem]:
            g.wait_ge(T.sem[sem], cnt[sem])
